import numpy as np
import ml_dtypes


def mxq(x, axis, fmt="e4m3"):
    dtype, down = {"e4m3": (ml_dtypes.float8_e4m3fn, 7), "e5m2": (ml_dtypes.float8_e5m2, 14)}[fmt]
    v = np.moveaxis(np.asarray(x, np.float32).astype(ml_dtypes.bfloat16).astype(np.float64), axis, -1)
    blocks = v.reshape(v.shape[:-1] + (-1, 32))
    amax = np.abs(blocks).max(-1, keepdims=True)
    byte = np.maximum(np.where(amax > 0, np.frexp(amax)[1] - 1 + 127, 0) - down, 1)
    scale = np.exp2(byte - 127.0)
    codes = (blocks / scale).astype(np.float32).astype(dtype).astype(np.float64)
    return np.moveaxis((codes * scale).reshape(v.shape), -1, axis)


WIDE = False


def mx_kscale(k):
    if not WIDE:
        return np.ones(k)
    levels = np.array([10, -10, 5, -5, 0])
    if k % 512:
        return np.exp2(np.random.permutation(np.resize(levels, k // 32))).repeat(32)
    a = np.empty((k // 512, 16))
    for p in range(k // 512):
        a[p, :8] = np.random.permutation(np.resize(levels, 8))
        for g in range(8):
            far = levels[np.abs(levels - a[p, g]) >= 10]
            a[p, g + 8] = far[np.random.randint(len(far))]
    return np.exp2(a.ravel()).repeat(32)


def f64(x):
    return np.asarray(x).astype(np.float64)


def striped(idx):
    return np.tile(idx.reshape(-1, 16).T, (8, 1)).astype(np.uint16)


def unstriped(offs):
    return offs[:16].T.reshape(-1).astype(np.int64)


E2M1 = np.array([0.0, 0.5, 1.0, 1.5, 2.0, 3.0, 4.0, 6.0, -0.0, -0.5, -1.0, -1.5, -2.0, -3.0, -4.0, -6.0])


def pack_weight(w, fmt):
    k, n = w.shape
    w = f64(np.asarray(w, np.float32).astype(ml_dtypes.bfloat16)).reshape(k // 32, 32, n)
    amax = np.abs(w).max(1)
    if fmt == "e4m3":
        byte = np.frexp(amax)[1] - 1 + 127 - 7
    else:
        mant, ex = np.frexp(amax / 6.0)
        byte = np.where(mant > 0.5, ex, ex - 1) + 127
    byte = np.clip(np.where(amax > 0, byte, 1), 1, 254)
    scaled = (w * np.exp2(127.0 - byte)[:, None, :]).reshape(k, n).astype(np.float32)
    by_word = np.ascontiguousarray(scaled.reshape(k // 512, 128, 4, n).transpose(0, 1, 3, 2))
    if fmt == "e4m3":
        words = by_word.astype(ml_dtypes.float8_e4m3fn).view(np.uint8)
    else:
        c = by_word.astype(ml_dtypes.float4_e2m1fn).view(np.uint8) & 0xF
        words = (c[..., 0::2] | (c[..., 1::2] << 4)).reshape(k // 512, 128, 2 * n)
    return np.ascontiguousarray(words), np.ascontiguousarray(byte.astype(np.uint8).reshape(k // 512, 16, n))


def unpack_weight(words, scales, fmt):
    g, _, n = scales.shape
    words = np.ascontiguousarray(words).reshape(g, 128, n, -1)
    if fmt == "e4m3":
        vals = words.view(ml_dtypes.float8_e4m3fn).astype(np.float64)
    else:
        nib = np.empty((g, 128, n, 4), np.uint8)
        nib[..., 0::2] = words & 0xF
        nib[..., 1::2] = words >> 4
        vals = E2M1[nib]
    vals = vals * np.repeat(np.exp2(scales.astype(np.float64) - 127.0), 8, axis=1)[..., None]
    return vals.transpose(0, 1, 3, 2).reshape(g * 512, n)


def gelu(v):
    return 0.5 * v * (1.0 + np.tanh(np.sqrt(2.0 / np.pi) * (v + 0.044715 * v**3)))


K, T, S, P, H, N = 1024, 4096, 1024, 512, 1024, 512

def setup_inputs():
    n = np.random.standard_normal
    s = mx_kscale(K)[:, None]
    u = mx_kscale(H)[:, None]
    tab_words, tab_scales = pack_weight(n((K, T)) * s, "e4m3")
    w1 = n((K, H)) / np.sqrt(K) / s * u.T
    w2_words, w2_scales = pack_weight(2.0 * n((H, N)) / np.sqrt(H) / u, "e2m1")
    return {
        "tab_words": tab_words,
        "tab_scales": tab_scales,
        "offs": striped(np.random.permutation(T)[:S]),
        "pos1": striped(np.random.permutation(S)[:P]),
        "pos2": striped(np.random.permutation(S)[:P]),
        "w1": w1.astype(np.float32),
        "w2_words": w2_words,
        "w2_scales": w2_scales,
    }

def reference(tab_words, tab_scales, offs, pos1, pos2, w1, w2_words, w2_scales):
    v = unpack_weight(tab_words, tab_scales, "e4m3")[:, unstriped(offs)]
    h = mxq(f64(w1), 0, "e4m3").T @ v
    a = h[:, unstriped(pos1)]
    b = h[:, unstriped(pos2)]
    z = np.maximum(0.25 * a + 0.75 * b, 0.0)
    w2 = unpack_weight(w2_words, w2_scales, "e2m1")
    y = w2.T @ mxq(z, 0, "e4m3")
    return 1.0 - np.exp(-np.abs(y))

@@ -1,0 +1,276 @@
+from contextlib import ExitStack
+
+import concourse.mybir as mybir
+from concourse.masks import make_identity
+
+K, T, S, M, H, N = 1024, 4096, 1024, 512, 1024, 512
+FLOPS = 2 * K * H * S + 2 * H * N * M
+
+F32 = mybir.dt.float32
+BF16 = mybir.dt.bfloat16
+I32 = mybir.dt.int32
+U32 = mybir.dt.uint32
+U16 = mybir.dt.uint16
+U8 = mybir.dt.uint8
+FP8X4 = mybir.dt.float8_e4m3fn_x4
+FP4X4 = mybir.dt.float4_e2m1fn_x4
+ACT = mybir.ActivationFunctionType
+ALU = mybir.AluOpType
+
+P = 128
+BANK = 512
+CHUNKS = H // P
+VECTOR_CASTS = (1, 7)
+GPSIMD_CASTS = ()
+RING = 768
+
+
+def tile_list_voxel_edge_opacity_kernel(tc, tab_words, tab_scales, offs, pos1, pos2, w1, w2_words, w2_scales, out):
+    nc = tc.nc
+    with ExitStack() as ctx:
+        keep = ctx.enter_context(tc.tile_pool(name="keep", bufs=1))
+        psum = ctx.enter_context(tc.psum_pool(name="psum", bufs=1))
+        banks = [psum.tile([P, BANK], F32, name="bank%d" % b) for b in range(8)]
+
+        def tile(shape, dtype, name, tag=None):
+            return keep.tile(shape, dtype, name=name, tag=tag or name, align_bytes=64)
+
+        offs_sb = tile([P, S // 16], U16, "offs_sb")
+        pos1_sb = tile([P, M // 16], U16, "pos1_sb")
+        pos2_sb = tile([P, M // 16], U16, "pos2_sb")
+        tab_w = [tile([P, T], I32, "tab_w%d" % a) for a in range(2)]
+        tab_s = tile([P, T // 4], I32, "tab_s")
+        v_w = [tile([P, S], U32, "v_w%d" % a) for a in range(2)]
+        v_s = tile([P, S], U8, "v_s")
+        w1_raw = [tile([P, 2, 4, P], F32, "w1_raw%d" % c) for c in range(CHUNKS)]
+        w1_bf = [tile([P, 2, P, 4], BF16, "w1_bf%d" % c) for c in range(CHUNKS)]
+        w1_w = [tile([P, 2 * P], U32, "w1_w%d" % c) for c in range(CHUNKS)]
+        w1_s = [tile([P, 2 * P], U8, "w1_s%d" % c) for c in range(CHUNKS)]
+        h = [tile([P, S], F32, "h%d" % c) for c in range(CHUNKS)]
+        near = [tile([P, M], F32, "near%d" % c) for c in range(CHUNKS)]
+        far3 = [w1_raw[c + 2][:, 1].rearrange("p j c -> p (j c)") for c in range(CHUNKS - 2)]
+        far3 += [tile([P, M], F32, "far3_%d" % c)[:] for c in range(CHUNKS - 2, CHUNKS)]
+        late = {}
+        threes = tile([P, M], F32, "threes")
+        warm = tile([P, 1], F32, "warm")
+        ident = tile([P, P], F32, "ident")
+        perm = tile([P, P], F32, "perm")
+        z_t = tile([P, 4, 2, 2, 4, 64], BF16, "z_t")
+        z_bf = {(g, u0): tile([P, 2 * P, 4], BF16, "z_bf%d%d" % (g, u0)) for g in range(2) for u0 in (0, 2)}
+        z_w = tile([P, 2, M], U32, "z_w")
+        z_s = tile([P, 2, M], U8, "z_s")
+        w2_w = tile([P, 2, 2 * N // 4], I32, "w2_w")
+        w2_s = tile([P, 2, N // 4], I32, "w2_s")
+        absy = [tile([P, BANK], F32, "absy%d" % u) for u in range(4)]
+        expy = [tile([P, BANK], F32, "expy%d" % u) for u in range(4)]
+        res = [tile([P, 4, P], F32, "res%d" % u) for u in range(4)]
+
+        nc.vector.memset(tab_s[:], 0)
+        nc.vector.memset(threes[:], 3.0)
+        nc.vector.memset(w2_s[:], 0)
+        nc.scalar.activation(warm[:], threes[:, 0:1], ACT.Exp, scale=-1.0)
+        make_identity(nc, ident[:])
+        nc.vector.tensor_copy(
+            out=perm[:].rearrange("k (e q i) -> k e q i", e=2, i=2),
+            in_=ident[:].rearrange("k (q e i) -> k e q i", e=2, i=2),
+        )
+
+        def load_table_words(a):
+            nc.sync.dma_start(out=tab_w[a][:], in_=tab_words[a].rearrange("p t i -> p (t i)").bitcast(I32))
+
+        def load_w1(c):
+            for a in range(2):
+                rows = w1[512 * a : 512 * (a + 1), P * c : P * (c + 1)]
+                nc.sync.dma_start(out=w1_raw[c][:, a, :, :], in_=rows.rearrange("(p j) c -> p j c", j=4))
+
+        nc.sync.dma_start(pos1_sb[:], pos1)
+        nc.sync.dma_start(pos2_sb[:], pos2)
+        nc.sync.dma_start(offs_sb[:], offs)
+        load_table_words(0)
+        for q in range(4):
+            nc.sync.dma_start(out=tab_s[32 * q : 32 * q + 8, :], in_=tab_scales[:, 4 * q : 4 * q + 4, :].bitcast(I32))
+        load_w1(0)
+        load_table_words(1)
+        for c in range(1, CHUNKS):
+            load_w1(c)
+        nc.sync.dma_start(out=w2_w[:], in_=w2_words.rearrange("a p b -> p a b").bitcast(I32))
+        for q in range(4):
+            rows = w2_scales[:, 4 * q : 4 * q + 4, :].rearrange("a r n -> r a n")
+            nc.sync.dma_start(out=w2_s[32 * q : 32 * q + 4, :, :], in_=rows.bitcast(I32))
+
+        def gather_table_words(a, first, last):
+            window = tab_w[a][:].bitcast(U32)
+            nc.vector.tensor_copy(out=v_w[a][:, first:last], in_=window.indirect(offs_sb[:, first // 16 : last // 16]))
+
+        def cast_w1(c):
+            src = w1_raw[c][:].rearrange("p a j c -> p a c j")
+            if c in VECTOR_CASTS:
+                nc.vector.tensor_copy(out=w1_bf[c][:], in_=src)
+            elif c in GPSIMD_CASTS:
+                for a in range(2):
+                    nc.gpsimd.tensor_scalar(w1_bf[c][:, a], src[:, a], 1.0, 0.0, ALU.mult, ALU.add)
+            else:
+                nc.scalar.copy(out=w1_bf[c][:], in_=src)
+
+        def quantize_w1(c):
+            nc.vector.quantize_mx(
+                out=w1_w[c][:].bitcast(FP8X4), scales=w1_s[c][:], in_=w1_bf[c][:].rearrange("p a c j -> p (a c j)")
+            )
+
+        def make_h(c, halves=(0, 1)):
+            for half in halves:
+                cols = slice(BANK * half, BANK * (half + 1))
+                acc = banks[2 * half + c % 2]
+                for a in range(2):
+                    nc.tensor.matmul_mx(
+                        out=acc[:],
+                        lhsT=w1_w[c][:, P * a : P * (a + 1)].bitcast(FP8X4),
+                        lhsT_scale=w1_s[c][:, P * a : P * (a + 1)],
+                        rhs=v_w[a][:, cols].bitcast(FP8X4),
+                        rhs_scale=v_s[4 * a :, cols],
+                        start=(a == 0),
+                        stop=(a == 1),
+                    )
+                nc.scalar.copy(out=h[c][:, cols], in_=acc[:])
+
+        def picked(c, u0, u1):
+            if (c, u0) in late:
+                return late[(c, u0)]
+            return near[c][:, P * u0 : P * u1], far3[c][:, P * u0 : P * u1]
+
+        def gather_near(c, u0, u1):
+            entries = slice(8 * u0, 8 * u1)
+            nc.vector.tensor_copy(out=picked(c, u0, u1)[0], in_=h[c][:].indirect(pos1_sb[:, entries]))
+
+        def gather_far(c, u0, u1):
+            entries = slice(8 * u0, 8 * u1)
+            nc.vector.tensor_tensor(
+                picked(c, u0, u1)[1], h[c][:].indirect(pos2_sb[:, entries]), threes[:, 0 : P * (u1 - u0)], ALU.mult
+            )
+
+        def add_transposed(dst, c, u):
+            second, first = picked(c, u, u + 1)
+            nc.tensor.matmul(dst, first, perm[:], start=True, stop=False, is_transpose=True)
+            nc.tensor.matmul(dst, second, perm[:], start=False, stop=True, is_transpose=True)
+
+        def relu(dst, src, on_vector):
+            if on_vector:
+                nc.vector.tensor_scalar(dst, src, 0.25, 0.0, ALU.mult, ALU.max)
+            else:
+                nc.scalar.activation(dst, src, ACT.Relu, scale=0.25)
+
+        def mix_chunk(c, u0, u1, bank):
+            for u in range(u0, u1):
+                add_transposed(bank[:, P * (u - u0) : P * (u - u0 + 1)], c, u)
+            src = bank[:, 0 : P * (u1 - u0)].rearrange("m (u e w) -> m u e w", e=2, w=64)
+            relu(z_t[:, u0:u1, c // 4, :, c % 4, :], src, False)
+
+        def mix_samples(u, c0, c1, bank, on_vector):
+            for c in range(c0, c1):
+                add_transposed(bank[:, P * (c - c0) : P * (c - c0 + 1)], c, u)
+            src = bank[:, 0 : P * (c1 - c0)].rearrange("m (c e w) -> m e c w", e=2, w=64)
+            relu(z_t[:, u, c0 // 4, :, c0 % 4 : c0 % 4 + c1 - c0, :], src, on_vector)
+
+        def z_cols(g, u0, u1):
+            return z_bf[(g, u0 - u0 % 2)][:, P * (u0 % 2) : P * (u0 % 2 + u1 - u0), :]
+
+        def turn_back(g, u0, u1, bank, on_vector):
+            words = z_t[:].rearrange("m u g e c w -> m u g e (c w)").bitcast(F32)
+            for u in range(u0, u1):
+                for e in range(2):
+                    slot = 2 * (u - u0) + e
+                    nc.tensor.transpose(bank[:, P * slot : P * (slot + 1)], words[:, u, g, e, :], ident[:])
+            dst = z_cols(g, u0, u1).bitcast(F32).rearrange("p (u m) e -> p u m e", m=P)
+            src = bank[:, 0 : 2 * P * (u1 - u0)].rearrange("p (u e m) -> p u m e", e=2, m=P)
+            if on_vector:
+                nc.vector.tensor_copy(out=dst, in_=src)
+            else:
+                nc.scalar.copy(out=dst, in_=src)
+
+        def quantize_z(g, u0, u1):
+            cols = slice(P * u0, P * u1)
+            nc.vector.quantize_mx(
+                out=z_w[:, g, cols].bitcast(FP8X4), scales=z_s[:, g, cols], in_=z_cols(g, u0, u1).rearrange("p m i -> p (m i)")
+            )
+
+        def finish(u, t0, t1, acc):
+            cols = slice(P * u, P * (u + 1))
+            codes = w2_w[:].bitcast(U8)
+            scales = w2_s[:].bitcast(U8)
+            for t in range(t0, t1):
+                for g in (1, 0):
+                    nc.tensor.matmul_mx(
+                        out=acc[:, P * (t - t0) : P * (t - t0 + 1)],
+                        lhsT=codes[:, g, 2 * P * t : 2 * P * (t + 1)].bitcast(FP4X4),
+                        lhsT_scale=scales[:, g, P * t : P * (t + 1)],
+                        rhs=z_w[:, g, cols].bitcast(FP8X4),
+                        rhs_scale=z_s[:, g, cols],
+                        start=(g == 1),
+                        stop=(g == 0),
+                    )
+            part = slice(P * t0, P * t1)
+            nc.scalar.activation(absy[u][:, part], acc[:, 0 : P * (t1 - t0)], ACT.Abs)
+            nc.scalar.activation(expy[u][:, part], absy[u][:, part], ACT.Exp, scale=-1.0)
+            flat = res[u][:].rearrange("n t m -> n (t m)")
+            nc.vector.tensor_scalar(flat[:, part], expy[u][:, part], -1.0, 1.0, ALU.mult, ALU.add)
+            rows = out[P * t0 : P * t1, cols].rearrange("(t n) m -> n t m", n=P)
+            nc.sync.dma_start(out=rows, in_=res[u][:, t0:t1, :])
+
+        gather_table_words(0, 0, S)
+        nc.vector.tensor_copy(out=v_s[:], in_=tab_s[:].bitcast(U8).indirect(offs_sb[:]))
+        cast_w1(0)
+        quantize_w1(0)
+        gather_table_words(1, 0, BANK)
+        gather_table_words(1, BANK, S)
+        make_h(0)
+        cast_w1(1)
+        quantize_w1(1)
+        for c in range(CHUNKS):
+            last = 4 if c < 5 else 2
+            if c + 2 < CHUNKS:
+                cast_w1(c + 2)
+            gather_near(c, 0, last)
+            if c + 1 < CHUNKS - 1:
+                make_h(c + 1)
+            if c + 2 < CHUNKS:
+                quantize_w1(c + 2)
+            if c == 5:
+                make_h(7)
+            gather_far(c, 0, last)
+            if c >= 1:
+                mix_chunk(c - 1, 0, 4 if c - 1 < 5 else 2, banks[3] if c == 6 else banks[4 + c % 2])
+            if c == 5:
+                turn_back(0, 0, 2, banks[6], False)
+                quantize_z(0, 0, 2)
+            if c == 6:
+                turn_back(0, 2, 4, banks[7], False)
+                quantize_z(0, 2, 4)
+        mix_chunk(7, 0, 2, banks[0])
+        turn_back(1, 0, 2, banks[6], False)
+        late[(5, 2)] = near[5][:, 0:P], far3[5][:, 0:P]
+        late[(6, 2)] = near[5][:, P : 2 * P], far3[5][:, P : 2 * P]
+        late[(5, 3)] = near[7][:, 0:P], far3[7][:, 0:P]
+        for c in range(5, CHUNKS):
+            gather_near(c, 2, 3)
+            gather_far(c, 2, 3)
+        mix_samples(2, 5, CHUNKS, banks[0], False)
+        gather_near(5, 3, 4)
+        gather_far(5, 3, 4)
+        quantize_z(1, 0, 2)
+        turn_back(1, 2, 3, banks[4], False)
+        last_picks = tile([P, 4, P], F32, "last_picks", tag="z_bf10")
+        late[(6, 3)] = last_picks[:, 0, :], last_picks[:, 1, :]
+        late[(7, 3)] = last_picks[:, 2, :], last_picks[:, 3, :]
+        for c in range(6, CHUNKS):
+            gather_near(c, 3, 4)
+            gather_far(c, 3, 4)
+        finish(0, 0, 4, banks[2])
+        finish(1, 0, 4, banks[3])
+        quantize_z(1, 2, 3)
+        mix_samples(3, 5, 7, banks[6], True)
+        mix_samples(3, 7, 8, banks[4], True)
+        turn_back(1, 3, 4, banks[0], True)
+        quantize_z(1, 3, 4)
+        finish(2, 0, 4, banks[5])
+        finish(3, 0, 2, banks[7])
+        finish(3, 2, 4, banks[1])

@@ -21,7 +21,6 @@ P = 128
 BANK = 512
 CHUNKS = H // P
 VECTOR_CASTS = (1, 7)
-GPSIMD_CASTS = ()
 RING = 768
 
 
@@ -42,13 +41,13 @@ def tile_list_voxel_edge_opacity_kernel(tc, tab_words, tab_scales, offs, pos1, p
         tab_s = tile([P, T // 4], I32, "tab_s")
         v_w = [tile([P, S], U32, "v_w%d" % a) for a in range(2)]
         v_s = tile([P, S], U8, "v_s")
-        w1_raw = [tile([P, 2, 4, P], F32, "w1_raw%d" % c) for c in range(CHUNKS)]
-        w1_bf = [tile([P, 2, P, 4], BF16, "w1_bf%d" % c) for c in range(CHUNKS)]
+        w1_raw = [tile([P, 4, 2, P], F32, "w1_raw%d" % c) for c in range(CHUNKS)]
+        w1_bf = {}
         w1_w = [tile([P, 2 * P], U32, "w1_w%d" % c) for c in range(CHUNKS)]
         w1_s = [tile([P, 2 * P], U8, "w1_s%d" % c) for c in range(CHUNKS)]
         h = [tile([P, S], F32, "h%d" % c) for c in range(CHUNKS)]
         near = [tile([P, M], F32, "near%d" % c) for c in range(CHUNKS)]
-        far3 = [w1_raw[c + 2][:, 1].rearrange("p j c -> p (j c)") for c in range(CHUNKS - 2)]
+        far3 = [w1_raw[c + 2][:, 2:4].rearrange("p j a c -> p (j a c)") for c in range(CHUNKS - 2)]
         far3 += [tile([P, M], F32, "far3_%d" % c)[:] for c in range(CHUNKS - 2, CHUNKS)]
         late = {}
         threes = tile([P, M], F32, "threes")
@@ -61,9 +60,10 @@ def tile_list_voxel_edge_opacity_kernel(tc, tab_words, tab_scales, offs, pos1, p
         z_s = tile([P, 2, M], U8, "z_s")
         w2_w = tile([P, 2, 2 * N // 4], I32, "w2_w")
         w2_s = tile([P, 2, N // 4], I32, "w2_s")
-        absy = [tile([P, BANK], F32, "absy%d" % u) for u in range(4)]
+        absy = [tile([P, BANK], F32, "absy%d" % u) for u in range(3)]
+        absy.append(absy[2])
         expy = [tile([P, BANK], F32, "expy%d" % u) for u in range(4)]
-        res = [tile([P, 4, P], F32, "res%d" % u) for u in range(4)]
+        res = {u: tile([P, 4, P], F32, "res%d" % u) for u in (2, 3)}
 
         nc.vector.memset(tab_s[:], 0)
         nc.vector.memset(threes[:], 3.0)
@@ -81,14 +81,14 @@ def tile_list_voxel_edge_opacity_kernel(tc, tab_words, tab_scales, offs, pos1, p
         def load_w1(c):
             for a in range(2):
                 rows = w1[512 * a : 512 * (a + 1), P * c : P * (c + 1)]
-                nc.sync.dma_start(out=w1_raw[c][:, a, :, :], in_=rows.rearrange("(p j) c -> p j c", j=4))
+                nc.sync.dma_start(out=w1_raw[c][:, :, a, :], in_=rows.rearrange("(p j) c -> p j c", j=4))
 
         nc.sync.dma_start(pos1_sb[:], pos1)
         nc.sync.dma_start(pos2_sb[:], pos2)
         nc.sync.dma_start(offs_sb[:], offs)
         load_table_words(0)
         for q in range(4):
-            nc.sync.dma_start(out=tab_s[32 * q : 32 * q + 8, :], in_=tab_scales[:, 4 * q : 4 * q + 4, :].bitcast(I32))
+            nc.gpsimd.dma_start(out=tab_s[32 * q : 32 * q + 8, :], in_=tab_scales[:, 4 * q : 4 * q + 4, :].bitcast(I32))
         load_w1(0)
         load_table_words(1)
         for c in range(1, CHUNKS):
@@ -103,18 +103,17 @@ def tile_list_voxel_edge_opacity_kernel(tc, tab_words, tab_scales, offs, pos1, p
             nc.vector.tensor_copy(out=v_w[a][:, first:last], in_=window.indirect(offs_sb[:, first // 16 : last // 16]))
 
         def cast_w1(c):
-            src = w1_raw[c][:].rearrange("p a j c -> p a c j")
+            w1_bf[c] = tile([P, 2 * P, 4], BF16, "w1_bf%d" % c, tag="w1_bf%d" % (c % 2))
+            src = w1_raw[c][:].rearrange("p j a (x i) -> p (a x) j i", i=4)
+            dst = w1_bf[c][:].rearrange("p (x i) j -> p x j i", i=4)
             if c in VECTOR_CASTS:
-                nc.vector.tensor_copy(out=w1_bf[c][:], in_=src)
-            elif c in GPSIMD_CASTS:
-                for a in range(2):
-                    nc.gpsimd.tensor_scalar(w1_bf[c][:, a], src[:, a], 1.0, 0.0, ALU.mult, ALU.add)
+                nc.vector.tensor_copy(out=dst, in_=src)
             else:
-                nc.scalar.copy(out=w1_bf[c][:], in_=src)
+                nc.scalar.copy(out=dst, in_=src)
 
         def quantize_w1(c):
             nc.vector.quantize_mx(
-                out=w1_w[c][:].bitcast(FP8X4), scales=w1_s[c][:], in_=w1_bf[c][:].rearrange("p a c j -> p (a c j)")
+                out=w1_w[c][:].bitcast(FP8X4), scales=w1_s[c][:], in_=w1_bf[c][:].rearrange("p c j -> p (c j)")
             )
 
         def make_h(c, halves=(0, 1)):
@@ -211,6 +210,10 @@ def tile_list_voxel_edge_opacity_kernel(tc, tab_words, tab_scales, offs, pos1, p
             part = slice(P * t0, P * t1)
             nc.scalar.activation(absy[u][:, part], acc[:, 0 : P * (t1 - t0)], ACT.Abs)
             nc.scalar.activation(expy[u][:, part], absy[u][:, part], ACT.Exp, scale=-1.0)
+
+        def store(u, t0, t1):
+            cols = slice(P * u, P * (u + 1))
+            part = slice(P * t0, P * t1)
             flat = res[u][:].rearrange("n t m -> n (t m)")
             nc.vector.tensor_scalar(flat[:, part], expy[u][:, part], -1.0, 1.0, ALU.mult, ALU.add)
             rows = out[P * t0 : P * t1, cols].rearrange("(t n) m -> n t m", n=P)
@@ -271,6 +274,13 @@ def tile_list_voxel_edge_opacity_kernel(tc, tab_words, tab_scales, offs, pos1, p
         mix_samples(3, 7, 8, banks[4], True)
         turn_back(1, 3, 4, banks[0], True)
         quantize_z(1, 3, 4)
+        first_res = tile([P, 2, 4, P], F32, "first_res", tag="z_bf12")
+        for u in range(2):
+            res[u] = first_res[:, u]
+            store(u, 0, 4)
         finish(2, 0, 4, banks[5])
         finish(3, 0, 2, banks[7])
         finish(3, 2, 4, banks[1])
+        store(2, 0, 4)
+        store(3, 0, 2)
+        store(3, 2, 4)

@@ -50,7 +50,6 @@ def tile_list_voxel_edge_opacity_kernel(tc, tab_words, tab_scales, offs, pos1, p
         far3 = [w1_raw[c + 2][:, 2:4].rearrange("p j a c -> p (j a c)") for c in range(CHUNKS - 2)]
         far3 += [tile([P, M], F32, "far3_%d" % c)[:] for c in range(CHUNKS - 2, CHUNKS)]
         late = {}
-        threes = tile([P, M], F32, "threes")
         warm = tile([P, 1], F32, "warm")
         ident = tile([P, P], F32, "ident")
         perm = tile([P, P], F32, "perm")
@@ -66,10 +65,9 @@ def tile_list_voxel_edge_opacity_kernel(tc, tab_words, tab_scales, offs, pos1, p
         res = {u: tile([P, 4, P], F32, "res%d" % u) for u in (2, 3)}
 
         nc.vector.memset(tab_s[:], 0)
-        nc.vector.memset(threes[:], 3.0)
         nc.vector.memset(w2_s[:], 0)
-        nc.scalar.activation(warm[:], threes[:, 0:1], ACT.Exp, scale=-1.0)
         make_identity(nc, ident[:])
+        nc.scalar.activation(warm[:], ident[:, 0:1], ACT.Exp, scale=-1.0)
         nc.vector.tensor_copy(
             out=perm[:].rearrange("k (e q i) -> k e q i", e=2, i=2),
             in_=ident[:].rearrange("k (q e i) -> k e q i", e=2, i=2),
@@ -88,7 +86,7 @@ def tile_list_voxel_edge_opacity_kernel(tc, tab_words, tab_scales, offs, pos1, p
         nc.sync.dma_start(offs_sb[:], offs)
         load_table_words(0)
         for q in range(4):
-            nc.gpsimd.dma_start(out=tab_s[32 * q : 32 * q + 8, :], in_=tab_scales[:, 4 * q : 4 * q + 4, :].bitcast(I32))
+            nc.sync.dma_start(out=tab_s[32 * q : 32 * q + 8, :], in_=tab_scales[:, 4 * q : 4 * q + 4, :].bitcast(I32))
         load_w1(0)
         load_table_words(1)
         for c in range(1, CHUNKS):
@@ -104,8 +102,8 @@ def tile_list_voxel_edge_opacity_kernel(tc, tab_words, tab_scales, offs, pos1, p
 
         def cast_w1(c):
             w1_bf[c] = tile([P, 2 * P, 4], BF16, "w1_bf%d" % c, tag="w1_bf%d" % (c % 2))
-            src = w1_raw[c][:].rearrange("p j a (x i) -> p (a x) j i", i=4)
-            dst = w1_bf[c][:].rearrange("p (x i) j -> p x j i", i=4)
+            src = w1_raw[c][:].rearrange("p j a c -> p (a c) j")
+            dst = w1_bf[c][:]
             if c in VECTOR_CASTS:
                 nc.vector.tensor_copy(out=dst, in_=src)
             else:
@@ -139,17 +137,16 @@ def tile_list_voxel_edge_opacity_kernel(tc, tab_words, tab_scales, offs, pos1, p
 
         def gather_near(c, u0, u1):
             entries = slice(8 * u0, 8 * u1)
-            nc.vector.tensor_copy(out=picked(c, u0, u1)[0], in_=h[c][:].indirect(pos1_sb[:, entries]))
+            nc.vector.tensor_copy(out=picked(c, u0, u1)[0], in_=h[c][:].indirect(pos2_sb[:, entries]))
 
         def gather_far(c, u0, u1):
             entries = slice(8 * u0, 8 * u1)
-            nc.vector.tensor_tensor(
-                picked(c, u0, u1)[1], h[c][:].indirect(pos2_sb[:, entries]), threes[:, 0 : P * (u1 - u0)], ALU.mult
-            )
+            nc.vector.tensor_copy(out=picked(c, u0, u1)[1], in_=h[c][:].indirect(pos1_sb[:, entries]))
 
         def add_transposed(dst, c, u):
-            second, first = picked(c, u, u + 1)
-            nc.tensor.matmul(dst, first, perm[:], start=True, stop=False, is_transpose=True)
+            first, second = picked(c, u, u + 1)
+            for k in range(3):
+                nc.tensor.matmul(dst, first, perm[:], start=(k == 0), stop=False, is_transpose=True)
             nc.tensor.matmul(dst, second, perm[:], start=False, stop=True, is_transpose=True)
 
         def relu(dst, src, on_vector):

@@ -1,7 +1,6 @@
 from contextlib import ExitStack
 
 import concourse.mybir as mybir
-from concourse.masks import make_identity
 
 K, T, S, M, H, N = 1024, 4096, 1024, 512, 1024, 512
 FLOPS = 2 * K * H * S + 2 * H * N * M
@@ -19,9 +18,8 @@ ALU = mybir.AluOpType
 
 P = 128
 BANK = 512
-CHUNKS = H // P
-VECTOR_CASTS = (1, 7)
-RING = 768
+PACK = 4
+WINDOW = 2 * S
 
 
 def tile_list_voxel_edge_opacity_kernel(tc, tab_words, tab_scales, offs, pos1, pos2, w1, w2_words, w2_scales, out):
@@ -41,169 +39,137 @@ def tile_list_voxel_edge_opacity_kernel(tc, tab_words, tab_scales, offs, pos1, p
         tab_s = tile([P, T // 4], I32, "tab_s")
         v_w = [tile([P, S], U32, "v_w%d" % a) for a in range(2)]
         v_s = tile([P, S], U8, "v_s")
-        w1_raw = [tile([P, 4, 2, P], F32, "w1_raw%d" % c) for c in range(CHUNKS)]
-        w1_bf = {}
-        w1_w = [tile([P, 2 * P], U32, "w1_w%d" % c) for c in range(CHUNKS)]
-        w1_s = [tile([P, 2 * P], U8, "w1_s%d" % c) for c in range(CHUNKS)]
-        h = [tile([P, S], F32, "h%d" % c) for c in range(CHUNKS)]
-        near = [tile([P, M], F32, "near%d" % c) for c in range(CHUNKS)]
-        far3 = [w1_raw[c + 2][:, 2:4].rearrange("p j a c -> p (j a c)") for c in range(CHUNKS - 2)]
-        far3 += [tile([P, M], F32, "far3_%d" % c)[:] for c in range(CHUNKS - 2, CHUNKS)]
-        late = {}
+        w1_raw = {}
+        w1_bf = {(0, a): tile([P, PACK, P, PACK], BF16, "w1_bf0%d" % a) for a in range(2)}
+        w1_w = {(g, a): tile([P, BANK], U32, "w1_w%d%d" % (g, a)) for g in range(2) for a in range(2)}
+        w1_s = {(g, a): tile([P, BANK], U8, "w1_s%d%d" % (g, a)) for g in range(2) for a in range(2)}
+        h = [tile([P, WINDOW], F32, "h%d" % t) for t in range(PACK)]
+        near3 = [tile([P, M], F32, "near3_%d" % t) for t in range(PACK)]
+        sum0 = tile([P, PACK, M], F32, "sum0")
+        sum1 = {}
+        z_bf = {}
         warm = tile([P, 1], F32, "warm")
-        ident = tile([P, P], F32, "ident")
-        perm = tile([P, P], F32, "perm")
-        z_t = tile([P, 4, 2, 2, 4, 64], BF16, "z_t")
-        z_bf = {(g, u0): tile([P, 2 * P, 4], BF16, "z_bf%d%d" % (g, u0)) for g in range(2) for u0 in (0, 2)}
         z_w = tile([P, 2, M], U32, "z_w")
         z_s = tile([P, 2, M], U8, "z_s")
         w2_w = tile([P, 2, 2 * N // 4], I32, "w2_w")
         w2_s = tile([P, 2, N // 4], I32, "w2_s")
-        absy = [tile([P, BANK], F32, "absy%d" % u) for u in range(3)]
-        absy.append(absy[2])
+        absy = [tile([P, BANK], F32, "absy%d" % u) for u in range(4)]
         expy = [tile([P, BANK], F32, "expy%d" % u) for u in range(4)]
-        res = {u: tile([P, 4, P], F32, "res%d" % u) for u in (2, 3)}
+        res = [tile([P, 4, P], F32, "res%d" % u) for u in range(4)]
 
         nc.vector.memset(tab_s[:], 0)
         nc.vector.memset(w2_s[:], 0)
-        make_identity(nc, ident[:])
-        nc.scalar.activation(warm[:], ident[:, 0:1], ACT.Exp, scale=-1.0)
-        nc.vector.tensor_copy(
-            out=perm[:].rearrange("k (e q i) -> k e q i", e=2, i=2),
-            in_=ident[:].rearrange("k (q e i) -> k e q i", e=2, i=2),
-        )
+        for t in range(PACK):
+            nc.vector.memset(h[t][:, S:WINDOW], 0.0)
+        nc.scalar.activation(warm[:], h[0][:, S : S + 1], ACT.Exp, scale=-1.0)
 
         def load_table_words(a):
             nc.sync.dma_start(out=tab_w[a][:], in_=tab_words[a].rearrange("p t i -> p (t i)").bitcast(I32))
 
-        def load_w1(c):
-            for a in range(2):
-                rows = w1[512 * a : 512 * (a + 1), P * c : P * (c + 1)]
-                nc.sync.dma_start(out=w1_raw[c][:, :, a, :], in_=rows.rearrange("(p j) c -> p j c", j=4))
+        def load_w1(g, a, m0, m1):
+            w1_raw[(g, a, m0)] = tile([P, PACK, PACK * (m1 - m0)], F32, "w1_raw%d%d_%d" % (g, a, m0))
+            rows = w1[512 * a : 512 * (a + 1), 512 * g + PACK * m0 : 512 * g + PACK * m1]
+            nc.sync.dma_start(out=w1_raw[(g, a, m0)][:], in_=rows.rearrange("(p j) c -> p j c", j=PACK))
 
-        nc.sync.dma_start(pos1_sb[:], pos1)
-        nc.sync.dma_start(pos2_sb[:], pos2)
         nc.sync.dma_start(offs_sb[:], offs)
         load_table_words(0)
         for q in range(4):
             nc.sync.dma_start(out=tab_s[32 * q : 32 * q + 8, :], in_=tab_scales[:, 4 * q : 4 * q + 4, :].bitcast(I32))
-        load_w1(0)
         load_table_words(1)
-        for c in range(1, CHUNKS):
-            load_w1(c)
+        load_w1(0, 0, 0, P)
+        load_w1(0, 1, 0, 80)
+        load_w1(0, 1, 80, P)
+        nc.sync.dma_start(pos2_sb[:], pos2)
+        nc.sync.dma_start(pos1_sb[:], pos1)
+        load_w1(1, 0, 0, P)
+        load_w1(1, 1, 0, P)
         nc.sync.dma_start(out=w2_w[:], in_=w2_words.rearrange("a p b -> p a b").bitcast(I32))
         for q in range(4):
             rows = w2_scales[:, 4 * q : 4 * q + 4, :].rearrange("a r n -> r a n")
             nc.sync.dma_start(out=w2_s[32 * q : 32 * q + 4, :, :], in_=rows.bitcast(I32))
 
-        def gather_table_words(a, first, last):
-            window = tab_w[a][:].bitcast(U32)
-            nc.vector.tensor_copy(out=v_w[a][:, first:last], in_=window.indirect(offs_sb[:, first // 16 : last // 16]))
+        def gather_table_words(a):
+            nc.vector.tensor_copy(out=v_w[a][:], in_=tab_w[a][:].bitcast(U32).indirect(offs_sb[:]))
 
-        def cast_w1(c):
-            w1_bf[c] = tile([P, 2 * P, 4], BF16, "w1_bf%d" % c, tag="w1_bf%d" % (c % 2))
-            src = w1_raw[c][:].rearrange("p j a c -> p (a c) j")
-            dst = w1_bf[c][:]
-            if c in VECTOR_CASTS:
+        def cast_w1(g, a, first, m0, m1, on_vector):
+            src = w1_raw[(g, a, first)][:, :, PACK * (m0 - first) : PACK * (m1 - first)].rearrange("p j (m t) -> p m t j", t=PACK)
+            dst = w1_bf[(g, a)][:, :, m0:m1, :].rearrange("p t m j -> p m t j")
+            if on_vector:
                 nc.vector.tensor_copy(out=dst, in_=src)
             else:
                 nc.scalar.copy(out=dst, in_=src)
 
-        def quantize_w1(c):
+        def quantize_w1(g, a, t0, t1):
+            cols = slice(P * t0, P * t1)
             nc.vector.quantize_mx(
-                out=w1_w[c][:].bitcast(FP8X4), scales=w1_s[c][:], in_=w1_bf[c][:].rearrange("p c j -> p (c j)")
+                out=w1_w[(g, a)][:, cols].bitcast(FP8X4),
+                scales=w1_s[(g, a)][:, cols],
+                in_=w1_bf[(g, a)][:, t0:t1].rearrange("p t m j -> p (t m j)"),
             )
 
-        def make_h(c, halves=(0, 1)):
-            for half in halves:
+        def h_pass(g, t, a, backwards=False):
+            for half in range(2):
                 cols = slice(BANK * half, BANK * (half + 1))
-                acc = banks[2 * half + c % 2]
-                for a in range(2):
-                    nc.tensor.matmul_mx(
-                        out=acc[:],
-                        lhsT=w1_w[c][:, P * a : P * (a + 1)].bitcast(FP8X4),
-                        lhsT_scale=w1_s[c][:, P * a : P * (a + 1)],
-                        rhs=v_w[a][:, cols].bitcast(FP8X4),
-                        rhs_scale=v_s[4 * a :, cols],
-                        start=(a == 0),
-                        stop=(a == 1),
-                    )
-                nc.scalar.copy(out=h[c][:, cols], in_=acc[:])
+                nc.tensor.matmul_mx(
+                    out=banks[2 * t + half][:],
+                    lhsT=w1_w[(g, a)][:, P * t : P * (t + 1)].bitcast(FP8X4),
+                    lhsT_scale=w1_s[(g, a)][:, P * t : P * (t + 1)],
+                    rhs=v_w[a][:, cols].bitcast(FP8X4),
+                    rhs_scale=v_s[4 * a :, cols],
+                    start=(a == int(backwards)),
+                    stop=(a != int(backwards)),
+                )
 
-        def picked(c, u0, u1):
-            if (c, u0) in late:
-                return late[(c, u0)]
-            return near[c][:, P * u0 : P * u1], far3[c][:, P * u0 : P * u1]
-
-        def gather_near(c, u0, u1):
-            entries = slice(8 * u0, 8 * u1)
-            nc.vector.tensor_copy(out=picked(c, u0, u1)[0], in_=h[c][:].indirect(pos2_sb[:, entries]))
-
-        def gather_far(c, u0, u1):
-            entries = slice(8 * u0, 8 * u1)
-            nc.vector.tensor_copy(out=picked(c, u0, u1)[1], in_=h[c][:].indirect(pos1_sb[:, entries]))
-
-        def add_transposed(dst, c, u):
-            first, second = picked(c, u, u + 1)
-            for k in range(3):
-                nc.tensor.matmul(dst, first, perm[:], start=(k == 0), stop=False, is_transpose=True)
-            nc.tensor.matmul(dst, second, perm[:], start=False, stop=True, is_transpose=True)
-
-        def relu(dst, src, on_vector):
-            if on_vector:
-                nc.vector.tensor_scalar(dst, src, 0.25, 0.0, ALU.mult, ALU.max)
+        def copy_h(t, second_on_vector=False):
+            nc.scalar.copy(out=h[t][:, 0:BANK], in_=banks[2 * t][:])
+            if second_on_vector:
+                nc.vector.tensor_copy(out=h[t][:, BANK:S], in_=banks[2 * t + 1][:])
             else:
-                nc.scalar.activation(dst, src, ACT.Relu, scale=0.25)
+                nc.scalar.copy(out=h[t][:, BANK:S], in_=banks[2 * t + 1][:])
 
-        def mix_chunk(c, u0, u1, bank):
-            for u in range(u0, u1):
-                add_transposed(bank[:, P * (u - u0) : P * (u - u0 + 1)], c, u)
-            src = bank[:, 0 : P * (u1 - u0)].rearrange("m (u e w) -> m u e w", e=2, w=64)
-            relu(z_t[:, u0:u1, c // 4, :, c % 4, :], src, False)
+        def gather_near(t):
+            nc.vector.tensor_scalar(near3[t][:], h[t][:].indirect(pos2_sb[:]), 3.0, 0.0, ALU.mult, ALU.add)
 
-        def mix_samples(u, c0, c1, bank, on_vector):
-            for c in range(c0, c1):
-                add_transposed(bank[:, P * (c - c0) : P * (c - c0 + 1)], c, u)
-            src = bank[:, 0 : P * (c1 - c0)].rearrange("m (c e w) -> m e c w", e=2, w=64)
-            relu(z_t[:, u, c0 // 4, :, c0 % 4 : c0 % 4 + c1 - c0, :], src, on_vector)
+        def gather_far(dst, t, u0, u1):
+            window = h[t][:].indirect(pos1_sb[:, 8 * u0 : 8 * u1])
+            nc.vector.tensor_tensor(dst, window, near3[t][:, P * u0 : P * u1], ALU.add)
 
-        def z_cols(g, u0, u1):
-            return z_bf[(g, u0 - u0 % 2)][:, P * (u0 % 2) : P * (u0 % 2 + u1 - u0), :]
-
-        def turn_back(g, u0, u1, bank, on_vector):
-            words = z_t[:].rearrange("m u g e c w -> m u g e (c w)").bitcast(F32)
-            for u in range(u0, u1):
-                for e in range(2):
-                    slot = 2 * (u - u0) + e
-                    nc.tensor.transpose(bank[:, P * slot : P * (slot + 1)], words[:, u, g, e, :], ident[:])
-            dst = z_cols(g, u0, u1).bitcast(F32).rearrange("p (u m) e -> p u m e", m=P)
-            src = bank[:, 0 : 2 * P * (u1 - u0)].rearrange("p (u e m) -> p u m e", e=2, m=P)
+        def relu(g, u0, u1, src, tag, on_vector=False):
+            z_bf[(g, u0)] = tile([P, P * (u1 - u0), PACK], BF16, "z_bf%d%d" % (g, u0), tag=tag)
+            src = src.rearrange("p t m -> p m t")
             if on_vector:
-                nc.vector.tensor_copy(out=dst, in_=src)
+                nc.vector.tensor_scalar(z_bf[(g, u0)][:], src, 0.25, 0.0, ALU.mult, ALU.max)
             else:
-                nc.scalar.copy(out=dst, in_=src)
+                nc.scalar.activation(z_bf[(g, u0)][:], src, ACT.Relu, scale=0.25)
 
         def quantize_z(g, u0, u1):
             cols = slice(P * u0, P * u1)
             nc.vector.quantize_mx(
-                out=z_w[:, g, cols].bitcast(FP8X4), scales=z_s[:, g, cols], in_=z_cols(g, u0, u1).rearrange("p m i -> p (m i)")
+                out=z_w[:, g, cols].bitcast(FP8X4), scales=z_s[:, g, cols], in_=z_bf[(g, u0)][:].rearrange("p m i -> p (m i)")
             )
 
-        def finish(u, t0, t1, acc):
+        def far_block(u, tag):
+            sum1[u] = tile([P, PACK, P], F32, "sum1_%d" % u, tag=tag)
+            for t in range(PACK):
+                gather_far(sum1[u][:, t, :], t, u, u + 1)
+
+        def density(u, t0, t1, acc):
             cols = slice(P * u, P * (u + 1))
             codes = w2_w[:].bitcast(U8)
             scales = w2_s[:].bitcast(U8)
             for t in range(t0, t1):
-                for g in (1, 0):
+                for g in range(2):
                     nc.tensor.matmul_mx(
                         out=acc[:, P * (t - t0) : P * (t - t0 + 1)],
                         lhsT=codes[:, g, 2 * P * t : 2 * P * (t + 1)].bitcast(FP4X4),
                         lhsT_scale=scales[:, g, P * t : P * (t + 1)],
                         rhs=z_w[:, g, cols].bitcast(FP8X4),
                         rhs_scale=z_s[:, g, cols],
-                        start=(g == 1),
-                        stop=(g == 0),
+                        start=(g == 0),
+                        stop=(g == 1),
                     )
+
+        def finish(u, t0, t1, acc):
             part = slice(P * t0, P * t1)
             nc.scalar.activation(absy[u][:, part], acc[:, 0 : P * (t1 - t0)], ACT.Abs)
             nc.scalar.activation(expy[u][:, part], absy[u][:, part], ACT.Exp, scale=-1.0)
@@ -216,68 +182,64 @@ def tile_list_voxel_edge_opacity_kernel(tc, tab_words, tab_scales, offs, pos1, p
             rows = out[P * t0 : P * t1, cols].rearrange("(t n) m -> n t m", n=P)
             nc.sync.dma_start(out=rows, in_=res[u][:, t0:t1, :])
 
-        gather_table_words(0, 0, S)
+        gather_table_words(0)
         nc.vector.tensor_copy(out=v_s[:], in_=tab_s[:].bitcast(U8).indirect(offs_sb[:]))
-        cast_w1(0)
-        quantize_w1(0)
-        gather_table_words(1, 0, BANK)
-        gather_table_words(1, BANK, S)
-        make_h(0)
-        cast_w1(1)
-        quantize_w1(1)
-        for c in range(CHUNKS):
-            last = 4 if c < 5 else 2
-            if c + 2 < CHUNKS:
-                cast_w1(c + 2)
-            gather_near(c, 0, last)
-            if c + 1 < CHUNKS - 1:
-                make_h(c + 1)
-            if c + 2 < CHUNKS:
-                quantize_w1(c + 2)
-            if c == 5:
-                make_h(7)
-            gather_far(c, 0, last)
-            if c >= 1:
-                mix_chunk(c - 1, 0, 4 if c - 1 < 5 else 2, banks[3] if c == 6 else banks[4 + c % 2])
-            if c == 5:
-                turn_back(0, 0, 2, banks[6], False)
-                quantize_z(0, 0, 2)
-            if c == 6:
-                turn_back(0, 2, 4, banks[7], False)
-                quantize_z(0, 2, 4)
-        mix_chunk(7, 0, 2, banks[0])
-        turn_back(1, 0, 2, banks[6], False)
-        late[(5, 2)] = near[5][:, 0:P], far3[5][:, 0:P]
-        late[(6, 2)] = near[5][:, P : 2 * P], far3[5][:, P : 2 * P]
-        late[(5, 3)] = near[7][:, 0:P], far3[7][:, 0:P]
-        for c in range(5, CHUNKS):
-            gather_near(c, 2, 3)
-            gather_far(c, 2, 3)
-        mix_samples(2, 5, CHUNKS, banks[0], False)
-        gather_near(5, 3, 4)
-        gather_far(5, 3, 4)
-        quantize_z(1, 0, 2)
-        turn_back(1, 2, 3, banks[4], False)
-        last_picks = tile([P, 4, P], F32, "last_picks", tag="z_bf10")
-        late[(6, 3)] = last_picks[:, 0, :], last_picks[:, 1, :]
-        late[(7, 3)] = last_picks[:, 2, :], last_picks[:, 3, :]
-        for c in range(6, CHUNKS):
-            gather_near(c, 3, 4)
-            gather_far(c, 3, 4)
-        finish(0, 0, 4, banks[2])
-        finish(1, 0, 4, banks[3])
+        gather_table_words(1)
+        cast_w1(0, 0, 0, 0, 48, False)
+        cast_w1(0, 0, 0, 48, P, True)
+        cast_w1(0, 1, 0, 0, 80, False)
+        quantize_w1(0, 0, 0, PACK)
+        h_pass(0, 0, 0)
+        cast_w1(0, 1, 80, 80, P, True)
+        for t0, t1 in ((0, 1), (1, 2), (2, 4)):
+            quantize_w1(0, 1, t0, t1)
+        h_pass(0, 0, 1)
+        for t in range(1, PACK):
+            h_pass(0, t, 1, True)
+            h_pass(0, t, 0, True)
+        for t in range(PACK):
+            copy_h(t, t == 0)
+            gather_near(t)
+            gather_far(sum0[:, t, :], t, 0, 4)
+            if t == 2:
+                for a in range(2):
+                    w1_bf[(1, a)] = tile([P, PACK, P, PACK], BF16, "w1_bf1%d" % a, tag="w1_w0%d" % a)
+                    cast_w1(1, a, 0, 0, P, False)
+                    quantize_w1(1, a, 0, PACK)
+        sum1[0] = tile([P, PACK, P], F32, "sum1_0")
+        for t in range(PACK):
+            h_pass(1, t, 1, True)
+            h_pass(1, t, 0, True)
+            copy_h(t)
+            gather_near(t)
+            gather_far(sum1[0][:, t, :], t, 0, 1)
+        relu(0, 0, 2, sum0[:, :, 0 : 2 * P], "w1_w10")
+        quantize_z(0, 0, 2)
+        relu(0, 2, 4, sum0[:, :, 2 * P : 4 * P], "w1_s10")
+        quantize_z(0, 2, 4)
+        relu(1, 0, 1, sum1[0][:], "z_bf10")
+        far_block(1, "sum0")
+        quantize_z(1, 0, 1)
+        density(0, 0, 4, banks[0])
+        relu(1, 1, 2, sum1[1][:], "z_bf11")
+        far_block(2, "z_bf10")
+        quantize_z(1, 1, 2)
+        finish(0, 0, 4, banks[0])
+        density(1, 0, 4, banks[1])
+        relu(1, 2, 3, sum1[2][:], "z_bf12")
+        far_block(3, "z_bf11")
         quantize_z(1, 2, 3)
-        mix_samples(3, 5, 7, banks[6], True)
-        mix_samples(3, 7, 8, banks[4], True)
-        turn_back(1, 3, 4, banks[0], True)
+        finish(1, 0, 4, banks[1])
+        density(2, 0, 4, banks[2])
+        relu(1, 3, 4, sum1[3][:], "z_bf13", True)
+        store(0, 0, 4)
         quantize_z(1, 3, 4)
-        first_res = tile([P, 2, 4, P], F32, "first_res", tag="z_bf12")
-        for u in range(2):
-            res[u] = first_res[:, u]
-            store(u, 0, 4)
-        finish(2, 0, 4, banks[5])
-        finish(3, 0, 2, banks[7])
-        finish(3, 2, 4, banks[1])
+        store(1, 0, 4)
+        finish(2, 0, 4, banks[2])
+        density(3, 0, 2, banks[3])
+        density(3, 2, 4, banks[4])
         store(2, 0, 4)
+        finish(3, 0, 2, banks[3])
         store(3, 0, 2)
+        finish(3, 2, 4, banks[4])
         store(3, 2, 4)

@@ -40,11 +40,14 @@ def tile_list_voxel_edge_opacity_kernel(tc, tab_words, tab_scales, offs, pos1, p
         v_w = [tile([P, S], U32, "v_w%d" % a) for a in range(2)]
         v_s = tile([P, S], U8, "v_s")
         w1_raw = {}
-        w1_bf = {(0, a): tile([P, PACK, P, PACK], BF16, "w1_bf0%d" % a) for a in range(2)}
-        w1_w = {(g, a): tile([P, BANK], U32, "w1_w%d%d" % (g, a)) for g in range(2) for a in range(2)}
-        w1_s = {(g, a): tile([P, BANK], U8, "w1_s%d%d" % (g, a)) for g in range(2) for a in range(2)}
+        w1_bf = {}
+        low_raw = [tile([P, 2, PACK, P * n], F32, "low_raw%d" % i) for i, n in enumerate((1, 1, 2))]
+        low_bf = [tile([P, 2, P, PACK], BF16, "low_bf%d" % c) for c in range(PACK)]
+        low_sum = {}
+        w1_w = {}
+        w1_s = {}
         h = [tile([P, WINDOW], F32, "h%d" % t) for t in range(PACK)]
-        near3 = [tile([P, M], F32, "near3_%d" % t) for t in range(PACK)]
+        near3 = {}
         sum0 = tile([P, PACK, M], F32, "sum0")
         sum1 = {}
         z_bf = {}
@@ -71,16 +74,23 @@ def tile_list_voxel_edge_opacity_kernel(tc, tab_words, tab_scales, offs, pos1, p
             rows = w1[512 * a : 512 * (a + 1), 512 * g + PACK * m0 : 512 * g + PACK * m1]
             nc.sync.dma_start(out=w1_raw[(g, a, m0)][:], in_=rows.rearrange("(p j) c -> p j c", j=PACK))
 
+        def load_low(i, a):
+            width = low_raw[i].shape[3]
+            rows = w1[512 * a : 512 * (a + 1), P * i : P * i + width]
+            nc.sync.dma_start(out=low_raw[i][:, a], in_=rows.rearrange("(p j) c -> p j c", j=PACK))
+
+        nc.sync.dma_start(pos2_sb[:], pos2)
+        nc.sync.dma_start(pos1_sb[:], pos1)
         nc.sync.dma_start(offs_sb[:], offs)
         load_table_words(0)
         for q in range(4):
             nc.sync.dma_start(out=tab_s[32 * q : 32 * q + 8, :], in_=tab_scales[:, 4 * q : 4 * q + 4, :].bitcast(I32))
+        load_low(0, 0)
         load_table_words(1)
-        load_w1(0, 0, 0, P)
-        load_w1(0, 1, 0, 80)
-        load_w1(0, 1, 80, P)
-        nc.sync.dma_start(pos2_sb[:], pos2)
-        nc.sync.dma_start(pos1_sb[:], pos1)
+        load_low(0, 1)
+        for i in (1, 2):
+            for a in range(2):
+                load_low(i, a)
         load_w1(1, 0, 0, P)
         load_w1(1, 1, 0, P)
         nc.sync.dma_start(out=w2_w[:], in_=w2_words.rearrange("a p b -> p a b").bitcast(I32))
@@ -88,37 +98,63 @@ def tile_list_voxel_edge_opacity_kernel(tc, tab_words, tab_scales, offs, pos1, p
             rows = w2_scales[:, 4 * q : 4 * q + 4, :].rearrange("a r n -> r a n")
             nc.sync.dma_start(out=w2_s[32 * q : 32 * q + 4, :, :], in_=rows.bitcast(I32))
 
-        def gather_table_words(a):
-            nc.vector.tensor_copy(out=v_w[a][:], in_=tab_w[a][:].bitcast(U32).indirect(offs_sb[:]))
+        def gather_table_words(a, first, last):
+            window = tab_w[a][:].bitcast(U32)
+            nc.vector.tensor_copy(out=v_w[a][:, first:last], in_=window.indirect(offs_sb[:, first // 16 : last // 16]))
+
+        def cast_low(c, a0, a1, on_vector):
+            i = min(c, 2)
+            src = low_raw[i][:, a0:a1, :, P * (c - i) : P * (c - i + 1)].rearrange("p a j c -> p a c j")
+            if on_vector:
+                nc.gpsimd.tensor_scalar(low_bf[c][:, a0:a1], src, 1.0, 0.0, ALU.mult, ALU.add)
+            else:
+                nc.scalar.copy(out=low_bf[c][:, a0:a1], in_=src)
+
+        def quantize_low(c, a0, a1):
+            codes = tile([P, P * (a1 - a0)], U32, "low_w%d%d" % (c, a0))
+            scales = tile([P, P * (a1 - a0)], U8, "low_s%d%d" % (c, a0))
+            for a in range(a0, a1):
+                w1_w[(0, a, c)] = codes[:, P * (a - a0) : P * (a - a0 + 1)]
+                w1_s[(0, a, c)] = scales[:, P * (a - a0) : P * (a - a0 + 1)]
+            nc.vector.quantize_mx(
+                out=codes[:].bitcast(FP8X4), scales=scales[:], in_=low_bf[c][:, a0:a1].rearrange("p a c j -> p (a c j)")
+            )
 
         def cast_w1(g, a, first, m0, m1, on_vector):
             src = w1_raw[(g, a, first)][:, :, PACK * (m0 - first) : PACK * (m1 - first)].rearrange("p j (m t) -> p m t j", t=PACK)
             dst = w1_bf[(g, a)][:, :, m0:m1, :].rearrange("p t m j -> p m t j")
             if on_vector:
-                nc.vector.tensor_copy(out=dst, in_=src)
+                nc.gpsimd.tensor_scalar(dst, src, 1.0, 0.0, ALU.mult, ALU.add)
             else:
                 nc.scalar.copy(out=dst, in_=src)
 
         def quantize_w1(g, a, t0, t1):
-            cols = slice(P * t0, P * t1)
+            codes = tile([P, P * (t1 - t0)], U32, "w1_w%d%d%d" % (g, a, t0))
+            scales = tile([P, P * (t1 - t0)], U8, "w1_s%d%d%d" % (g, a, t0))
+            for t in range(t0, t1):
+                w1_w[(g, a, t)] = codes[:, P * (t - t0) : P * (t - t0 + 1)]
+                w1_s[(g, a, t)] = scales[:, P * (t - t0) : P * (t - t0 + 1)]
             nc.vector.quantize_mx(
-                out=w1_w[(g, a)][:, cols].bitcast(FP8X4),
-                scales=w1_s[(g, a)][:, cols],
+                out=codes[:].bitcast(FP8X4),
+                scales=scales[:],
                 in_=w1_bf[(g, a)][:, t0:t1].rearrange("p t m j -> p (t m j)"),
             )
 
-        def h_pass(g, t, a, backwards=False):
-            for half in range(2):
+        def h_passes(g, t, order, first):
+            for half, a in order:
                 cols = slice(BANK * half, BANK * (half + 1))
                 nc.tensor.matmul_mx(
                     out=banks[2 * t + half][:],
-                    lhsT=w1_w[(g, a)][:, P * t : P * (t + 1)].bitcast(FP8X4),
-                    lhsT_scale=w1_s[(g, a)][:, P * t : P * (t + 1)],
+                    lhsT=w1_w[(g, a, t)].bitcast(FP8X4),
+                    lhsT_scale=w1_s[(g, a, t)],
                     rhs=v_w[a][:, cols].bitcast(FP8X4),
                     rhs_scale=v_s[4 * a :, cols],
-                    start=(a == int(backwards)),
-                    stop=(a != int(backwards)),
+                    start=(a == first),
+                    stop=(a != first),
                 )
+
+        def make_h(g, t):
+            h_passes(g, t, ((0, 1), (0, 0), (1, 1), (1, 0)), 1)
 
         def copy_h(t, second_on_vector=False):
             nc.scalar.copy(out=h[t][:, 0:BANK], in_=banks[2 * t][:])
@@ -149,7 +185,8 @@ def tile_list_voxel_edge_opacity_kernel(tc, tab_words, tab_scales, offs, pos1, p
             )
 
         def far_block(u, tag):
-            sum1[u] = tile([P, PACK, P], F32, "sum1_%d" % u, tag=tag)
+            if tag:
+                sum1[u] = tile([P, PACK, P], F32, "sum1_%d" % u, tag=tag)[:]
             for t in range(PACK):
                 gather_far(sum1[u][:, t, :], t, u, u + 1)
 
@@ -182,56 +219,69 @@ def tile_list_voxel_edge_opacity_kernel(tc, tab_words, tab_scales, offs, pos1, p
             rows = out[P * t0 : P * t1, cols].rearrange("(t n) m -> n t m", n=P)
             nc.sync.dma_start(out=rows, in_=res[u][:, t0:t1, :])
 
-        gather_table_words(0)
+        gather_table_words(0, 0, S)
         nc.vector.tensor_copy(out=v_s[:], in_=tab_s[:].bitcast(U8).indirect(offs_sb[:]))
-        gather_table_words(1)
-        cast_w1(0, 0, 0, 0, 48, False)
-        cast_w1(0, 0, 0, 48, P, True)
-        cast_w1(0, 1, 0, 0, 80, False)
-        quantize_w1(0, 0, 0, PACK)
-        h_pass(0, 0, 0)
-        cast_w1(0, 1, 80, 80, P, True)
-        for t0, t1 in ((0, 1), (1, 2), (2, 4)):
-            quantize_w1(0, 1, t0, t1)
-        h_pass(0, 0, 1)
-        for t in range(1, PACK):
-            h_pass(0, t, 1, True)
-            h_pass(0, t, 0, True)
+        cast_low(0, 0, 1, False)
+        quantize_low(0, 0, 1)
+        h_passes(0, 0, ((0, 0), (1, 0)), 0)
+        gather_table_words(1, 0, BANK)
+        cast_low(0, 1, 2, False)
+        quantize_low(0, 1, 2)
+        gather_table_words(1, BANK, S)
+        h_passes(0, 0, ((0, 1), (1, 1)), 0)
+        cast_low(1, 0, 2, False)
+        quantize_low(1, 0, 2)
+        low_near3 = tile([P, M], F32, "low_near3", tag="low_bf1")
+        for c in range(PACK):
+            near3[c] = low_near3
+        for c in range(PACK):
+            if c == 2:
+                w1_bf[(1, 0)] = tile([P, PACK, P, PACK], BF16, "w1_bf10")
+                cast_w1(1, 0, 0, 0, P, False)
+                w1_bf[(1, 1)] = tile([P, PACK, P, PACK], BF16, "w1_bf11")
+                for m0 in range(0, P, 32):
+                    cast_w1(1, 1, 0, m0, m0 + 32, True)
+            copy_h(c, c == 0)
+            if c + 1 < PACK:
+                make_h(0, c + 1)
+            if c + 2 < PACK:
+                cast_low(c + 2, 0, 2, True)
+            gather_near(c)
+            if c + 2 < PACK:
+                quantize_low(c + 2, 0, 2)
+            elif c == 2:
+                quantize_w1(1, 0, 0, PACK)
+                quantize_w1(1, 1, 0, PACK)
+            low_sum[c] = tile([P, M], F32, "low_sum%d" % c, tag=("low_bf2", "low_bf3", "w1_bf11", None)[c])
+            gather_far(low_sum[c][:], c, 0, 4)
+            nc.sync.dma_start(out=sum0[32 * c : 32 * (c + 1)], in_=low_sum[c][:])
         for t in range(PACK):
-            copy_h(t, t == 0)
-            gather_near(t)
-            gather_far(sum0[:, t, :], t, 0, 4)
-            if t == 2:
-                for a in range(2):
-                    w1_bf[(1, a)] = tile([P, PACK, P, PACK], BF16, "w1_bf1%d" % a, tag="w1_w0%d" % a)
-                    cast_w1(1, a, 0, 0, P, False)
-                    quantize_w1(1, a, 0, PACK)
-        sum1[0] = tile([P, PACK, P], F32, "sum1_0")
-        for t in range(PACK):
-            h_pass(1, t, 1, True)
-            h_pass(1, t, 0, True)
+            near3[t] = tile([P, M], F32, "near3_%d" % t)
+            make_h(1, t)
             copy_h(t)
             gather_near(t)
-            gather_far(sum1[0][:, t, :], t, 0, 1)
-        relu(0, 0, 2, sum0[:, :, 0 : 2 * P], "w1_w10")
+        relu(0, 0, 2, sum0[:, :, 0 : 2 * P], "w1_w100")
         quantize_z(0, 0, 2)
-        relu(0, 2, 4, sum0[:, :, 2 * P : 4 * P], "w1_s10")
+        relu(0, 2, 4, sum0[:, :, 2 * P : 4 * P], "w1_s100")
         quantize_z(0, 2, 4)
-        relu(1, 0, 1, sum1[0][:], "z_bf10")
-        far_block(1, "sum0")
+        first_sums = tile([P, 2, PACK, P], F32, "first_sums", tag="sum0")
+        sum1[0], sum1[1] = first_sums[:, 0], first_sums[:, 1]
+        far_block(0, None)
+        relu(1, 0, 1, sum1[0], "w1_w100")
+        far_block(1, None)
         quantize_z(1, 0, 1)
         density(0, 0, 4, banks[0])
-        relu(1, 1, 2, sum1[1][:], "z_bf11")
-        far_block(2, "z_bf10")
+        relu(1, 1, 2, sum1[1], "z_bf11")
+        far_block(2, "w1_w100")
         quantize_z(1, 1, 2)
         finish(0, 0, 4, banks[0])
         density(1, 0, 4, banks[1])
-        relu(1, 2, 3, sum1[2][:], "z_bf12")
+        relu(1, 2, 3, sum1[2], "z_bf12")
         far_block(3, "z_bf11")
         quantize_z(1, 2, 3)
         finish(1, 0, 4, banks[1])
         density(2, 0, 4, banks[2])
-        relu(1, 3, 4, sum1[3][:], "z_bf13", True)
+        relu(1, 3, 4, sum1[3], "z_bf13", True)
         store(0, 0, 4)
         quantize_z(1, 3, 4)
         store(1, 0, 4)

@@ -38,20 +38,23 @@ def tile_list_voxel_edge_opacity_kernel(tc, tab_words, tab_scales, offs, pos1, p
         tab_w = [tile([P, T], I32, "tab_w%d" % a) for a in range(2)]
         tab_s = tile([P, T // 4], I32, "tab_s")
         v_w = [tile([P, S], U32, "v_w%d" % a) for a in range(2)]
-        v_s = tile([P, S], U8, "v_s")
+        v_rows = tile([P, S], U8, "v_rows")
+        v_s = tile([P, 2, S // 4], I32, "v_s")
         w1_raw = {}
         w1_bf = {}
-        low_raw = [tile([P, 2, PACK, P * n], F32, "low_raw%d" % i) for i, n in enumerate((1, 1, 2))]
         low_bf = [tile([P, 2, P, PACK], BF16, "low_bf%d" % c) for c in range(PACK)]
         low_sum = {}
         w1_w = {}
         w1_s = {}
         h = [tile([P, WINDOW], F32, "h%d" % t) for t in range(PACK)]
+        low_raw = [h[c][:, S:WINDOW].rearrange("p (a j c) -> p a j c", a=2, j=PACK) for c in range(2)]
+        low_raw.append(tile([P, 2, PACK, 2 * P], F32, "low_raw2")[:])
         near3 = {}
         sum0 = tile([P, PACK, M], F32, "sum0")
         sum1 = {}
         z_bf = {}
         warm = tile([P, 1], F32, "warm")
+        zero = tile([P, 1], F32, "zero")
         z_w = tile([P, 2, M], U32, "z_w")
         z_s = tile([P, 2, M], U8, "z_s")
         w2_w = tile([P, 2, 2 * N // 4], I32, "w2_w")
@@ -60,37 +63,38 @@ def tile_list_voxel_edge_opacity_kernel(tc, tab_words, tab_scales, offs, pos1, p
         expy = [tile([P, BANK], F32, "expy%d" % u) for u in range(4)]
         res = [tile([P, 4, P], F32, "res%d" % u) for u in range(4)]
 
-        nc.vector.memset(tab_s[:], 0)
+        nc.vector.memset(tab_s[32:64, :], 0)
+        nc.vector.memset(tab_s[64:P, :], 0)
+        nc.vector.memset(v_s[:], 0)
         nc.vector.memset(w2_s[:], 0)
-        for t in range(PACK):
-            nc.vector.memset(h[t][:, S:WINDOW], 0.0)
-        nc.scalar.activation(warm[:], h[0][:, S : S + 1], ACT.Exp, scale=-1.0)
+        nc.vector.memset(zero[:], 0.0)
+        nc.scalar.activation(warm[:], zero[:], ACT.Exp, scale=-1.0)
 
         def load_table_words(a):
             nc.sync.dma_start(out=tab_w[a][:], in_=tab_words[a].rearrange("p t i -> p (t i)").bitcast(I32))
 
         def load_w1(g, a, m0, m1):
-            w1_raw[(g, a, m0)] = tile([P, PACK, PACK * (m1 - m0)], F32, "w1_raw%d%d_%d" % (g, a, m0))
+            w1_raw[(g, a, m0)] = h[2 + a][:].rearrange("p (j c) -> p j c", j=PACK)
             rows = w1[512 * a : 512 * (a + 1), 512 * g + PACK * m0 : 512 * g + PACK * m1]
-            nc.sync.dma_start(out=w1_raw[(g, a, m0)][:], in_=rows.rearrange("(p j) c -> p j c", j=PACK))
+            nc.sync.dma_start(out=w1_raw[(g, a, m0)], in_=rows.rearrange("(p j) c -> p j c", j=PACK))
 
         def load_low(i, a):
             width = low_raw[i].shape[3]
             rows = w1[512 * a : 512 * (a + 1), P * i : P * i + width]
             nc.sync.dma_start(out=low_raw[i][:, a], in_=rows.rearrange("(p j) c -> p j c", j=PACK))
 
-        nc.sync.dma_start(pos2_sb[:], pos2)
-        nc.sync.dma_start(pos1_sb[:], pos1)
         nc.sync.dma_start(offs_sb[:], offs)
+        nc.sync.dma_start(out=tab_s[0:32, :], in_=tab_scales.rearrange("a s t -> s a t").bitcast(I32))
         load_table_words(0)
-        for q in range(4):
-            nc.sync.dma_start(out=tab_s[32 * q : 32 * q + 8, :], in_=tab_scales[:, 4 * q : 4 * q + 4, :].bitcast(I32))
         load_low(0, 0)
         load_table_words(1)
         load_low(0, 1)
-        for i in (1, 2):
-            for a in range(2):
-                load_low(i, a)
+        for a in range(2):
+            load_low(1, a)
+        nc.sync.dma_start(pos2_sb[:], pos2)
+        nc.sync.dma_start(pos1_sb[:], pos1)
+        for a in range(2):
+            load_low(2, a)
         load_w1(1, 0, 0, P)
         load_w1(1, 1, 0, P)
         nc.sync.dma_start(out=w2_w[:], in_=w2_words.rearrange("a p b -> p a b").bitcast(I32))
@@ -106,7 +110,7 @@ def tile_list_voxel_edge_opacity_kernel(tc, tab_words, tab_scales, offs, pos1, p
             i = min(c, 2)
             src = low_raw[i][:, a0:a1, :, P * (c - i) : P * (c - i + 1)].rearrange("p a j c -> p a c j")
             if on_vector:
-                nc.gpsimd.tensor_scalar(low_bf[c][:, a0:a1], src, 1.0, 0.0, ALU.mult, ALU.add)
+                nc.vector.tensor_copy(out=low_bf[c][:, a0:a1], in_=src)
             else:
                 nc.scalar.copy(out=low_bf[c][:, a0:a1], in_=src)
 
@@ -148,7 +152,7 @@ def tile_list_voxel_edge_opacity_kernel(tc, tab_words, tab_scales, offs, pos1, p
                     lhsT=w1_w[(g, a, t)].bitcast(FP8X4),
                     lhsT_scale=w1_s[(g, a, t)],
                     rhs=v_w[a][:, cols].bitcast(FP8X4),
-                    rhs_scale=v_s[4 * a :, cols],
+                    rhs_scale=v_s[:, a, :].bitcast(U8)[:, cols],
                     start=(a == first),
                     stop=(a != first),
                 )
@@ -219,8 +223,10 @@ def tile_list_voxel_edge_opacity_kernel(tc, tab_words, tab_scales, offs, pos1, p
             rows = out[P * t0 : P * t1, cols].rearrange("(t n) m -> n t m", n=P)
             nc.sync.dma_start(out=rows, in_=res[u][:, t0:t1, :])
 
+        nc.vector.tensor_copy(out=v_rows[:], in_=tab_s[:].bitcast(U8).indirect(offs_sb[:]))
+        for q in range(4):
+            nc.scalar.dma_start(out=v_s[32 * q : 32 * q + 4], in_=v_rows[8 * q : 8 * q + 8, :].bitcast(I32))
         gather_table_words(0, 0, S)
-        nc.vector.tensor_copy(out=v_s[:], in_=tab_s[:].bitcast(U8).indirect(offs_sb[:]))
         cast_low(0, 0, 1, False)
         quantize_low(0, 0, 1)
         h_passes(0, 0, ((0, 0), (1, 0)), 0)
@@ -235,12 +241,10 @@ def tile_list_voxel_edge_opacity_kernel(tc, tab_words, tab_scales, offs, pos1, p
         for c in range(PACK):
             near3[c] = low_near3
         for c in range(PACK):
-            if c == 2:
-                w1_bf[(1, 0)] = tile([P, PACK, P, PACK], BF16, "w1_bf10")
-                cast_w1(1, 0, 0, 0, P, False)
-                w1_bf[(1, 1)] = tile([P, PACK, P, PACK], BF16, "w1_bf11")
-                for m0 in range(0, P, 32):
-                    cast_w1(1, 1, 0, m0, m0 + 32, True)
+            if c >= 2:
+                w1_bf[(1, c - 2)] = tile([P, PACK, P, PACK], BF16, "w1_bf1%d" % (c - 2))
+                cast_w1(1, c - 2, 0, 0, P, False)
+                quantize_w1(1, c - 2, 0, PACK)
             copy_h(c, c == 0)
             if c + 1 < PACK:
                 make_h(0, c + 1)
@@ -249,10 +253,7 @@ def tile_list_voxel_edge_opacity_kernel(tc, tab_words, tab_scales, offs, pos1, p
             gather_near(c)
             if c + 2 < PACK:
                 quantize_low(c + 2, 0, 2)
-            elif c == 2:
-                quantize_w1(1, 0, 0, PACK)
-                quantize_w1(1, 1, 0, PACK)
-            low_sum[c] = tile([P, M], F32, "low_sum%d" % c, tag=("low_bf2", "low_bf3", "w1_bf11", None)[c])
+            low_sum[c] = tile([P, M], F32, "low_sum%d" % c, tag=("low_bf2", "low_bf3", None, None)[c])
             gather_far(low_sum[c][:], c, 0, 4)
             nc.sync.dma_start(out=sum0[32 * c : 32 * (c + 1)], in_=low_sum[c][:])
         for t in range(PACK):
@@ -264,20 +265,20 @@ def tile_list_voxel_edge_opacity_kernel(tc, tab_words, tab_scales, offs, pos1, p
         quantize_z(0, 0, 2)
         relu(0, 2, 4, sum0[:, :, 2 * P : 4 * P], "w1_s100")
         quantize_z(0, 2, 4)
-        first_sums = tile([P, 2, PACK, P], F32, "first_sums", tag="sum0")
+        first_sums = tile([P, 2, PACK, P], F32, "first_sums", tag="w1_w110")
         sum1[0], sum1[1] = first_sums[:, 0], first_sums[:, 1]
         far_block(0, None)
-        relu(1, 0, 1, sum1[0], "w1_w100")
+        relu(1, 0, 1, sum1[0], "sum0")
         far_block(1, None)
         quantize_z(1, 0, 1)
         density(0, 0, 4, banks[0])
-        relu(1, 1, 2, sum1[1], "z_bf11")
-        far_block(2, "w1_w100")
+        relu(1, 1, 2, sum1[1], "w1_s100")
+        far_block(2, "sum0")
         quantize_z(1, 1, 2)
         finish(0, 0, 4, banks[0])
         density(1, 0, 4, banks[1])
         relu(1, 2, 3, sum1[2], "z_bf12")
-        far_block(3, "z_bf11")
+        far_block(3, "w1_s100")
         quantize_z(1, 2, 3)
         finish(1, 0, 4, banks[1])
         density(2, 0, 4, banks[2])

@@ -42,14 +42,10 @@ def tile_list_voxel_edge_opacity_kernel(tc, tab_words, tab_scales, offs, pos1, p
         v_s = tile([P, 2, S // 4], I32, "v_s")
         w1_raw = {}
         w1_bf = {}
-        low_bf = [tile([P, 2, P, PACK], BF16, "low_bf%d" % c) for c in range(PACK)]
-        low_sum = {}
         w1_w = {}
         w1_s = {}
         h = [tile([P, WINDOW], F32, "h%d" % t) for t in range(PACK)]
-        low_raw = [h[c][:, S:WINDOW].rearrange("p (a j c) -> p a j c", a=2, j=PACK) for c in range(2)]
-        low_raw.append(tile([P, 2, PACK, 2 * P], F32, "low_raw2")[:])
-        near3 = {}
+        near3 = [tile([P, M], F32, "near3_%d" % t) for t in range(PACK)]
         sum0 = tile([P, PACK, M], F32, "sum0")
         sum1 = {}
         z_bf = {}
@@ -73,30 +69,22 @@ def tile_list_voxel_edge_opacity_kernel(tc, tab_words, tab_scales, offs, pos1, p
         def load_table_words(a):
             nc.sync.dma_start(out=tab_w[a][:], in_=tab_words[a].rearrange("p t i -> p (t i)").bitcast(I32))
 
-        def load_w1(g, a, m0, m1):
-            w1_raw[(g, a, m0)] = h[2 + a][:].rearrange("p (j c) -> p j c", j=PACK)
+        def load_w1(g, a, m0, m1, stage):
+            w1_raw[(g, a, m0)] = stage.rearrange("p (j c) -> p j c", j=PACK)
             rows = w1[512 * a : 512 * (a + 1), 512 * g + PACK * m0 : 512 * g + PACK * m1]
             nc.sync.dma_start(out=w1_raw[(g, a, m0)], in_=rows.rearrange("(p j) c -> p j c", j=PACK))
-
-        def load_low(i, a):
-            width = low_raw[i].shape[3]
-            rows = w1[512 * a : 512 * (a + 1), P * i : P * i + width]
-            nc.sync.dma_start(out=low_raw[i][:, a], in_=rows.rearrange("(p j) c -> p j c", j=PACK))
 
         nc.sync.dma_start(offs_sb[:], offs)
         nc.sync.dma_start(out=tab_s[0:32, :], in_=tab_scales.rearrange("a s t -> s a t").bitcast(I32))
         load_table_words(0)
-        load_low(0, 0)
         load_table_words(1)
-        load_low(0, 1)
-        for a in range(2):
-            load_low(1, a)
+        load_w1(0, 0, 0, P, tile([P, WINDOW], F32, "first_raw")[:])
+        load_w1(0, 1, 0, 64, h[0][:, S:WINDOW])
+        load_w1(0, 1, 64, P, h[1][:, S:WINDOW])
         nc.sync.dma_start(pos2_sb[:], pos2)
         nc.sync.dma_start(pos1_sb[:], pos1)
-        for a in range(2):
-            load_low(2, a)
-        load_w1(1, 0, 0, P)
-        load_w1(1, 1, 0, P)
+        load_w1(1, 0, 0, P, h[2][:])
+        load_w1(1, 1, 0, P, h[3][:])
         nc.sync.dma_start(out=w2_w[:], in_=w2_words.rearrange("a p b -> p a b").bitcast(I32))
         for q in range(4):
             rows = w2_scales[:, 4 * q : 4 * q + 4, :].rearrange("a r n -> r a n")
@@ -106,29 +94,11 @@ def tile_list_voxel_edge_opacity_kernel(tc, tab_words, tab_scales, offs, pos1, p
             window = tab_w[a][:].bitcast(U32)
             nc.vector.tensor_copy(out=v_w[a][:, first:last], in_=window.indirect(offs_sb[:, first // 16 : last // 16]))
 
-        def cast_low(c, a0, a1, on_vector):
-            i = min(c, 2)
-            src = low_raw[i][:, a0:a1, :, P * (c - i) : P * (c - i + 1)].rearrange("p a j c -> p a c j")
-            if on_vector:
-                nc.vector.tensor_copy(out=low_bf[c][:, a0:a1], in_=src)
-            else:
-                nc.scalar.copy(out=low_bf[c][:, a0:a1], in_=src)
-
-        def quantize_low(c, a0, a1):
-            codes = tile([P, P * (a1 - a0)], U32, "low_w%d%d" % (c, a0))
-            scales = tile([P, P * (a1 - a0)], U8, "low_s%d%d" % (c, a0))
-            for a in range(a0, a1):
-                w1_w[(0, a, c)] = codes[:, P * (a - a0) : P * (a - a0 + 1)]
-                w1_s[(0, a, c)] = scales[:, P * (a - a0) : P * (a - a0 + 1)]
-            nc.vector.quantize_mx(
-                out=codes[:].bitcast(FP8X4), scales=scales[:], in_=low_bf[c][:, a0:a1].rearrange("p a c j -> p (a c j)")
-            )
-
         def cast_w1(g, a, first, m0, m1, on_vector):
             src = w1_raw[(g, a, first)][:, :, PACK * (m0 - first) : PACK * (m1 - first)].rearrange("p j (m t) -> p m t j", t=PACK)
             dst = w1_bf[(g, a)][:, :, m0:m1, :].rearrange("p t m j -> p m t j")
             if on_vector:
-                nc.gpsimd.tensor_scalar(dst, src, 1.0, 0.0, ALU.mult, ALU.add)
+                nc.vector.tensor_copy(out=dst, in_=src)
             else:
                 nc.scalar.copy(out=dst, in_=src)
 
@@ -174,18 +144,18 @@ def tile_list_voxel_edge_opacity_kernel(tc, tab_words, tab_scales, offs, pos1, p
             window = h[t][:].indirect(pos1_sb[:, 8 * u0 : 8 * u1])
             nc.vector.tensor_tensor(dst, window, near3[t][:, P * u0 : P * u1], ALU.add)
 
-        def relu(g, u0, u1, src, tag, on_vector=False):
-            z_bf[(g, u0)] = tile([P, P * (u1 - u0), PACK], BF16, "z_bf%d%d" % (g, u0), tag=tag)
+        def relu(g, u0, u1, src, tag, on_vector=False, into=None):
+            z_bf[(g, u0)] = into if into is not None else tile([P, P * (u1 - u0), PACK], BF16, "z_bf%d%d" % (g, u0), tag=tag)[:]
             src = src.rearrange("p t m -> p m t")
             if on_vector:
-                nc.vector.tensor_scalar(z_bf[(g, u0)][:], src, 0.25, 0.0, ALU.mult, ALU.max)
+                nc.vector.tensor_scalar(z_bf[(g, u0)], src, 0.25, 0.0, ALU.mult, ALU.max)
             else:
-                nc.scalar.activation(z_bf[(g, u0)][:], src, ACT.Relu, scale=0.25)
+                nc.scalar.activation(z_bf[(g, u0)], src, ACT.Relu, scale=0.25)
 
         def quantize_z(g, u0, u1):
             cols = slice(P * u0, P * u1)
             nc.vector.quantize_mx(
-                out=z_w[:, g, cols].bitcast(FP8X4), scales=z_s[:, g, cols], in_=z_bf[(g, u0)][:].rearrange("p m i -> p (m i)")
+                out=z_w[:, g, cols].bitcast(FP8X4), scales=z_s[:, g, cols], in_=z_bf[(g, u0)].rearrange("p m i -> p (m i)")
             )
 
         def far_block(u, tag):
@@ -227,69 +197,63 @@ def tile_list_voxel_edge_opacity_kernel(tc, tab_words, tab_scales, offs, pos1, p
         for q in range(4):
             nc.scalar.dma_start(out=v_s[32 * q : 32 * q + 4], in_=v_rows[8 * q : 8 * q + 8, :].bitcast(I32))
         gather_table_words(0, 0, S)
-        cast_low(0, 0, 1, False)
-        quantize_low(0, 0, 1)
+        gather_table_words(1, 0, S)
+        for a in range(2):
+            w1_bf[(0, a)] = tile([P, PACK, P, PACK], BF16, "w1_bf0%d" % a)
+        cast_w1(0, 0, 0, 0, 48, False)
+        cast_w1(0, 0, 0, 48, P, True)
+        cast_w1(0, 1, 0, 0, 64, False)
+        quantize_w1(0, 0, 0, PACK)
         h_passes(0, 0, ((0, 0), (1, 0)), 0)
-        gather_table_words(1, 0, BANK)
-        cast_low(0, 1, 2, False)
-        quantize_low(0, 1, 2)
-        gather_table_words(1, BANK, S)
-        h_passes(0, 0, ((0, 1), (1, 1)), 0)
-        cast_low(1, 0, 2, False)
-        quantize_low(1, 0, 2)
-        low_near3 = tile([P, M], F32, "low_near3", tag="low_bf1")
-        for c in range(PACK):
-            near3[c] = low_near3
-        for c in range(PACK):
-            if c >= 2:
-                w1_bf[(1, c - 2)] = tile([P, PACK, P, PACK], BF16, "w1_bf1%d" % (c - 2))
-                cast_w1(1, c - 2, 0, 0, P, False)
-                quantize_w1(1, c - 2, 0, PACK)
-            copy_h(c, c == 0)
-            if c + 1 < PACK:
-                make_h(0, c + 1)
-            if c + 2 < PACK:
-                cast_low(c + 2, 0, 2, True)
-            gather_near(c)
-            if c + 2 < PACK:
-                quantize_low(c + 2, 0, 2)
-            low_sum[c] = tile([P, M], F32, "low_sum%d" % c, tag=("low_bf2", "low_bf3", None, None)[c])
-            gather_far(low_sum[c][:], c, 0, 4)
-            nc.sync.dma_start(out=sum0[32 * c : 32 * (c + 1)], in_=low_sum[c][:])
+        cast_w1(0, 1, 64, 64, P, True)
         for t in range(PACK):
-            near3[t] = tile([P, M], F32, "near3_%d" % t)
-            make_h(1, t)
+            quantize_w1(0, 1, t, t + 1)
+        h_passes(0, 0, ((0, 1), (1, 1)), 0)
+        for t in range(1, PACK):
+            make_h(0, t)
+        for t in range(PACK):
+            if t >= 2:
+                w1_bf[(1, t - 2)] = tile([P, PACK, P, PACK], BF16, "w1_bf1%d" % (t - 2))
+                cast_w1(1, t - 2, 0, 0, P if t == 2 else 96, False)
+                if t == 3:
+                    cast_w1(1, 1, 0, 96, P, True)
+                quantize_w1(1, t - 2, 0, PACK)
+            copy_h(t, t == 0)
+            gather_near(t)
+            gather_far(sum0[:, t, :], t, 0, 4)
+        for t in range(PACK):
+            h_passes(1, t, ((0, 0), (1, 0), (0, 1), (1, 1)), 0)
             copy_h(t)
             gather_near(t)
-        relu(0, 0, 2, sum0[:, :, 0 : 2 * P], "w1_w100")
+        relu(0, 0, 2, sum0[:, :, 0 : 2 * P], "w1_w110")
         quantize_z(0, 0, 2)
-        relu(0, 2, 4, sum0[:, :, 2 * P : 4 * P], "w1_s100")
+        relu(0, 2, 4, sum0[:, :, 2 * P : 4 * P], "w1_s110")
         quantize_z(0, 2, 4)
-        first_sums = tile([P, 2, PACK, P], F32, "first_sums", tag="w1_w110")
-        sum1[0], sum1[1] = first_sums[:, 0], first_sums[:, 1]
-        far_block(0, None)
-        relu(1, 0, 1, sum1[0], "sum0")
-        far_block(1, None)
+        far_block(0, "v_w1")
+        relu(1, 0, 1, sum1[0], None)
         quantize_z(1, 0, 1)
         density(0, 0, 4, banks[0])
-        relu(1, 1, 2, sum1[1], "w1_s100")
-        far_block(2, "sum0")
+        late_sums = tile([P, 3, PACK, P], F32, "late_sums", tag="sum0")
+        for u in range(1, 4):
+            sum1[u] = late_sums[:, u - 1]
+        far_block(1, None)
+        relu(1, 1, 2, sum1[1], None)
         quantize_z(1, 1, 2)
-        finish(0, 0, 4, banks[0])
         density(1, 0, 4, banks[1])
-        relu(1, 2, 3, sum1[2], "z_bf12")
-        far_block(3, "w1_s100")
+        far_block(2, None)
+        third = sum1[3][:, 2:4, :].rearrange("p t m -> p (t m)").bitcast(BF16).rearrange("p (m t) -> p m t", t=PACK)
+        relu(1, 2, 3, sum1[2], None, False, third)
         quantize_z(1, 2, 3)
-        finish(1, 0, 4, banks[1])
         density(2, 0, 4, banks[2])
-        relu(1, 3, 4, sum1[3], "z_bf13", True)
-        store(0, 0, 4)
+        far_block(3, None)
+        relu(1, 3, 4, sum1[3], None, True)
         quantize_z(1, 3, 4)
-        store(1, 0, 4)
-        finish(2, 0, 4, banks[2])
+        for u in range(3):
+            finish(u, 0, 4, banks[u])
         density(3, 0, 2, banks[3])
         density(3, 2, 4, banks[4])
-        store(2, 0, 4)
+        for u in range(3):
+            store(u, 0, 4)
         finish(3, 0, 2, banks[3])
         store(3, 0, 2)
         finish(3, 2, 4, banks[4])

@@ -60,7 +60,7 @@ def tile_list_voxel_edge_opacity_kernel(tc, tab_words, tab_scales, offs, pos1, p
         res = [tile([P, 4, P], F32, "res%d" % u) for u in range(4)]
 
         nc.vector.memset(tab_s[32:64, :], 0)
-        nc.vector.memset(tab_s[64:P, :], 0)
+        nc.gpsimd.memset(tab_s[64:P, :], 0)
         nc.vector.memset(v_s[:], 0)
         nc.vector.memset(w2_s[:], 0)
         nc.vector.memset(zero[:], 0.0)
@@ -77,13 +77,16 @@ def tile_list_voxel_edge_opacity_kernel(tc, tab_words, tab_scales, offs, pos1, p
         nc.sync.dma_start(offs_sb[:], offs)
         nc.sync.dma_start(out=tab_s[0:32, :], in_=tab_scales.rearrange("a s t -> s a t").bitcast(I32))
         load_table_words(0)
-        load_table_words(1)
         load_w1(0, 0, 0, P, tile([P, WINDOW], F32, "first_raw")[:])
+        nc.vector.tensor_copy(out=v_rows[:], in_=tab_s[:].bitcast(U8).indirect(offs_sb[:]))
+        for q in range(4):
+            nc.sync.dma_start(out=v_s[32 * q : 32 * q + 4], in_=v_rows[8 * q : 8 * q + 8, :].bitcast(I32))
+        load_table_words(1)
         load_w1(0, 1, 0, 64, h[0][:, S:WINDOW])
         load_w1(0, 1, 64, P, h[1][:, S:WINDOW])
         nc.sync.dma_start(pos2_sb[:], pos2)
-        nc.sync.dma_start(pos1_sb[:], pos1)
         load_w1(1, 0, 0, P, h[2][:])
+        nc.sync.dma_start(pos1_sb[:], pos1)
         load_w1(1, 1, 0, P, h[3][:])
         nc.sync.dma_start(out=w2_w[:], in_=w2_words.rearrange("a p b -> p a b").bitcast(I32))
         for q in range(4):
@@ -146,11 +149,12 @@ def tile_list_voxel_edge_opacity_kernel(tc, tab_words, tab_scales, offs, pos1, p
 
         def relu(g, u0, u1, src, tag, on_vector=False, into=None):
             z_bf[(g, u0)] = into if into is not None else tile([P, P * (u1 - u0), PACK], BF16, "z_bf%d%d" % (g, u0), tag=tag)[:]
-            src = src.rearrange("p t m -> p m t")
+            src = src.rearrange("p t (c i) -> p c t i", i=PACK)
+            dst = z_bf[(g, u0)].rearrange("p (c i) t -> p c t i", i=PACK)
             if on_vector:
-                nc.vector.tensor_scalar(z_bf[(g, u0)], src, 0.25, 0.0, ALU.mult, ALU.max)
+                nc.vector.tensor_scalar(dst, src, 0.25, 0.0, ALU.mult, ALU.max)
             else:
-                nc.scalar.activation(z_bf[(g, u0)], src, ACT.Relu, scale=0.25)
+                nc.scalar.activation(dst, src, ACT.Relu, scale=0.25)
 
         def quantize_z(g, u0, u1):
             cols = slice(P * u0, P * u1)
@@ -193,42 +197,34 @@ def tile_list_voxel_edge_opacity_kernel(tc, tab_words, tab_scales, offs, pos1, p
             rows = out[P * t0 : P * t1, cols].rearrange("(t n) m -> n t m", n=P)
             nc.sync.dma_start(out=rows, in_=res[u][:, t0:t1, :])
 
-        nc.vector.tensor_copy(out=v_rows[:], in_=tab_s[:].bitcast(U8).indirect(offs_sb[:]))
-        for q in range(4):
-            nc.scalar.dma_start(out=v_s[32 * q : 32 * q + 4], in_=v_rows[8 * q : 8 * q + 8, :].bitcast(I32))
         gather_table_words(0, 0, S)
-        gather_table_words(1, 0, S)
         for a in range(2):
             w1_bf[(0, a)] = tile([P, PACK, P, PACK], BF16, "w1_bf0%d" % a)
-        cast_w1(0, 0, 0, 0, 48, False)
-        cast_w1(0, 0, 0, 48, P, True)
-        cast_w1(0, 1, 0, 0, 64, False)
+        cast_w1(0, 0, 0, 0, P, False)
         quantize_w1(0, 0, 0, PACK)
-        h_passes(0, 0, ((0, 0), (1, 0)), 0)
+        for t in range(PACK):
+            h_passes(0, t, ((0, 0), (1, 0)), 0)
+        gather_table_words(1, 0, S)
+        cast_w1(0, 1, 0, 0, 64, False)
         cast_w1(0, 1, 64, 64, P, True)
         for t in range(PACK):
             quantize_w1(0, 1, t, t + 1)
-        h_passes(0, 0, ((0, 1), (1, 1)), 0)
-        for t in range(1, PACK):
-            make_h(0, t)
+            h_passes(0, t, ((0, 1), (1, 1)), 0)
         for t in range(PACK):
             if t >= 2:
                 w1_bf[(1, t - 2)] = tile([P, PACK, P, PACK], BF16, "w1_bf1%d" % (t - 2))
-                cast_w1(1, t - 2, 0, 0, P if t == 2 else 96, False)
-                if t == 3:
-                    cast_w1(1, 1, 0, 96, P, True)
+                cast_w1(1, t - 2, 0, 0, P, False)
                 quantize_w1(1, t - 2, 0, PACK)
             copy_h(t, t == 0)
             gather_near(t)
-            gather_far(sum0[:, t, :], t, 0, 4)
+            for late in ((), (0, 1), (2,), (3,))[t]:
+                gather_far(sum0[:, late, :], late, 0, 4)
         for t in range(PACK):
             h_passes(1, t, ((0, 0), (1, 0), (0, 1), (1, 1)), 0)
             copy_h(t)
             gather_near(t)
-        relu(0, 0, 2, sum0[:, :, 0 : 2 * P], "w1_w110")
-        quantize_z(0, 0, 2)
-        relu(0, 2, 4, sum0[:, :, 2 * P : 4 * P], "w1_s110")
-        quantize_z(0, 2, 4)
+        relu(0, 0, 4, sum0[:], "w1_w110")
+        quantize_z(0, 0, 4)
         far_block(0, "v_w1")
         relu(1, 0, 1, sum1[0], None)
         quantize_z(1, 0, 1)
@@ -239,6 +235,7 @@ def tile_list_voxel_edge_opacity_kernel(tc, tab_words, tab_scales, offs, pos1, p
         far_block(1, None)
         relu(1, 1, 2, sum1[1], None)
         quantize_z(1, 1, 2)
+        finish(0, 0, 4, banks[0])
         density(1, 0, 4, banks[1])
         far_block(2, None)
         third = sum1[3][:, 2:4, :].rearrange("p t m -> p (t m)").bitcast(BF16).rearrange("p (m t) -> p m t", t=PACK)
@@ -248,7 +245,7 @@ def tile_list_voxel_edge_opacity_kernel(tc, tab_words, tab_scales, offs, pos1, p
         far_block(3, None)
         relu(1, 3, 4, sum1[3], None, True)
         quantize_z(1, 3, 4)
-        for u in range(3):
+        for u in range(1, 3):
             finish(u, 0, 4, banks[u])
         density(3, 0, 2, banks[3])
         density(3, 2, 4, banks[4])

@@ -98,8 +98,8 @@ def tile_list_voxel_edge_opacity_kernel(tc, tab_words, tab_scales, offs, pos1, p
             nc.vector.tensor_copy(out=v_w[a][:, first:last], in_=window.indirect(offs_sb[:, first // 16 : last // 16]))
 
         def cast_w1(g, a, first, m0, m1, on_vector):
-            src = w1_raw[(g, a, first)][:, :, PACK * (m0 - first) : PACK * (m1 - first)].rearrange("p j (m t) -> p m t j", t=PACK)
-            dst = w1_bf[(g, a)][:, :, m0:m1, :].rearrange("p t m j -> p m t j")
+            src = w1_raw[(g, a, first)][:, :, PACK * (m0 - first) : PACK * (m1 - first)].rearrange("p j (m t) -> p m j t", t=PACK)
+            dst = w1_bf[(g, a)][:, :, m0:m1, :].rearrange("p t m j -> p m j t")
             if on_vector:
                 nc.vector.tensor_copy(out=dst, in_=src)
             else:

@@ -19,7 +19,10 @@ ALU = mybir.AluOpType
 P = 128
 BANK = 512
 PACK = 4
+BLOCKS = M // P
 WINDOW = 2 * S
+HALF = P // 2
+SCALAR_SHARE = 20
 
 
 def tile_list_voxel_edge_opacity_kernel(tc, tab_words, tab_scales, offs, pos1, pos2, w1, w2_words, w2_scales, out):
@@ -49,29 +52,29 @@ def tile_list_voxel_edge_opacity_kernel(tc, tab_words, tab_scales, offs, pos1, p
         sum0 = tile([P, PACK, M], F32, "sum0")
         sum1 = {}
         z_bf = {}
-        warm = tile([P, 1], F32, "warm")
+        one = tile([P, 1], F32, "one")
         zero = tile([P, 1], F32, "zero")
         z_w = tile([P, 2, M], U32, "z_w")
         z_s = tile([P, 2, M], U8, "z_s")
         w2_w = tile([P, 2, 2 * N // 4], I32, "w2_w")
         w2_s = tile([P, 2, N // 4], I32, "w2_s")
-        absy = [tile([P, BANK], F32, "absy%d" % u) for u in range(4)]
-        expy = [tile([P, BANK], F32, "expy%d" % u) for u in range(4)]
-        res = [tile([P, 4, P], F32, "res%d" % u) for u in range(4)]
+        absy = [tile([P, BANK], F32, "absy%d" % u) for u in range(BLOCKS)]
+        expy = [tile([P, BANK], F32, "expy%d" % u) for u in range(BLOCKS)]
+        res = [tile([P, N // P, P], F32, "res%d" % u) for u in range(BLOCKS)]
 
         nc.vector.memset(tab_s[32:64, :], 0)
         nc.gpsimd.memset(tab_s[64:P, :], 0)
         nc.vector.memset(v_s[:], 0)
         nc.vector.memset(w2_s[:], 0)
         nc.vector.memset(zero[:], 0.0)
-        nc.scalar.activation(warm[:], zero[:], ACT.Exp, scale=-1.0)
+        nc.scalar.activation(one[:], zero[:], ACT.Exp, scale=-1.0)
 
         def load_table_words(a):
             nc.sync.dma_start(out=tab_w[a][:], in_=tab_words[a].rearrange("p t i -> p (t i)").bitcast(I32))
 
         def load_w1(g, a, m0, m1, stage):
             w1_raw[(g, a, m0)] = stage.rearrange("p (j c) -> p j c", j=PACK)
-            rows = w1[512 * a : 512 * (a + 1), 512 * g + PACK * m0 : 512 * g + PACK * m1]
+            rows = w1[BANK * a : BANK * (a + 1), BANK * g + PACK * m0 : BANK * g + PACK * m1]
             nc.sync.dma_start(out=w1_raw[(g, a, m0)], in_=rows.rearrange("(p j) c -> p j c", j=PACK))
 
         nc.sync.dma_start(offs_sb[:], offs)
@@ -82,8 +85,8 @@ def tile_list_voxel_edge_opacity_kernel(tc, tab_words, tab_scales, offs, pos1, p
         for q in range(4):
             nc.sync.dma_start(out=v_s[32 * q : 32 * q + 4], in_=v_rows[8 * q : 8 * q + 8, :].bitcast(I32))
         load_table_words(1)
-        load_w1(0, 1, 0, 64, h[0][:, S:WINDOW])
-        load_w1(0, 1, 64, P, h[1][:, S:WINDOW])
+        load_w1(0, 1, 0, HALF, h[0][:, S:WINDOW])
+        load_w1(0, 1, HALF, P, h[1][:, S:WINDOW])
         nc.sync.dma_start(pos2_sb[:], pos2)
         load_w1(1, 0, 0, P, h[2][:])
         nc.sync.dma_start(pos1_sb[:], pos1)
@@ -93,17 +96,13 @@ def tile_list_voxel_edge_opacity_kernel(tc, tab_words, tab_scales, offs, pos1, p
             rows = w2_scales[:, 4 * q : 4 * q + 4, :].rearrange("a r n -> r a n")
             nc.sync.dma_start(out=w2_s[32 * q : 32 * q + 4, :, :], in_=rows.bitcast(I32))
 
-        def gather_table_words(a, first, last):
-            window = tab_w[a][:].bitcast(U32)
-            nc.vector.tensor_copy(out=v_w[a][:, first:last], in_=window.indirect(offs_sb[:, first // 16 : last // 16]))
+        def gather_table_words(a):
+            nc.vector.tensor_copy(out=v_w[a][:], in_=tab_w[a][:].bitcast(U32).indirect(offs_sb[:]))
 
-        def cast_w1(g, a, first, m0, m1, on_vector):
-            src = w1_raw[(g, a, first)][:, :, PACK * (m0 - first) : PACK * (m1 - first)].rearrange("p j (m t) -> p m j t", t=PACK)
+        def cast_w1(copy, g, a, loaded_from, m0, m1):
+            raw = w1_raw[(g, a, loaded_from)][:, :, PACK * (m0 - loaded_from) : PACK * (m1 - loaded_from)]
             dst = w1_bf[(g, a)][:, :, m0:m1, :].rearrange("p t m j -> p m j t")
-            if on_vector:
-                nc.vector.tensor_copy(out=dst, in_=src)
-            else:
-                nc.scalar.copy(out=dst, in_=src)
+            copy(out=dst, in_=raw.rearrange("p j (m t) -> p m j t", t=PACK))
 
         def quantize_w1(g, a, t0, t1):
             codes = tile([P, P * (t1 - t0)], U32, "w1_w%d%d%d" % (g, a, t0))
@@ -117,8 +116,8 @@ def tile_list_voxel_edge_opacity_kernel(tc, tab_words, tab_scales, offs, pos1, p
                 in_=w1_bf[(g, a)][:, t0:t1].rearrange("p t m j -> p (t m j)"),
             )
 
-        def h_passes(g, t, order, first):
-            for half, a in order:
+        def h_pass(g, t, a):
+            for half in range(2):
                 cols = slice(BANK * half, BANK * (half + 1))
                 nc.tensor.matmul_mx(
                     out=banks[2 * t + half][:],
@@ -126,31 +125,28 @@ def tile_list_voxel_edge_opacity_kernel(tc, tab_words, tab_scales, offs, pos1, p
                     lhsT_scale=w1_s[(g, a, t)],
                     rhs=v_w[a][:, cols].bitcast(FP8X4),
                     rhs_scale=v_s[:, a, :].bitcast(U8)[:, cols],
-                    start=(a == first),
-                    stop=(a != first),
+                    start=(a == 0),
+                    stop=(a == 1),
                 )
 
-        def make_h(g, t):
-            h_passes(g, t, ((0, 1), (0, 0), (1, 1), (1, 0)), 1)
-
-        def copy_h(t, second_on_vector=False):
+        def copy_h(t, second_copy):
             nc.scalar.copy(out=h[t][:, 0:BANK], in_=banks[2 * t][:])
-            if second_on_vector:
-                nc.vector.tensor_copy(out=h[t][:, BANK:S], in_=banks[2 * t + 1][:])
-            else:
-                nc.scalar.copy(out=h[t][:, BANK:S], in_=banks[2 * t + 1][:])
+            second_copy(out=h[t][:, BANK:S], in_=banks[2 * t + 1][:])
 
         def gather_near(t):
             nc.vector.tensor_scalar(near3[t][:], h[t][:].indirect(pos2_sb[:]), 3.0, 0.0, ALU.mult, ALU.add)
 
         def gather_far(dst, t, u0, u1):
-            window = h[t][:].indirect(pos1_sb[:, 8 * u0 : 8 * u1])
+            window = h[t][:].indirect(pos1_sb[:, P // 16 * u0 : P // 16 * u1])
             nc.vector.tensor_tensor(dst, window, near3[t][:, P * u0 : P * u1], ALU.add)
 
-        def relu(g, u0, u1, src, tag, on_vector=False, into=None):
-            z_bf[(g, u0)] = into if into is not None else tile([P, P * (u1 - u0), PACK], BF16, "z_bf%d%d" % (g, u0), tag=tag)[:]
-            src = src.rearrange("p t (c i) -> p c t i", i=PACK)
-            dst = z_bf[(g, u0)].rearrange("p (c i) t -> p c t i", i=PACK)
+        def far_block(u):
+            for t in range(PACK):
+                gather_far(sum1[u][:, t, :], t, u, u + 1)
+
+        def relu(g, u, sums, on_vector=False):
+            src = sums.rearrange("p t (c i) -> p c t i", i=PACK)
+            dst = z_bf[(g, u)].rearrange("p (c i) t -> p c t i", i=PACK)
             if on_vector:
                 nc.vector.tensor_scalar(dst, src, 0.25, 0.0, ALU.mult, ALU.max)
             else:
@@ -162,96 +158,102 @@ def tile_list_voxel_edge_opacity_kernel(tc, tab_words, tab_scales, offs, pos1, p
                 out=z_w[:, g, cols].bitcast(FP8X4), scales=z_s[:, g, cols], in_=z_bf[(g, u0)].rearrange("p m i -> p (m i)")
             )
 
-        def far_block(u, tag):
-            if tag:
-                sum1[u] = tile([P, PACK, P], F32, "sum1_%d" % u, tag=tag)[:]
-            for t in range(PACK):
-                gather_far(sum1[u][:, t, :], t, u, u + 1)
-
-        def density(u, t0, t1, acc):
+        def density(u, n0, n1, acc):
             cols = slice(P * u, P * (u + 1))
             codes = w2_w[:].bitcast(U8)
             scales = w2_s[:].bitcast(U8)
-            for t in range(t0, t1):
+            for n in range(n0, n1):
                 for g in range(2):
                     nc.tensor.matmul_mx(
-                        out=acc[:, P * (t - t0) : P * (t - t0 + 1)],
-                        lhsT=codes[:, g, 2 * P * t : 2 * P * (t + 1)].bitcast(FP4X4),
-                        lhsT_scale=scales[:, g, P * t : P * (t + 1)],
+                        out=acc[:, P * (n - n0) : P * (n - n0 + 1)],
+                        lhsT=codes[:, g, 2 * P * n : 2 * P * (n + 1)].bitcast(FP4X4),
+                        lhsT_scale=scales[:, g, P * n : P * (n + 1)],
                         rhs=z_w[:, g, cols].bitcast(FP8X4),
                         rhs_scale=z_s[:, g, cols],
                         start=(g == 0),
                         stop=(g == 1),
                     )
 
-        def finish(u, t0, t1, acc):
-            part = slice(P * t0, P * t1)
-            nc.scalar.activation(absy[u][:, part], acc[:, 0 : P * (t1 - t0)], ACT.Abs)
+        def decay(u, n0, n1, acc):
+            part = slice(P * n0, P * n1)
+            nc.scalar.activation(absy[u][:, part], acc[:, 0 : P * (n1 - n0)], ACT.Abs)
             nc.scalar.activation(expy[u][:, part], absy[u][:, part], ACT.Exp, scale=-1.0)
 
-        def store(u, t0, t1):
-            cols = slice(P * u, P * (u + 1))
-            part = slice(P * t0, P * t1)
-            flat = res[u][:].rearrange("n t m -> n (t m)")
-            nc.vector.tensor_scalar(flat[:, part], expy[u][:, part], -1.0, 1.0, ALU.mult, ALU.add)
-            rows = out[P * t0 : P * t1, cols].rearrange("(t n) m -> n t m", n=P)
-            nc.sync.dma_start(out=rows, in_=res[u][:, t0:t1, :])
+        def store(u, n0, n1):
+            part = slice(P * n0, P * n1)
+            flat = res[u][:].rearrange("p n m -> p (n m)")
+            nc.vector.tensor_scalar(flat[:, part], expy[u][:, part], -1.0, one[:], ALU.mult, ALU.add)
+            rows = out[part, P * u : P * (u + 1)].rearrange("(n p) m -> p n m", p=P)
+            nc.sync.dma_start(out=rows, in_=res[u][:, n0:n1, :])
 
-        gather_table_words(0, 0, S)
+        gather_table_words(0)
         for a in range(2):
             w1_bf[(0, a)] = tile([P, PACK, P, PACK], BF16, "w1_bf0%d" % a)
-        cast_w1(0, 0, 0, 0, P, False)
+        cast_w1(nc.scalar.copy, 0, 0, 0, 0, P)
         quantize_w1(0, 0, 0, PACK)
         for t in range(PACK):
-            h_passes(0, t, ((0, 0), (1, 0)), 0)
-        gather_table_words(1, 0, S)
-        cast_w1(0, 1, 0, 0, 64, False)
-        cast_w1(0, 1, 64, 64, P, True)
+            h_pass(0, t, 0)
+        gather_table_words(1)
+        cast_w1(nc.scalar.copy, 0, 1, 0, 0, HALF)
+        cast_w1(nc.scalar.copy, 0, 1, HALF, HALF, HALF + SCALAR_SHARE)
+        cast_w1(nc.vector.tensor_copy, 0, 1, HALF, HALF + SCALAR_SHARE, P)
         for t in range(PACK):
             quantize_w1(0, 1, t, t + 1)
-            h_passes(0, t, ((0, 1), (1, 1)), 0)
+            h_pass(0, t, 1)
         for t in range(PACK):
             if t >= 2:
-                w1_bf[(1, t - 2)] = tile([P, PACK, P, PACK], BF16, "w1_bf1%d" % (t - 2))
-                cast_w1(1, t - 2, 0, 0, P, False)
-                quantize_w1(1, t - 2, 0, PACK)
-            copy_h(t, t == 0)
+                a = t - 2
+                w1_bf[(1, a)] = tile([P, PACK, P, PACK], BF16, "w1_bf1%d" % a)
+                cast_w1(nc.scalar.copy, 1, a, 0, 0, P)
+                quantize_w1(1, a, 0, PACK)
+            copy_h(t, nc.vector.tensor_copy if t == 0 else nc.scalar.copy)
             gather_near(t)
-            for late in ((), (0, 1), (2,), (3,))[t]:
-                gather_far(sum0[:, late, :], late, 0, 4)
+            if t == 1:
+                gather_far(sum0[:, 0, :], 0, 0, BLOCKS)
+            if t >= 1:
+                gather_far(sum0[:, t, :], t, 0, BLOCKS)
+
         for t in range(PACK):
-            h_passes(1, t, ((0, 0), (1, 0), (0, 1), (1, 1)), 0)
-            copy_h(t)
+            h_pass(1, t, 0)
+            h_pass(1, t, 1)
+            copy_h(t, nc.scalar.copy)
             gather_near(t)
-        relu(0, 0, 4, sum0[:], "w1_w110")
-        quantize_z(0, 0, 4)
-        far_block(0, "v_w1")
-        relu(1, 0, 1, sum1[0], None)
+
+        z_bf[(0, 0)] = tile([P, M, PACK], BF16, "z_bf00", tag="w1_w110")[:]
+        relu(0, 0, sum0[:])
+        quantize_z(0, 0, BLOCKS)
+
+        sum1[0] = tile([P, PACK, P], F32, "sum1_0", tag="v_w1")[:]
+        far_block(0)
+        z_bf[(1, 0)] = tile([P, P, PACK], BF16, "z_bf10")[:]
+        relu(1, 0, sum1[0])
         quantize_z(1, 0, 1)
         density(0, 0, 4, banks[0])
-        late_sums = tile([P, 3, PACK, P], F32, "late_sums", tag="sum0")
-        for u in range(1, 4):
+        late_sums = tile([P, BLOCKS - 1, PACK, P], F32, "late_sums", tag="sum0")
+        for u in range(1, BLOCKS):
             sum1[u] = late_sums[:, u - 1]
-        far_block(1, None)
-        relu(1, 1, 2, sum1[1], None)
+        far_block(1)
+        z_bf[(1, 1)] = tile([P, P, PACK], BF16, "z_bf11")[:]
+        relu(1, 1, sum1[1])
         quantize_z(1, 1, 2)
-        finish(0, 0, 4, banks[0])
+        decay(0, 0, 4, banks[0])
         density(1, 0, 4, banks[1])
-        far_block(2, None)
-        third = sum1[3][:, 2:4, :].rearrange("p t m -> p (t m)").bitcast(BF16).rearrange("p (m t) -> p m t", t=PACK)
-        relu(1, 2, 3, sum1[2], None, False, third)
+        far_block(2)
+        last_rows = sum1[3][:, 2:4, :].rearrange("p t m -> p (t m)")
+        z_bf[(1, 2)] = last_rows.bitcast(BF16).rearrange("p (m t) -> p m t", t=PACK)
+        relu(1, 2, sum1[2])
         quantize_z(1, 2, 3)
         density(2, 0, 4, banks[2])
-        far_block(3, None)
-        relu(1, 3, 4, sum1[3], None, True)
+        far_block(3)
+        z_bf[(1, 3)] = tile([P, P, PACK], BF16, "z_bf13")[:]
+        relu(1, 3, sum1[3], on_vector=True)
         quantize_z(1, 3, 4)
-        for u in range(1, 3):
-            finish(u, 0, 4, banks[u])
-        density(3, 0, 2, banks[3])
-        density(3, 2, 4, banks[4])
+        for u in (1, 2):
+            decay(u, 0, 4, banks[u])
+        for half in range(2):
+            density(3, 2 * half, 2 * half + 2, banks[3 + half])
         for u in range(3):
             store(u, 0, 4)
-        finish(3, 0, 2, banks[3])
-        store(3, 0, 2)
-        finish(3, 2, 4, banks[4])
-        store(3, 2, 4)
+        for half in range(2):
+            decay(3, 2 * half, 2 * half + 2, banks[3 + half])
+            store(3, 2 * half, 2 * half + 2)

@@ -49,16 +49,19 @@ def tile_list_voxel_edge_opacity_kernel(tc, tab_words, tab_scales, offs, pos1, p
         w1_s = {}
         h = [tile([P, WINDOW], F32, "h%d" % t) for t in range(PACK)]
         near3 = [tile([P, M], F32, "near3_%d" % t) for t in range(PACK)]
-        sum0 = tile([P, PACK, M], F32, "sum0")
-        sum1 = {}
-        z_bf = {}
+        shared = tile([P, 13, M], F32, "shared")
+        sums = shared[:, 0:13:PACK, :]
+        late_raw = [shared[:, 5:9, :], shared[:, 9:13, :]]
         one = tile([P, 1], F32, "one")
         zero = tile([P, 1], F32, "zero")
+        three = tile([P, 3 * P], F32, "three")
+        z0_bf = tile([P, M, PACK], BF16, "z0_bf")
         z_w = tile([P, 2, M], U32, "z_w")
         z_s = tile([P, 2, M], U8, "z_s")
         w2_w = tile([P, 2, 2 * N // 4], I32, "w2_w")
         w2_s = tile([P, 2, N // 4], I32, "w2_s")
-        absy = [tile([P, BANK], F32, "absy%d" % u) for u in range(BLOCKS)]
+        absy = [tile([P, BANK], F32, "absy%d" % u) for u in range(BLOCKS - 1)]
+        absy.append(absy[2])
         expy = [tile([P, BANK], F32, "expy%d" % u) for u in range(BLOCKS)]
         res = [tile([P, N // P, P], F32, "res%d" % u) for u in range(BLOCKS)]
 
@@ -67,6 +70,8 @@ def tile_list_voxel_edge_opacity_kernel(tc, tab_words, tab_scales, offs, pos1, p
         nc.vector.memset(v_s[:], 0)
         nc.vector.memset(w2_s[:], 0)
         nc.vector.memset(zero[:], 0.0)
+        nc.vector.memset(three[:], 3.0)
+        nc.gpsimd.memset(h[3][:, S:WINDOW], 0.0)
         nc.scalar.activation(one[:], zero[:], ACT.Exp, scale=-1.0)
 
         def load_table_words(a):
@@ -80,17 +85,17 @@ def tile_list_voxel_edge_opacity_kernel(tc, tab_words, tab_scales, offs, pos1, p
         nc.sync.dma_start(offs_sb[:], offs)
         nc.sync.dma_start(out=tab_s[0:32, :], in_=tab_scales.rearrange("a s t -> s a t").bitcast(I32))
         load_table_words(0)
-        load_w1(0, 0, 0, P, tile([P, WINDOW], F32, "first_raw")[:])
+        load_w1(0, 0, 0, P, h[2][:])
         nc.vector.tensor_copy(out=v_rows[:], in_=tab_s[:].bitcast(U8).indirect(offs_sb[:]))
         for q in range(4):
             nc.sync.dma_start(out=v_s[32 * q : 32 * q + 4], in_=v_rows[8 * q : 8 * q + 8, :].bitcast(I32))
         load_table_words(1)
+        nc.sync.dma_start(pos2_sb[:], pos2)
         load_w1(0, 1, 0, HALF, h[0][:, S:WINDOW])
         load_w1(0, 1, HALF, P, h[1][:, S:WINDOW])
-        nc.sync.dma_start(pos2_sb[:], pos2)
-        load_w1(1, 0, 0, P, h[2][:])
+        for a in range(2):
+            load_w1(1, a, 0, P, late_raw[a].rearrange("p j c -> p (j c)"))
         nc.sync.dma_start(pos1_sb[:], pos1)
-        load_w1(1, 1, 0, P, h[3][:])
         nc.sync.dma_start(out=w2_w[:], in_=w2_words.rearrange("a p b -> p a b").bitcast(I32))
         for q in range(4):
             rows = w2_scales[:, 4 * q : 4 * q + 4, :].rearrange("a r n -> r a n")
@@ -99,10 +104,10 @@ def tile_list_voxel_edge_opacity_kernel(tc, tab_words, tab_scales, offs, pos1, p
         def gather_table_words(a):
             nc.vector.tensor_copy(out=v_w[a][:], in_=tab_w[a][:].bitcast(U32).indirect(offs_sb[:]))
 
-        def cast_w1(copy, g, a, loaded_from, m0, m1):
+        def cast_w1(copy, g, a, loaded_from, m0, m1, t0, t1):
             raw = w1_raw[(g, a, loaded_from)][:, :, PACK * (m0 - loaded_from) : PACK * (m1 - loaded_from)]
-            dst = w1_bf[(g, a)][:, :, m0:m1, :].rearrange("p t m j -> p m j t")
-            copy(out=dst, in_=raw.rearrange("p j (m t) -> p m j t", t=PACK))
+            dst = w1_bf[(g, a)][:, t0:t1, m0:m1, :].rearrange("p t m j -> p m j t")
+            copy(out=dst, in_=raw.rearrange("p j (m t) -> p m j t", t=PACK)[:, :, :, t0:t1])
 
         def quantize_w1(g, a, t0, t1):
             codes = tile([P, P * (t1 - t0)], U32, "w1_w%d%d%d" % (g, a, t0))
@@ -129,54 +134,55 @@ def tile_list_voxel_edge_opacity_kernel(tc, tab_words, tab_scales, offs, pos1, p
                     stop=(a == 1),
                 )
 
-        def copy_h(t, second_copy):
+        def copy_h(t, second_copy=nc.scalar.copy):
             nc.scalar.copy(out=h[t][:, 0:BANK], in_=banks[2 * t][:])
             second_copy(out=h[t][:, BANK:S], in_=banks[2 * t + 1][:])
+
+        def entries(pos_sb, u0, u1):
+            return pos_sb[:, P // 16 * u0 : P // 16 * u1]
 
         def gather_near(t):
             nc.vector.tensor_scalar(near3[t][:], h[t][:].indirect(pos2_sb[:]), 3.0, 0.0, ALU.mult, ALU.add)
 
-        def gather_far(dst, t, u0, u1):
-            window = h[t][:].indirect(pos1_sb[:, P // 16 * u0 : P // 16 * u1])
-            nc.vector.tensor_tensor(dst, window, near3[t][:, P * u0 : P * u1], ALU.add)
+        def gather_near_part(dst, t, u0, u1):
+            window = h[t][:].indirect(entries(pos2_sb, u0, u1))
+            nc.vector.tensor_tensor(dst, window, three[:, 0 : P * (u1 - u0)], ALU.mult)
 
-        def far_block(u):
-            for t in range(PACK):
-                gather_far(sum1[u][:, t, :], t, u, u + 1)
+        def gather_far(dst, t, u0, u1, near):
+            nc.vector.tensor_tensor(dst, h[t][:].indirect(entries(pos1_sb, u0, u1)), near, ALU.add)
 
-        def relu(g, u, sums, on_vector=False):
-            src = sums.rearrange("p t (c i) -> p c t i", i=PACK)
-            dst = z_bf[(g, u)].rearrange("p (c i) t -> p c t i", i=PACK)
+        def relu(dst, src, on_vector=False):
+            src = src.rearrange("p t (c i) -> p c t i", i=PACK)
+            dst = dst.rearrange("p (c i) t -> p c t i", i=PACK)
             if on_vector:
                 nc.vector.tensor_scalar(dst, src, 0.25, 0.0, ALU.mult, ALU.max)
             else:
                 nc.scalar.activation(dst, src, ACT.Relu, scale=0.25)
 
-        def quantize_z(g, u0, u1):
+        def quantize_z(g, u0, u1, src):
             cols = slice(P * u0, P * u1)
-            nc.vector.quantize_mx(
-                out=z_w[:, g, cols].bitcast(FP8X4), scales=z_s[:, g, cols], in_=z_bf[(g, u0)].rearrange("p m i -> p (m i)")
-            )
+            nc.vector.quantize_mx(out=z_w[:, g, cols].bitcast(FP8X4), scales=z_s[:, g, cols], in_=src.rearrange("p m i -> p (m i)"))
 
-        def density(u, n0, n1, acc):
+        def density(g, u, n0, n1, acc):
             cols = slice(P * u, P * (u + 1))
             codes = w2_w[:].bitcast(U8)
             scales = w2_s[:].bitcast(U8)
             for n in range(n0, n1):
-                for g in range(2):
-                    nc.tensor.matmul_mx(
-                        out=acc[:, P * (n - n0) : P * (n - n0 + 1)],
-                        lhsT=codes[:, g, 2 * P * n : 2 * P * (n + 1)].bitcast(FP4X4),
-                        lhsT_scale=scales[:, g, P * n : P * (n + 1)],
-                        rhs=z_w[:, g, cols].bitcast(FP8X4),
-                        rhs_scale=z_s[:, g, cols],
-                        start=(g == 0),
-                        stop=(g == 1),
-                    )
+                nc.tensor.matmul_mx(
+                    out=acc[:, P * (n - n0) : P * (n - n0 + 1)],
+                    lhsT=codes[:, g, 2 * P * n : 2 * P * (n + 1)].bitcast(FP4X4),
+                    lhsT_scale=scales[:, g, P * n : P * (n + 1)],
+                    rhs=z_w[:, g, cols].bitcast(FP8X4),
+                    rhs_scale=z_s[:, g, cols],
+                    start=(g == 0 and n == n0),
+                    stop=(g == 1 and n == n1 - 1),
+                )
 
-        def decay(u, n0, n1, acc):
+        def magnitude(u, n0, n1, acc):
+            nc.scalar.activation(absy[u][:, P * n0 : P * n1], acc[:, 0 : P * (n1 - n0)], ACT.Abs)
+
+        def decay(u, n0, n1):
             part = slice(P * n0, P * n1)
-            nc.scalar.activation(absy[u][:, part], acc[:, 0 : P * (n1 - n0)], ACT.Abs)
             nc.scalar.activation(expy[u][:, part], absy[u][:, part], ACT.Exp, scale=-1.0)
 
         def store(u, n0, n1):
@@ -186,74 +192,103 @@ def tile_list_voxel_edge_opacity_kernel(tc, tab_words, tab_scales, offs, pos1, p
             rows = out[part, P * u : P * (u + 1)].rearrange("(n p) m -> p n m", p=P)
             nc.sync.dma_start(out=rows, in_=res[u][:, n0:n1, :])
 
+        for g in range(2):
+            for a in range(2):
+                w1_bf[(g, a)] = tile([P, PACK, P, PACK], BF16, "w1_bf%d%d" % (g, a))
+
         gather_table_words(0)
-        for a in range(2):
-            w1_bf[(0, a)] = tile([P, PACK, P, PACK], BF16, "w1_bf0%d" % a)
-        cast_w1(nc.scalar.copy, 0, 0, 0, 0, P)
+        cast_w1(nc.scalar.copy, 0, 0, 0, 0, P, 0, PACK)
         quantize_w1(0, 0, 0, PACK)
         for t in range(PACK):
             h_pass(0, t, 0)
         gather_table_words(1)
-        cast_w1(nc.scalar.copy, 0, 1, 0, 0, HALF)
-        cast_w1(nc.scalar.copy, 0, 1, HALF, HALF, HALF + SCALAR_SHARE)
-        cast_w1(nc.vector.tensor_copy, 0, 1, HALF, HALF + SCALAR_SHARE, P)
+        cast_w1(nc.scalar.copy, 0, 1, 0, 0, HALF, 0, PACK)
+        cast_w1(nc.scalar.copy, 0, 1, HALF, HALF, HALF + SCALAR_SHARE, 0, PACK)
+        cast_w1(nc.vector.tensor_copy, 0, 1, HALF, HALF + SCALAR_SHARE, P, 0, PACK)
         for t in range(PACK):
             quantize_w1(0, 1, t, t + 1)
             h_pass(0, t, 1)
-        for t in range(PACK):
-            if t >= 2:
-                a = t - 2
-                w1_bf[(1, a)] = tile([P, PACK, P, PACK], BF16, "w1_bf1%d" % a)
-                cast_w1(nc.scalar.copy, 1, a, 0, 0, P)
-                quantize_w1(1, a, 0, PACK)
-            copy_h(t, nc.vector.tensor_copy if t == 0 else nc.scalar.copy)
-            gather_near(t)
-            if t == 1:
-                gather_far(sum0[:, 0, :], 0, 0, BLOCKS)
-            if t >= 1:
-                gather_far(sum0[:, t, :], t, 0, BLOCKS)
 
-        for t in range(PACK):
+        def late_weights(a, t0):
+            cast_w1(nc.scalar.copy, 1, a, 0, 0, P, t0, t0 + 2)
+            quantize_w1(1, a, t0, t0 + 2)
+
+        def late_chunk(t):
             h_pass(1, t, 0)
             h_pass(1, t, 1)
-            copy_h(t, nc.scalar.copy)
-            gather_near(t)
+            copy_h(t)
 
-        z_bf[(0, 0)] = tile([P, M, PACK], BF16, "z_bf00", tag="w1_w110")[:]
-        relu(0, 0, sum0[:])
-        quantize_z(0, 0, BLOCKS)
+        def far_whole(t):
+            gather_far(sums[:, t, :], t, 0, BLOCKS, near3[t][:])
 
-        sum1[0] = tile([P, PACK, P], F32, "sum1_0", tag="v_w1")[:]
+        copy_h(0, nc.vector.tensor_copy)
+        gather_near(0)
+        copy_h(1)
+        gather_near(1)
+        copy_h(2)
+        gather_near(2)
+        late_weights(0, 0)
+        far_whole(0)
+        late_weights(1, 0)
+        far_whole(1)
+        copy_h(3)
+        gather_near(3)
+        late_weights(0, 2)
+        far_whole(2)
+        late_weights(1, 2)
+        far_whole(3)
+        for t in range(PACK):
+            late_chunk(t)
+            gather_near_part(near3[t][:, 0 : 3 * P], t, 0, 3)
+
+        first_place = sums[:, :, 0:P]
+        second_place = sums[:, :, 2 * P : 3 * P]
+        block_sums = [first_place, second_place, first_place, first_place]
+        z1_bf = [tile([P, P, PACK], BF16, "z_bf1%d" % u)[:] for u in range(BLOCKS)]
+        parts = [(0, 0, 4, 0), (1, 0, 4, 1), (2, 0, 4, 2), (3, 0, 2, 3), (3, 2, 4, 4)]
+
+        def far_block(u):
+            for t in range(PACK):
+                near = second_place[:, t, :] if u == 3 else near3[t][:, P * u : P * (u + 1)]
+                gather_far(block_sums[u][:, t, :], t, u, u + 1, near)
+
+        def early_half(half):
+            cols = slice(2 * P * half, 2 * P * (half + 1))
+            relu(z0_bf[:, cols, :], sums[:, :, cols])
+            quantize_z(0, 2 * half, 2 * half + 2, z0_bf[:, cols, :])
+            for u, n0, n1, b in parts:
+                if u // 2 == half:
+                    density(0, u, n0, n1, banks[b])
+
+        def finish_block(u):
+            relu(z1_bf[u], block_sums[u], on_vector=(u == 3))
+            quantize_z(1, u, u + 1, z1_bf[u])
+            for v, n0, n1, b in parts:
+                if v == u:
+                    density(1, u, n0, n1, banks[b])
+
+        early_half(0)
         far_block(0)
-        z_bf[(1, 0)] = tile([P, P, PACK], BF16, "z_bf10")[:]
-        relu(1, 0, sum1[0])
-        quantize_z(1, 0, 1)
-        density(0, 0, 4, banks[0])
-        late_sums = tile([P, BLOCKS - 1, PACK, P], F32, "late_sums", tag="sum0")
-        for u in range(1, BLOCKS):
-            sum1[u] = late_sums[:, u - 1]
+        early_half(1)
         far_block(1)
-        z_bf[(1, 1)] = tile([P, P, PACK], BF16, "z_bf11")[:]
-        relu(1, 1, sum1[1])
-        quantize_z(1, 1, 2)
-        decay(0, 0, 4, banks[0])
-        density(1, 0, 4, banks[1])
+        finish_block(0)
         far_block(2)
-        last_rows = sum1[3][:, 2:4, :].rearrange("p t m -> p (t m)")
-        z_bf[(1, 2)] = last_rows.bitcast(BF16).rearrange("p (m t) -> p m t", t=PACK)
-        relu(1, 2, sum1[2])
-        quantize_z(1, 2, 3)
-        density(2, 0, 4, banks[2])
+        finish_block(1)
+        for t in range(PACK):
+            gather_near_part(second_place[:, t, :], t, 3, 4)
+        magnitude(0, 0, 4, banks[0])
+        finish_block(2)
+        decay(0, 0, 4)
         far_block(3)
-        z_bf[(1, 3)] = tile([P, P, PACK], BF16, "z_bf13")[:]
-        relu(1, 3, sum1[3], on_vector=True)
-        quantize_z(1, 3, 4)
-        for u in (1, 2):
-            decay(u, 0, 4, banks[u])
-        for half in range(2):
-            density(3, 2 * half, 2 * half + 2, banks[3 + half])
+        finish_block(3)
+        magnitude(1, 0, 4, banks[1])
+        decay(1, 0, 4)
+        magnitude(2, 0, 4, banks[2])
+        decay(2, 0, 4)
         for u in range(3):
             store(u, 0, 4)
-        for half in range(2):
-            decay(3, 2 * half, 2 * half + 2, banks[3 + half])
-            store(3, 2 * half, 2 * half + 2)
+        for u, n0, n1, b in parts[3:]:
+            magnitude(u, n0, n1, banks[b])
+        for u, n0, n1, b in parts[3:]:
+            decay(u, n0, n1)
+            store(u, n0, n1)

@@ -22,7 +22,7 @@ PACK = 4
 BLOCKS = M // P
 WINDOW = 2 * S
 HALF = P // 2
-SCALAR_SHARE = 20
+LAST = 96
 
 
 def tile_list_voxel_edge_opacity_kernel(tc, tab_words, tab_scales, offs, pos1, pos2, w1, w2_words, w2_scales, out):
@@ -49,14 +49,15 @@ def tile_list_voxel_edge_opacity_kernel(tc, tab_words, tab_scales, offs, pos1, p
         w1_s = {}
         h = [tile([P, WINDOW], F32, "h%d" % t) for t in range(PACK)]
         near3 = [tile([P, M], F32, "near3_%d" % t) for t in range(PACK)]
+        dealt = tile([P, PACK, M], F32, "dealt")
         shared = tile([P, 13, M], F32, "shared")
         sums = shared[:, 0:13:PACK, :]
-        late_raw = [shared[:, 5:9, :], shared[:, 9:13, :]]
+        late_raw = [shared[:, 5:9, :].rearrange("p j c -> p (j c)"), shared[:, 9:13, :].rearrange("p j c -> p (j c)")]
         one = tile([P, 1], F32, "one")
         zero = tile([P, 1], F32, "zero")
         three = tile([P, 3 * P], F32, "three")
         z0_bf = tile([P, M, PACK], BF16, "z0_bf")
-        z_w = tile([P, 2, M], U32, "z_w")
+        z_w = {}
         z_s = tile([P, 2, M], U8, "z_s")
         w2_w = tile([P, 2, 2 * N // 4], I32, "w2_w")
         w2_s = tile([P, 2, N // 4], I32, "w2_s")
@@ -71,7 +72,6 @@ def tile_list_voxel_edge_opacity_kernel(tc, tab_words, tab_scales, offs, pos1, p
         nc.vector.memset(w2_s[:], 0)
         nc.vector.memset(zero[:], 0.0)
         nc.vector.memset(three[:], 3.0)
-        nc.gpsimd.memset(h[3][:, S:WINDOW], 0.0)
         nc.scalar.activation(one[:], zero[:], ACT.Exp, scale=-1.0)
 
         def load_table_words(a):
@@ -82,20 +82,25 @@ def tile_list_voxel_edge_opacity_kernel(tc, tab_words, tab_scales, offs, pos1, p
             rows = w1[BANK * a : BANK * (a + 1), BANK * g + PACK * m0 : BANK * g + PACK * m1]
             nc.sync.dma_start(out=w1_raw[(g, a, m0)], in_=rows.rearrange("(p j) c -> p j c", j=PACK))
 
+        def move_scales(q):
+            nc.sync.dma_start(out=v_s[32 * q : 32 * q + 4], in_=v_rows[8 * q : 8 * q + 8, :].bitcast(I32))
+
         nc.sync.dma_start(offs_sb[:], offs)
         nc.sync.dma_start(out=tab_s[0:32, :], in_=tab_scales.rearrange("a s t -> s a t").bitcast(I32))
         load_table_words(0)
-        load_w1(0, 0, 0, P, h[2][:])
+        load_w1(0, 0, 0, HALF, h[0][:, S:WINDOW])
         nc.vector.tensor_copy(out=v_rows[:], in_=tab_s[:].bitcast(U8).indirect(offs_sb[:]))
-        for q in range(4):
-            nc.sync.dma_start(out=v_s[32 * q : 32 * q + 4], in_=v_rows[8 * q : 8 * q + 8, :].bitcast(I32))
+        for q in range(3):
+            move_scales(q)
         load_table_words(1)
+        move_scales(3)
+        load_w1(0, 1, 0, HALF, h[1][:, S:WINDOW])
         nc.sync.dma_start(pos2_sb[:], pos2)
-        load_w1(0, 1, 0, HALF, h[0][:, S:WINDOW])
-        load_w1(0, 1, HALF, P, h[1][:, S:WINDOW])
-        for a in range(2):
-            load_w1(1, a, 0, P, late_raw[a].rearrange("p j c -> p (j c)"))
+        load_w1(0, 0, HALF, P, h[2][:, S:WINDOW])
+        load_w1(0, 1, HALF, P, h[3][:, S:WINDOW])
+        load_w1(1, 0, 0, P, late_raw[0])
         nc.sync.dma_start(pos1_sb[:], pos1)
+        load_w1(1, 1, 0, P, late_raw[1])
         nc.sync.dma_start(out=w2_w[:], in_=w2_words.rearrange("a p b -> p a b").bitcast(I32))
         for q in range(4):
             rows = w2_scales[:, 4 * q : 4 * q + 4, :].rearrange("a r n -> r a n")
@@ -106,7 +111,7 @@ def tile_list_voxel_edge_opacity_kernel(tc, tab_words, tab_scales, offs, pos1, p
 
         def cast_w1(copy, g, a, loaded_from, m0, m1, t0, t1):
             raw = w1_raw[(g, a, loaded_from)][:, :, PACK * (m0 - loaded_from) : PACK * (m1 - loaded_from)]
-            dst = w1_bf[(g, a)][:, t0:t1, m0:m1, :].rearrange("p t m j -> p m j t")
+            dst = w1_bf[(g, a, t0)][:, :, m0:m1, :].rearrange("p t m j -> p m j t")
             copy(out=dst, in_=raw.rearrange("p j (m t) -> p m j t", t=PACK)[:, :, :, t0:t1])
 
         def quantize_w1(g, a, t0, t1):
@@ -118,7 +123,7 @@ def tile_list_voxel_edge_opacity_kernel(tc, tab_words, tab_scales, offs, pos1, p
             nc.vector.quantize_mx(
                 out=codes[:].bitcast(FP8X4),
                 scales=scales[:],
-                in_=w1_bf[(g, a)][:, t0:t1].rearrange("p t m j -> p (t m j)"),
+                in_=w1_bf[(g, a, t0)].rearrange("p t m j -> p (t m j)"),
             )
 
         def h_pass(g, t, a):
@@ -161,7 +166,10 @@ def tile_list_voxel_edge_opacity_kernel(tc, tab_words, tab_scales, offs, pos1, p
 
         def quantize_z(g, u0, u1, src):
             cols = slice(P * u0, P * u1)
-            nc.vector.quantize_mx(out=z_w[:, g, cols].bitcast(FP8X4), scales=z_s[:, g, cols], in_=src.rearrange("p m i -> p (m i)"))
+            codes = tile([P, P * (u1 - u0)], U32, "z_w%d%d" % (g, u0))
+            for u in range(u0, u1):
+                z_w[(g, u)] = codes[:, P * (u - u0) : P * (u - u0 + 1)]
+            nc.vector.quantize_mx(out=codes[:].bitcast(FP8X4), scales=z_s[:, g, cols], in_=src.rearrange("p m i -> p (m i)"))
 
         def density(g, u, n0, n1, acc):
             cols = slice(P * u, P * (u + 1))
@@ -172,7 +180,7 @@ def tile_list_voxel_edge_opacity_kernel(tc, tab_words, tab_scales, offs, pos1, p
                     out=acc[:, P * (n - n0) : P * (n - n0 + 1)],
                     lhsT=codes[:, g, 2 * P * n : 2 * P * (n + 1)].bitcast(FP4X4),
                     lhsT_scale=scales[:, g, P * n : P * (n + 1)],
-                    rhs=z_w[:, g, cols].bitcast(FP8X4),
+                    rhs=z_w[(g, u)].bitcast(FP8X4),
                     rhs_scale=z_s[:, g, cols],
                     start=(g == 0 and n == n0),
                     stop=(g == 1 and n == n1 - 1),
@@ -194,20 +202,27 @@ def tile_list_voxel_edge_opacity_kernel(tc, tab_words, tab_scales, offs, pos1, p
 
         for g in range(2):
             for a in range(2):
-                w1_bf[(g, a)] = tile([P, PACK, P, PACK], BF16, "w1_bf%d%d" % (g, a))
+                for t0 in (0, 2):
+                    if (g, a, t0) != (1, 0, 2):
+                        w1_bf[(g, a, t0)] = tile([P, 2, P, PACK], BF16, "w1_bf%d%d%d" % (g, a, t0))[:]
+
+        def early_cast(a, c0):
+            raw = w1_raw[(0, a, 32 * c0)].rearrange("p j (c i) -> p c j i", i=PACK)
+            nc.scalar.copy(out=w1_bf[(0, a, c0)].rearrange("p t (c i) j -> p (t c) j i", i=PACK), in_=raw)
 
         gather_table_words(0)
-        cast_w1(nc.scalar.copy, 0, 0, 0, 0, P, 0, PACK)
-        quantize_w1(0, 0, 0, PACK)
-        for t in range(PACK):
-            h_pass(0, t, 0)
+        early_cast(0, 0)
+        quantize_w1(0, 0, 0, 2)
+        for c in range(2):
+            h_pass(0, c, 0)
         gather_table_words(1)
-        cast_w1(nc.scalar.copy, 0, 1, 0, 0, HALF, 0, PACK)
-        cast_w1(nc.scalar.copy, 0, 1, HALF, HALF, HALF + SCALAR_SHARE, 0, PACK)
-        cast_w1(nc.vector.tensor_copy, 0, 1, HALF, HALF + SCALAR_SHARE, P, 0, PACK)
-        for t in range(PACK):
-            quantize_w1(0, 1, t, t + 1)
-            h_pass(0, t, 1)
+        early_cast(1, 0)
+        w1_bf[(0, 1, 1)] = w1_bf[(0, 1, 0)][:, 1:2]
+        w1_bf[(0, 1, 0)] = w1_bf[(0, 1, 0)][:, 0:1]
+        for c in range(2):
+            quantize_w1(0, 1, c, c + 1)
+            h_pass(0, c, 1)
+        early_cast(0, 2)
 
         def late_weights(a, t0):
             cast_w1(nc.scalar.copy, 1, a, 0, 0, P, t0, t0 + 2)
@@ -220,19 +235,27 @@ def tile_list_voxel_edge_opacity_kernel(tc, tab_words, tab_scales, offs, pos1, p
 
         def far_whole(t):
             gather_far(sums[:, t, :], t, 0, BLOCKS, near3[t][:])
+            nc.sync.dma_start(out=dealt[32 * t : 32 * (t + 1)], in_=sums[:, t, :])
 
         copy_h(0, nc.vector.tensor_copy)
+        quantize_w1(0, 0, 2, 4)
         gather_near(0)
         copy_h(1)
         gather_near(1)
+        early_cast(1, 2)
+        quantize_w1(0, 1, 2, 4)
+        for c in range(2, 4):
+            h_pass(0, c, 0)
+            h_pass(0, c, 1)
+        far_whole(0)
+        far_whole(1)
+        late_weights(0, 0)
         copy_h(2)
         gather_near(2)
-        late_weights(0, 0)
-        far_whole(0)
-        late_weights(1, 0)
-        far_whole(1)
         copy_h(3)
         gather_near(3)
+        late_weights(1, 0)
+        w1_bf[(1, 0, 2)] = tile([P, 2, P, PACK], BF16, "w1_bf102", tag="w1_w012")[:]
         late_weights(0, 2)
         far_whole(2)
         late_weights(1, 2)
@@ -241,11 +264,10 @@ def tile_list_voxel_edge_opacity_kernel(tc, tab_words, tab_scales, offs, pos1, p
             late_chunk(t)
             gather_near_part(near3[t][:, 0 : 3 * P], t, 0, 3)
 
-        first_place = sums[:, :, 0:P]
-        second_place = sums[:, :, 2 * P : 3 * P]
+        first_place = sums[:, 2, :].rearrange("p (t m) -> p t m", t=PACK)
+        second_place = dealt[:, :, 0:P]
         block_sums = [first_place, second_place, first_place, first_place]
-        z1_bf = [tile([P, P, PACK], BF16, "z_bf1%d" % u)[:] for u in range(BLOCKS)]
-        parts = [(0, 0, 4, 0), (1, 0, 4, 1), (2, 0, 4, 2), (3, 0, 2, 3), (3, 2, 4, 4)]
+        parts = [(0, 0, 4, 0), (1, 0, 4, 1), (2, 0, 4, 0), (3, 0, 2, 1), (3, 2, 4, 2)]
 
         def far_block(u):
             for t in range(PACK):
@@ -254,36 +276,42 @@ def tile_list_voxel_edge_opacity_kernel(tc, tab_words, tab_scales, offs, pos1, p
 
         def early_half(half):
             cols = slice(2 * P * half, 2 * P * (half + 1))
-            relu(z0_bf[:, cols, :], sums[:, :, cols])
+            relu(z0_bf[:, cols, :], dealt[:, :, cols])
             quantize_z(0, 2 * half, 2 * half + 2, z0_bf[:, cols, :])
             for u, n0, n1, b in parts:
-                if u // 2 == half:
+                if u // 2 == half and (u < 2 or b == 2):
                     density(0, u, n0, n1, banks[b])
 
         def finish_block(u):
-            relu(z1_bf[u], block_sums[u], on_vector=(u == 3))
-            quantize_z(1, u, u + 1, z1_bf[u])
+            if u < 2:
+                z_bf = dealt[:, u, 2 * P : 4 * P].bitcast(BF16).rearrange("p (m t) -> p m t", t=PACK)
+            else:
+                z_bf = tile([P, P, PACK], BF16, "z_bf1%d" % u, tag="z_w10" if u == 2 else None)[:]
+            relu(z_bf, block_sums[u], on_vector=(u == 3))
+            quantize_z(1, u, u + 1, z_bf)
             for v, n0, n1, b in parts:
                 if v == u:
                     density(1, u, n0, n1, banks[b])
 
-        early_half(0)
         far_block(0)
-        early_half(1)
+        early_half(0)
         far_block(1)
+        early_half(1)
         finish_block(0)
         far_block(2)
         finish_block(1)
+        magnitude(0, 0, 4, banks[0])
+        density(0, 2, 0, 4, banks[0])
         for t in range(PACK):
             gather_near_part(second_place[:, t, :], t, 3, 4)
-        magnitude(0, 0, 4, banks[0])
         finish_block(2)
         decay(0, 0, 4)
+        magnitude(1, 0, 4, banks[1])
+        density(0, 3, 0, 2, banks[1])
         far_block(3)
         finish_block(3)
-        magnitude(1, 0, 4, banks[1])
         decay(1, 0, 4)
-        magnitude(2, 0, 4, banks[2])
+        magnitude(2, 0, 4, banks[0])
         decay(2, 0, 4)
         for u in range(3):
             store(u, 0, 4)

@@ -22,7 +22,7 @@ PACK = 4
 BLOCKS = M // P
 WINDOW = 2 * S
 HALF = P // 2
-LAST = 96
+QUARTER = S // 4
 
 
 def tile_list_voxel_edge_opacity_kernel(tc, tab_words, tab_scales, offs, pos1, pos2, w1, w2_words, w2_scales, out):
@@ -50,9 +50,8 @@ def tile_list_voxel_edge_opacity_kernel(tc, tab_words, tab_scales, offs, pos1, p
         h = [tile([P, WINDOW], F32, "h%d" % t) for t in range(PACK)]
         near3 = [tile([P, M], F32, "near3_%d" % t) for t in range(PACK)]
         dealt = tile([P, PACK, M], F32, "dealt")
-        shared = tile([P, 13, M], F32, "shared")
-        sums = shared[:, 0:13:PACK, :]
-        late_raw = [shared[:, 5:9, :].rearrange("p j c -> p (j c)"), shared[:, 9:13, :].rearrange("p j c -> p (j c)")]
+        late_raw = [tile([P, PACK, M], F32, "late_raw%d" % a) for a in range(2)]
+        sums = [tile([P, M], F32, "sums%d" % c)[:] for c in range(2)] + [late_raw[1][:, j, :] for j in range(2)]
         one = tile([P, 1], F32, "one")
         zero = tile([P, 1], F32, "zero")
         three = tile([P, 3 * P], F32, "three")
@@ -72,6 +71,7 @@ def tile_list_voxel_edge_opacity_kernel(tc, tab_words, tab_scales, offs, pos1, p
         nc.vector.memset(w2_s[:], 0)
         nc.vector.memset(zero[:], 0.0)
         nc.vector.memset(three[:], 3.0)
+        nc.gpsimd.memset(h[0][:, 3 * QUARTER + S : WINDOW], 0.0)
         nc.scalar.activation(one[:], zero[:], ACT.Exp, scale=-1.0)
 
         def load_table_words(a):
@@ -88,19 +88,19 @@ def tile_list_voxel_edge_opacity_kernel(tc, tab_words, tab_scales, offs, pos1, p
         nc.sync.dma_start(offs_sb[:], offs)
         nc.sync.dma_start(out=tab_s[0:32, :], in_=tab_scales.rearrange("a s t -> s a t").bitcast(I32))
         load_table_words(0)
-        load_w1(0, 0, 0, HALF, h[0][:, S:WINDOW])
+        load_w1(0, 0, 0, HALF, h[3][:, S:WINDOW])
+        nc.sync.dma_start(pos2_sb[:], pos2)
+        nc.sync.dma_start(pos1_sb[:], pos1)
         nc.vector.tensor_copy(out=v_rows[:], in_=tab_s[:].bitcast(U8).indirect(offs_sb[:]))
         for q in range(3):
             move_scales(q)
         load_table_words(1)
         move_scales(3)
         load_w1(0, 1, 0, HALF, h[1][:, S:WINDOW])
-        nc.sync.dma_start(pos2_sb[:], pos2)
         load_w1(0, 0, HALF, P, h[2][:, S:WINDOW])
-        load_w1(0, 1, HALF, P, h[3][:, S:WINDOW])
-        load_w1(1, 0, 0, P, late_raw[0])
-        nc.sync.dma_start(pos1_sb[:], pos1)
-        load_w1(1, 1, 0, P, late_raw[1])
+        load_w1(0, 1, HALF, P, h[0][:, 3 * QUARTER : 3 * QUARTER + S])
+        load_w1(1, 0, 0, P, late_raw[0][:].rearrange("p j c -> p (j c)"))
+        load_w1(1, 1, 0, P, late_raw[1][:].rearrange("p j c -> p (j c)"))
         nc.sync.dma_start(out=w2_w[:], in_=w2_words.rearrange("a p b -> p a b").bitcast(I32))
         for q in range(4):
             rows = w2_scales[:, 4 * q : 4 * q + 4, :].rearrange("a r n -> r a n")
@@ -126,22 +126,28 @@ def tile_list_voxel_edge_opacity_kernel(tc, tab_words, tab_scales, offs, pos1, p
                 in_=w1_bf[(g, a, t0)].rearrange("p t m j -> p (t m j)"),
             )
 
-        def h_pass(g, t, a):
-            for half in range(2):
-                cols = slice(BANK * half, BANK * (half + 1))
+        def pieces(g, t):
+            if (g, t) == (0, 0):
+                return [(b, QUARTER * i, QUARTER) for i, b in enumerate((0, 1, 6, 7))]
+            return [(2 * t + half, BANK * half, BANK) for half in range(2)]
+
+        def h_pass(g, t, a, first=0):
+            for b, c0, width in pieces(g, t):
+                cols = slice(c0, c0 + width)
                 nc.tensor.matmul_mx(
-                    out=banks[2 * t + half][:],
+                    out=banks[b][:, 0:width],
                     lhsT=w1_w[(g, a, t)].bitcast(FP8X4),
                     lhsT_scale=w1_s[(g, a, t)],
                     rhs=v_w[a][:, cols].bitcast(FP8X4),
                     rhs_scale=v_s[:, a, :].bitcast(U8)[:, cols],
-                    start=(a == 0),
-                    stop=(a == 1),
+                    start=(a == first),
+                    stop=(a != first),
                 )
 
-        def copy_h(t, second_copy=nc.scalar.copy):
-            nc.scalar.copy(out=h[t][:, 0:BANK], in_=banks[2 * t][:])
-            second_copy(out=h[t][:, BANK:S], in_=banks[2 * t + 1][:])
+        def copy_h(g, t):
+            for i, (b, c0, width) in enumerate(pieces(g, t)):
+                copy = nc.vector.tensor_copy if (g, t, i) == (0, 0, 3) else nc.scalar.copy
+                copy(out=h[t][:, c0 : c0 + width], in_=banks[b][:, 0:width])
 
         def entries(pos_sb, u0, u1):
             return pos_sb[:, P // 16 * u0 : P // 16 * u1]
@@ -200,74 +206,80 @@ def tile_list_voxel_edge_opacity_kernel(tc, tab_words, tab_scales, offs, pos1, p
             rows = out[part, P * u : P * (u + 1)].rearrange("(n p) m -> p n m", p=P)
             nc.sync.dma_start(out=rows, in_=res[u][:, n0:n1, :])
 
-        for g in range(2):
-            for a in range(2):
-                for t0 in (0, 2):
-                    if (g, a, t0) != (1, 0, 2):
-                        w1_bf[(g, a, t0)] = tile([P, 2, P, PACK], BF16, "w1_bf%d%d%d" % (g, a, t0))[:]
-
-        def early_cast(a, c0):
+        def early_cast(copy, dst, a, c0):
             raw = w1_raw[(0, a, 32 * c0)].rearrange("p j (c i) -> p c j i", i=PACK)
-            nc.scalar.copy(out=w1_bf[(0, a, c0)].rearrange("p t (c i) j -> p (t c) j i", i=PACK), in_=raw)
+            copy(out=dst.rearrange("p t (c i) j -> p (t c) j i", i=PACK), in_=raw)
 
         gather_table_words(0)
-        early_cast(0, 0)
-        quantize_w1(0, 0, 0, 2)
-        for c in range(2):
-            h_pass(0, c, 0)
-        gather_table_words(1)
-        early_cast(1, 0)
-        w1_bf[(0, 1, 1)] = w1_bf[(0, 1, 0)][:, 1:2]
-        w1_bf[(0, 1, 0)] = w1_bf[(0, 1, 0)][:, 0:1]
-        for c in range(2):
-            quantize_w1(0, 1, c, c + 1)
-            h_pass(0, c, 1)
-        early_cast(0, 2)
+        for a in range(2):
+            if a == 1:
+                gather_table_words(1)
+            w1_bf[(0, a, 0)] = tile([P, 2, P, PACK], BF16, "w1_bf0%d0" % a)[:]
+            early_cast(nc.scalar.copy, w1_bf[(0, a, 0)], a, 0)
+            quantize_w1(0, a, 0, 2)
+            for c in range(2):
+                h_pass(0, c, a)
+        second_bf = tile([P, 2, 2, P, PACK], BF16, "second_bf")
+        early_cast(nc.scalar.copy, second_bf[:, 0], 0, 2)
+        early_cast(nc.vector.tensor_copy, second_bf[:, 1], 1, 2)
 
-        def late_weights(a, t0):
-            cast_w1(nc.scalar.copy, 1, a, 0, 0, P, t0, t0 + 2)
-            quantize_w1(1, a, t0, t0 + 2)
+        def quantize_second():
+            codes = tile([P, 2, 2, P], U32, "second_w")
+            scales = tile([P, 2, 2, P], U8, "second_s")
+            flat = "p a c m -> p (a c m)"
+            nc.vector.quantize_mx(
+                out=codes[:].rearrange(flat).bitcast(FP8X4),
+                scales=scales[:].rearrange(flat),
+                in_=second_bf[:].rearrange("p a c m j -> p (a c m j)"),
+            )
+            for a in range(2):
+                for c in range(2):
+                    w1_w[(0, a, 2 + c)] = codes[:, a, c, :]
+                    w1_s[(0, a, 2 + c)] = scales[:, a, c, :]
+
+        def late_weights(a, t0, t1):
+            w1_bf[(1, a, t0)] = tile([P, t1 - t0, P, PACK], BF16, "w1_bf1%d%d" % (a, t0))[:]
+            cast_w1(nc.scalar.copy, 1, a, 0, 0, P, t0, t1)
+            quantize_w1(1, a, t0, t1)
 
         def late_chunk(t):
-            h_pass(1, t, 0)
-            h_pass(1, t, 1)
-            copy_h(t)
+            first = t // 2
+            h_pass(1, t, first, first)
+            h_pass(1, t, 1 - first, first)
+            copy_h(1, t)
 
         def far_whole(t):
-            gather_far(sums[:, t, :], t, 0, BLOCKS, near3[t][:])
-            nc.sync.dma_start(out=dealt[32 * t : 32 * (t + 1)], in_=sums[:, t, :])
+            gather_far(sums[t], t, 0, BLOCKS, near3[t][:])
+            for cols in ([slice(0, M)] if t < 3 else [slice(0, M // 2), slice(M // 2, M)]):
+                nc.sync.dma_start(out=dealt[32 * t : 32 * (t + 1), :, cols], in_=sums[t][:, cols])
 
-        copy_h(0, nc.vector.tensor_copy)
-        quantize_w1(0, 0, 2, 4)
+        copy_h(0, 0)
+        quantize_second()
         gather_near(0)
-        copy_h(1)
+        copy_h(0, 1)
         gather_near(1)
-        early_cast(1, 2)
-        quantize_w1(0, 1, 2, 4)
         for c in range(2, 4):
             h_pass(0, c, 0)
             h_pass(0, c, 1)
         far_whole(0)
         far_whole(1)
-        late_weights(0, 0)
-        copy_h(2)
+        late_weights(0, 0, 4)
+        copy_h(0, 2)
         gather_near(2)
-        copy_h(3)
+        late_weights(1, 0, 2)
+        copy_h(0, 3)
         gather_near(3)
-        late_weights(1, 0)
-        w1_bf[(1, 0, 2)] = tile([P, 2, P, PACK], BF16, "w1_bf102", tag="w1_w012")[:]
-        late_weights(0, 2)
+        late_weights(1, 2, 4)
         far_whole(2)
-        late_weights(1, 2)
         far_whole(3)
         for t in range(PACK):
             late_chunk(t)
             gather_near_part(near3[t][:, 0 : 3 * P], t, 0, 3)
 
-        first_place = sums[:, 2, :].rearrange("p (t m) -> p t m", t=PACK)
+        first_place = late_raw[1][:, 0:2, :].rearrange("p j c -> p (j c)")[:, 2 * P : 6 * P].rearrange("p (t m) -> p t m", t=PACK)
         second_place = dealt[:, :, 0:P]
         block_sums = [first_place, second_place, first_place, first_place]
-        parts = [(0, 0, 4, 0), (1, 0, 4, 1), (2, 0, 4, 0), (3, 0, 2, 1), (3, 2, 4, 2)]
+        parts = [(0, 0, 4, 0), (1, 0, 2, 1), (1, 2, 4, 3), (2, 0, 4, 2), (3, 0, 2, 1), (3, 2, 4, 3)]
 
         def far_block(u):
             for t in range(PACK):
@@ -279,14 +291,11 @@ def tile_list_voxel_edge_opacity_kernel(tc, tab_words, tab_scales, offs, pos1, p
             relu(z0_bf[:, cols, :], dealt[:, :, cols])
             quantize_z(0, 2 * half, 2 * half + 2, z0_bf[:, cols, :])
             for u, n0, n1, b in parts:
-                if u // 2 == half and (u < 2 or b == 2):
+                if u // 2 == half and u < 3:
                     density(0, u, n0, n1, banks[b])
 
         def finish_block(u):
-            if u < 2:
-                z_bf = dealt[:, u, 2 * P : 4 * P].bitcast(BF16).rearrange("p (m t) -> p m t", t=PACK)
-            else:
-                z_bf = tile([P, P, PACK], BF16, "z_bf1%d" % u, tag="z_w10" if u == 2 else None)[:]
+            z_bf = tile([P, P, PACK], BF16, "z_bf1%d" % u)[:]
             relu(z_bf, block_sums[u], on_vector=(u == 3))
             quantize_z(1, u, u + 1, z_bf)
             for v, n0, n1, b in parts:
@@ -296,27 +305,27 @@ def tile_list_voxel_edge_opacity_kernel(tc, tab_words, tab_scales, offs, pos1, p
         far_block(0)
         early_half(0)
         far_block(1)
-        early_half(1)
         finish_block(0)
+        early_half(1)
         far_block(2)
         finish_block(1)
-        magnitude(0, 0, 4, banks[0])
-        density(0, 2, 0, 4, banks[0])
         for t in range(PACK):
             gather_near_part(second_place[:, t, :], t, 3, 4)
+        magnitude(0, 0, 4, banks[0])
         finish_block(2)
         decay(0, 0, 4)
-        magnitude(1, 0, 4, banks[1])
-        density(0, 3, 0, 2, banks[1])
+        for half in range(2):
+            magnitude(*parts[1 + half][0:3], banks[parts[1 + half][3]])
+            density(0, *parts[4 + half][0:3], banks[parts[4 + half][3]])
         far_block(3)
         finish_block(3)
         decay(1, 0, 4)
-        magnitude(2, 0, 4, banks[0])
+        magnitude(2, 0, 4, banks[2])
         decay(2, 0, 4)
         for u in range(3):
             store(u, 0, 4)
-        for u, n0, n1, b in parts[3:]:
+        for u, n0, n1, b in parts[4:]:
             magnitude(u, n0, n1, banks[b])
-        for u, n0, n1, b in parts[3:]:
+        for u, n0, n1, b in parts[4:]:
             decay(u, n0, n1)
             store(u, n0, n1)

@@ -20,9 +20,6 @@ P = 128
 BANK = 512
 PACK = 4
 BLOCKS = M // P
-WINDOW = 2 * S
-HALF = P // 2
-QUARTER = S // 4
 
 
 def tile_list_voxel_edge_opacity_kernel(tc, tab_words, tab_scales, offs, pos1, pos2, w1, w2_words, w2_scales, out):
@@ -32,8 +29,8 @@ def tile_list_voxel_edge_opacity_kernel(tc, tab_words, tab_scales, offs, pos1, p
         psum = ctx.enter_context(tc.psum_pool(name="psum", bufs=1))
         banks = [psum.tile([P, BANK], F32, name="bank%d" % b) for b in range(8)]
 
-        def tile(shape, dtype, name, tag=None):
-            return keep.tile(shape, dtype, name=name, tag=tag or name, align_bytes=64)
+        def tile(shape, dtype, name):
+            return keep.tile(shape, dtype, name=name, align_bytes=64)
 
         offs_sb = tile([P, S // 16], U16, "offs_sb")
         pos1_sb = tile([P, M // 16], U16, "pos1_sb")
@@ -43,124 +40,154 @@ def tile_list_voxel_edge_opacity_kernel(tc, tab_words, tab_scales, offs, pos1, p
         v_w = [tile([P, S], U32, "v_w%d" % a) for a in range(2)]
         v_rows = tile([P, S], U8, "v_rows")
         v_s = tile([P, 2, S // 4], I32, "v_s")
-        w1_raw = {}
-        w1_bf = {}
-        w1_w = {}
-        w1_s = {}
-        h = [tile([P, WINDOW], F32, "h%d" % t) for t in range(PACK)]
-        near3 = [tile([P, M], F32, "near3_%d" % t) for t in range(PACK)]
-        dealt = tile([P, PACK, M], F32, "dealt")
-        late_raw = [tile([P, PACK, M], F32, "late_raw%d" % a) for a in range(2)]
-        sums = [tile([P, M], F32, "sums%d" % c)[:] for c in range(2)] + [late_raw[1][:, j, :] for j in range(2)]
+        h = [tile([P, 2 * S if c == 2 else S], F32, "h%d" % c) for c in range(8)]
+        raw_first = [[tile([P, PACK * P], F32, "raw%d%d" % (c, a))[:] for a in range(2 - c)] for c in range(2)]
+        raw_first[1].append(h[0][:, 3 * P : 7 * P])
+        raw_second = [tile([P, S], F32, "raw_second0")[:], h[1][:]]
+        arena = tile([P, 3 * S], F32, "arena")
+        raw_late = [h[2][:].rearrange("p (j c) -> p j c", j=PACK), arena[:, S : 3 * S].rearrange("p (j c) -> p j c", j=PACK)]
+        near_early = [tile([P, M], F32, "near%d" % c) for c in range(4)]
+        sums_early = [tile([P, M], F32, "sums%d" % c)[:] for c in range(3)] + [raw_late[1][:, 0, :]]
+        near_tile = tile([P, P + 3 * M], F32, "near_tile")
+        last_tile = tile([P, 6 * P], F32, "last_tile")
+        near_late = [near_tile[:, P + M * t : P + M * (t + 1)] for t in range(3)] + [last_tile[:, 3 * P : 6 * P]]
+        dealt = [arena[:, 0:S].rearrange("p (t m) -> p t m", t=PACK), tile([P, PACK, 2 * P], F32, "dealt1")[:]]
+        block_sums = [arena[:, P * s : P * (s + PACK)].rearrange("p (t m) -> p t m", t=PACK) for s in (8, 5, 8, 7)]
+        last_near = [near_late[0][:, 3 * P : M], near_late[1][:, 3 * P : M], arena[:, 5 * P : 6 * P], arena[:, 6 * P : 7 * P]]
         one = tile([P, 1], F32, "one")
         zero = tile([P, 1], F32, "zero")
-        three = tile([P, 3 * P], F32, "three")
-        z0_bf = tile([P, M, PACK], BF16, "z0_bf")
+        three = tile([P, M], F32, "three")
+        w1_w = {}
+        w1_s = {}
         z_w = {}
         z_s = tile([P, 2, M], U8, "z_s")
         w2_w = tile([P, 2, 2 * N // 4], I32, "w2_w")
         w2_s = tile([P, 2, N // 4], I32, "w2_s")
         absy = [tile([P, BANK], F32, "absy%d" % u) for u in range(BLOCKS - 1)]
-        absy.append(absy[2])
-        expy = [tile([P, BANK], F32, "expy%d" % u) for u in range(BLOCKS)]
+        absy.append(absy[1])
+        expy = [near_tile[:, 0:BANK]] + [tile([P, BANK], F32, "expy%d" % u)[:] for u in range(1, BLOCKS)]
         res = [tile([P, N // P, P], F32, "res%d" % u) for u in range(BLOCKS)]
 
-        nc.vector.memset(tab_s[32:64, :], 0)
-        nc.gpsimd.memset(tab_s[64:P, :], 0)
-        nc.vector.memset(v_s[:], 0)
-        nc.vector.memset(w2_s[:], 0)
         nc.vector.memset(zero[:], 0.0)
-        nc.vector.memset(three[:], 3.0)
-        nc.gpsimd.memset(h[0][:, 3 * QUARTER + S : WINDOW], 0.0)
+        nc.vector.memset(tab_s[0:96, :], 0)
+        nc.vector.memset(v_s[:], 0)
+        nc.gpsimd.memset(w2_s[:], 0)
+        nc.gpsimd.memset(three[:], 3.0)
         nc.scalar.activation(one[:], zero[:], ACT.Exp, scale=-1.0)
 
         def load_table_words(a):
             nc.sync.dma_start(out=tab_w[a][:], in_=tab_words[a].rearrange("p t i -> p (t i)").bitcast(I32))
 
-        def load_w1(g, a, m0, m1, stage):
-            w1_raw[(g, a, m0)] = stage.rearrange("p (j c) -> p j c", j=PACK)
-            rows = w1[BANK * a : BANK * (a + 1), BANK * g + PACK * m0 : BANK * g + PACK * m1]
-            nc.sync.dma_start(out=w1_raw[(g, a, m0)], in_=rows.rearrange("(p j) c -> p j c", j=PACK))
+        def load_w1(a, c0, c1, stage):
+            rows = w1[BANK * a : BANK * (a + 1), c0:c1]
+            nc.sync.dma_start(out=stage, in_=rows.rearrange("(p j) c -> p j c", j=PACK))
 
-        def move_scales(q):
-            nc.sync.dma_start(out=v_s[32 * q : 32 * q + 4], in_=v_rows[8 * q : 8 * q + 8, :].bitcast(I32))
+        def by_row(stage):
+            return stage.rearrange("p (j c) -> p j c", j=PACK)
 
         nc.sync.dma_start(offs_sb[:], offs)
-        nc.sync.dma_start(out=tab_s[0:32, :], in_=tab_scales.rearrange("a s t -> s a t").bitcast(I32))
-        load_table_words(0)
-        load_w1(0, 0, 0, HALF, h[3][:, S:WINDOW])
+        nc.sync.dma_start(out=tab_s[96:P, :], in_=tab_scales.rearrange("a s t -> s a t").bitcast(I32))
         nc.sync.dma_start(pos2_sb[:], pos2)
         nc.sync.dma_start(pos1_sb[:], pos1)
+        load_table_words(0)
+        for a in range(2):
+            load_w1(a, 0, P, by_row(raw_first[0][a]))
         nc.vector.tensor_copy(out=v_rows[:], in_=tab_s[:].bitcast(U8).indirect(offs_sb[:]))
-        for q in range(3):
-            move_scales(q)
+        for q in range(4):
+            nc.sync.dma_start(out=v_s[32 * q : 32 * q + 4], in_=v_rows[96 + 8 * q : 96 + 8 * q + 8, :].bitcast(I32))
         load_table_words(1)
-        move_scales(3)
-        load_w1(0, 1, 0, HALF, h[1][:, S:WINDOW])
-        load_w1(0, 0, HALF, P, h[2][:, S:WINDOW])
-        load_w1(0, 1, HALF, P, h[0][:, 3 * QUARTER : 3 * QUARTER + S])
-        load_w1(1, 0, 0, P, late_raw[0][:].rearrange("p j c -> p (j c)"))
-        load_w1(1, 1, 0, P, late_raw[1][:].rearrange("p j c -> p (j c)"))
+        for a in range(2):
+            load_w1(a, P, 2 * P, by_row(raw_first[1][a]))
+        for a in range(2):
+            load_w1(a, 2 * P, 4 * P, by_row(raw_second[a]))
+        for a in range(2):
+            load_w1(a, BANK, 2 * BANK, raw_late[a])
         nc.sync.dma_start(out=w2_w[:], in_=w2_words.rearrange("a p b -> p a b").bitcast(I32))
         for q in range(4):
             rows = w2_scales[:, 4 * q : 4 * q + 4, :].rearrange("a r n -> r a n")
             nc.sync.dma_start(out=w2_s[32 * q : 32 * q + 4, :, :], in_=rows.bitcast(I32))
 
-        def gather_table_words(a):
-            nc.vector.tensor_copy(out=v_w[a][:], in_=tab_w[a][:].bitcast(U32).indirect(offs_sb[:]))
+        def gather_table_words(a, j0, j1):
+            window = tab_w[a][:].bitcast(U32).indirect(offs_sb[:, j0 // 16 : j1 // 16])
+            nc.vector.tensor_copy(out=v_w[a][:, j0:j1], in_=window)
 
-        def cast_w1(copy, g, a, loaded_from, m0, m1, t0, t1):
-            raw = w1_raw[(g, a, loaded_from)][:, :, PACK * (m0 - loaded_from) : PACK * (m1 - loaded_from)]
-            dst = w1_bf[(g, a, t0)][:, :, m0:m1, :].rearrange("p t m j -> p m j t")
-            copy(out=dst, in_=raw.rearrange("p j (m t) -> p m j t", t=PACK)[:, :, :, t0:t1])
+        def weights_tile(members):
+            return tile([P, len(members), P, PACK], BF16, "w1_bf%d%d" % members[0])
 
-        def quantize_w1(g, a, t0, t1):
-            codes = tile([P, P * (t1 - t0)], U32, "w1_w%d%d%d" % (g, a, t0))
-            scales = tile([P, P * (t1 - t0)], U8, "w1_s%d%d%d" % (g, a, t0))
-            for t in range(t0, t1):
-                w1_w[(g, a, t)] = codes[:, P * (t - t0) : P * (t - t0 + 1)]
-                w1_s[(g, a, t)] = scales[:, P * (t - t0) : P * (t - t0 + 1)]
-            nc.vector.quantize_mx(
-                out=codes[:].bitcast(FP8X4),
-                scales=scales[:],
-                in_=w1_bf[(g, a, t0)].rearrange("p t m j -> p (t m j)"),
+        def quantize_w1(members, src):
+            codes = tile([P, P * len(members)], U32, "w1_w%d%d" % members[0])
+            scales = tile([P, P * len(members)], U8, "w1_s%d%d" % members[0])
+            for i, member in enumerate(members):
+                w1_w[member] = codes[:, P * i : P * (i + 1)]
+                w1_s[member] = scales[:, P * i : P * (i + 1)]
+            nc.vector.quantize_mx(out=codes[:].bitcast(FP8X4), scales=scales[:], in_=src[:].rearrange("p t m j -> p (t m j)"))
+
+        def cast_neighbours(dst, rows, copy=nc.scalar.copy):
+            raw = rows.rearrange("p j (c i) -> p c j i", i=PACK)
+            copy(out=dst.rearrange("p t (c i) j -> p (t c) j i", i=PACK), in_=raw)
+
+        def cast_dealing(dst, a, t0, t1):
+            raw = raw_late[a].rearrange("p j (m t) -> p m j t", t=PACK)[:, :, :, t0:t1]
+            nc.scalar.copy(out=dst.rearrange("p t m j -> p m j t"), in_=raw)
+
+        def pieces(c):
+            if c == 0:
+                return [(0, 0, 512), (1, 512, 768), (2, 768, 1024)]
+            return [((2 * c + 1 + half) % 8, BANK * half, BANK * (half + 1)) for half in range(2)]
+
+        def h_pass(c, a, piece, first=0):
+            b, j0, j1 = piece
+            nc.tensor.matmul_mx(
+                out=banks[b][:, 0 : j1 - j0],
+                lhsT=w1_w[(c, a)].bitcast(FP8X4),
+                lhsT_scale=w1_s[(c, a)],
+                rhs=v_w[a][:, j0:j1].bitcast(FP8X4),
+                rhs_scale=v_s[:, a, :].bitcast(U8)[:, j0:j1],
+                start=(a == first),
+                stop=(a != first),
             )
 
-        def pieces(g, t):
-            if (g, t) == (0, 0):
-                return [(b, QUARTER * i, QUARTER) for i, b in enumerate((0, 1, 6, 7))]
-            return [(2 * t + half, BANK * half, BANK) for half in range(2)]
+        def h_passes(c, first=0):
+            for piece in pieces(c):
+                for a in (first, 1 - first):
+                    h_pass(c, a, piece, first)
 
-        def h_pass(g, t, a, first=0):
-            for b, c0, width in pieces(g, t):
-                cols = slice(c0, c0 + width)
-                nc.tensor.matmul_mx(
-                    out=banks[b][:, 0:width],
-                    lhsT=w1_w[(g, a, t)].bitcast(FP8X4),
-                    lhsT_scale=w1_s[(g, a, t)],
-                    rhs=v_w[a][:, cols].bitcast(FP8X4),
-                    rhs_scale=v_s[:, a, :].bitcast(U8)[:, cols],
-                    start=(a == first),
-                    stop=(a != first),
-                )
+        def copy_piece(copy, c, piece):
+            b, j0, j1 = piece
+            copy(out=h[c][:, j0:j1], in_=banks[b][:, 0 : j1 - j0])
 
-        def copy_h(g, t):
-            for i, (b, c0, width) in enumerate(pieces(g, t)):
-                copy = nc.vector.tensor_copy if (g, t, i) == (0, 0, 3) else nc.scalar.copy
-                copy(out=h[t][:, c0 : c0 + width], in_=banks[b][:, 0:width])
+        def copy_h(c):
+            for piece in pieces(c):
+                copy_piece(nc.scalar.copy, c, piece)
 
         def entries(pos_sb, u0, u1):
             return pos_sb[:, P // 16 * u0 : P // 16 * u1]
 
-        def gather_near(t):
-            nc.vector.tensor_scalar(near3[t][:], h[t][:].indirect(pos2_sb[:]), 3.0, 0.0, ALU.mult, ALU.add)
+        def gather_near(dst, c, u0, u1):
+            nc.vector.tensor_tensor(dst, h[c][:].indirect(entries(pos2_sb, u0, u1)), three[:, 0 : P * (u1 - u0)], ALU.mult)
 
-        def gather_near_part(dst, t, u0, u1):
-            window = h[t][:].indirect(entries(pos2_sb, u0, u1))
-            nc.vector.tensor_tensor(dst, window, three[:, 0 : P * (u1 - u0)], ALU.mult)
+        def gather_far(dst, c, u0, u1, near):
+            nc.vector.tensor_tensor(dst, h[c][:].indirect(entries(pos1_sb, u0, u1)), near, ALU.add)
 
-        def gather_far(dst, t, u0, u1, near):
-            nc.vector.tensor_tensor(dst, h[t][:].indirect(entries(pos1_sb, u0, u1)), near, ALU.add)
+        halves = [slice(2 * P * half, 2 * P * (half + 1)) for half in range(2)]
+
+        def deal(c, half):
+            nc.sync.dma_start(out=dealt[half][32 * c : 32 * (c + 1)], in_=sums_early[c][:, halves[half]])
+
+        def early_gathers(c):
+            for half in range(2):
+                gather_near(near_early[c][:, halves[half]], c, 2 * half, 2 * half + 2)
+            for half in range(2):
+                gather_far(sums_early[c][:, halves[half]], c, 2 * half, 2 * half + 2, near_early[c][:, halves[half]])
+                deal(c, half)
+
+        def near_whole(c):
+            gather_near(near_early[c][:], c, 0, BLOCKS)
+
+        def far_whole(c):
+            gather_far(sums_early[c], c, 0, BLOCKS, near_early[c][:])
+            for half in range(2):
+                deal(c, half)
 
         def relu(dst, src, on_vector=False):
             src = src.rearrange("p t (c i) -> p c t i", i=PACK)
@@ -177,23 +204,27 @@ def tile_list_voxel_edge_opacity_kernel(tc, tab_words, tab_scales, offs, pos1, p
                 z_w[(g, u)] = codes[:, P * (u - u0) : P * (u - u0 + 1)]
             nc.vector.quantize_mx(out=codes[:].bitcast(FP8X4), scales=z_s[:, g, cols], in_=src.rearrange("p m i -> p (m i)"))
 
-        def density(g, u, n0, n1, acc):
+        parts = {0: [(0, 4, 1)], 1: [(0, 2, 2), (2, 4, 3)], 2: [(0, 4, 4)], 3: [(0, 2, 2), (2, 4, 3)]}
+
+        def density(g, u, which=None):
             cols = slice(P * u, P * (u + 1))
             codes = w2_w[:].bitcast(U8)
             scales = w2_s[:].bitcast(U8)
-            for n in range(n0, n1):
-                nc.tensor.matmul_mx(
-                    out=acc[:, P * (n - n0) : P * (n - n0 + 1)],
-                    lhsT=codes[:, g, 2 * P * n : 2 * P * (n + 1)].bitcast(FP4X4),
-                    lhsT_scale=scales[:, g, P * n : P * (n + 1)],
-                    rhs=z_w[(g, u)].bitcast(FP8X4),
-                    rhs_scale=z_s[:, g, cols],
-                    start=(g == 0 and n == n0),
-                    stop=(g == 1 and n == n1 - 1),
-                )
+            for n0, n1, b in parts[u] if which is None else [parts[u][which]]:
+                for n in range(n0, n1):
+                    nc.tensor.matmul_mx(
+                        out=banks[b][:, P * (n - n0) : P * (n - n0 + 1)],
+                        lhsT=codes[:, g, 2 * P * n : 2 * P * (n + 1)].bitcast(FP4X4),
+                        lhsT_scale=scales[:, g, P * n : P * (n + 1)],
+                        rhs=z_w[(g, u)].bitcast(FP8X4),
+                        rhs_scale=z_s[:, g, cols],
+                        start=(g == 0 and n == n0),
+                        stop=(g == 1 and n == n1 - 1),
+                    )
 
-        def magnitude(u, n0, n1, acc):
-            nc.scalar.activation(absy[u][:, P * n0 : P * n1], acc[:, 0 : P * (n1 - n0)], ACT.Abs)
+        def magnitude(u, which=None):
+            for n0, n1, b in parts[u] if which is None else [parts[u][which]]:
+                nc.scalar.activation(absy[u][:, P * n0 : P * n1], banks[b][:, 0 : P * (n1 - n0)], ACT.Abs)
 
         def decay(u, n0, n1):
             part = slice(P * n0, P * n1)
@@ -206,126 +237,111 @@ def tile_list_voxel_edge_opacity_kernel(tc, tab_words, tab_scales, offs, pos1, p
             rows = out[part, P * u : P * (u + 1)].rearrange("(n p) m -> p n m", p=P)
             nc.sync.dma_start(out=rows, in_=res[u][:, n0:n1, :])
 
-        def early_cast(copy, dst, a, c0):
-            raw = w1_raw[(0, a, 32 * c0)].rearrange("p j (c i) -> p c j i", i=PACK)
-            copy(out=dst.rearrange("p t (c i) j -> p (t c) j i", i=PACK), in_=raw)
-
-        gather_table_words(0)
-        for a in range(2):
-            if a == 1:
-                gather_table_words(1)
-            w1_bf[(0, a, 0)] = tile([P, 2, P, PACK], BF16, "w1_bf0%d0" % a)[:]
-            early_cast(nc.scalar.copy, w1_bf[(0, a, 0)], a, 0)
-            quantize_w1(0, a, 0, 2)
-            for c in range(2):
-                h_pass(0, c, a)
-        second_bf = tile([P, 2, 2, P, PACK], BF16, "second_bf")
-        early_cast(nc.scalar.copy, second_bf[:, 0], 0, 2)
-        early_cast(nc.vector.tensor_copy, second_bf[:, 1], 1, 2)
-
-        def quantize_second():
-            codes = tile([P, 2, 2, P], U32, "second_w")
-            scales = tile([P, 2, 2, P], U8, "second_s")
-            flat = "p a c m -> p (a c m)"
-            nc.vector.quantize_mx(
-                out=codes[:].rearrange(flat).bitcast(FP8X4),
-                scales=scales[:].rearrange(flat),
-                in_=second_bf[:].rearrange("p a c m j -> p (a c m j)"),
-            )
+        def first_weights(c):
+            bf = weights_tile([(c, 0), (c, 1)])
             for a in range(2):
-                for c in range(2):
-                    w1_w[(0, a, 2 + c)] = codes[:, a, c, :]
-                    w1_s[(0, a, 2 + c)] = scales[:, a, c, :]
+                cast_neighbours(bf[:, a : a + 1], by_row(raw_first[c][a]))
+            return bf
 
-        def late_weights(a, t0, t1):
-            w1_bf[(1, a, t0)] = tile([P, t1 - t0, P, PACK], BF16, "w1_bf1%d%d" % (a, t0))[:]
-            cast_w1(nc.scalar.copy, 1, a, 0, 0, P, t0, t1)
-            quantize_w1(1, a, t0, t1)
-
-        def late_chunk(t):
-            first = t // 2
-            h_pass(1, t, first, first)
-            h_pass(1, t, 1 - first, first)
-            copy_h(1, t)
-
-        def far_whole(t):
-            gather_far(sums[t], t, 0, BLOCKS, near3[t][:])
-            for cols in ([slice(0, M)] if t < 3 else [slice(0, M // 2), slice(M // 2, M)]):
-                nc.sync.dma_start(out=dealt[32 * t : 32 * (t + 1), :, cols], in_=sums[t][:, cols])
-
-        copy_h(0, 0)
-        quantize_second()
-        gather_near(0)
-        copy_h(0, 1)
-        gather_near(1)
-        for c in range(2, 4):
-            h_pass(0, c, 0)
-            h_pass(0, c, 1)
+        gather_table_words(0, 0, S)
+        quantize_w1([(0, 0), (0, 1)], first_weights(0))
+        for piece in pieces(0):
+            h_pass(0, 0, piece)
+        for piece in pieces(0):
+            gather_table_words(1, piece[1], piece[2])
+            h_pass(0, 1, piece)
+        bf1 = first_weights(1)
+        quantize_w1([(1, 0), (1, 1)], bf1)
+        h_passes(1)
+        second = [[(2, a), (3, a)] for a in range(2)]
+        bf_second = [weights_tile(second[a]) for a in range(2)]
+        copy_piece(nc.scalar.copy, 0, pieces(0)[0])
+        for i in range(2):
+            copy_piece(nc.vector.tensor_copy, 0, pieces(0)[1 + i])
+        for i, copy in enumerate((nc.scalar.copy, nc.vector.tensor_copy)):
+            cast_neighbours(bf_second[0][:, i : i + 1], by_row(raw_second[0])[:, :, P * i : P * (i + 1)], copy)
+        cast_neighbours(bf_second[1][:], by_row(raw_second[1]))
+        near_whole(0)
+        quantize_w1(second[0], bf_second[0])
         far_whole(0)
-        far_whole(1)
-        late_weights(0, 0, 4)
-        copy_h(0, 2)
-        gather_near(2)
-        late_weights(1, 0, 2)
-        copy_h(0, 3)
-        gather_near(3)
-        late_weights(1, 2, 4)
-        far_whole(2)
+        quantize_w1(second[1], bf_second[1])
+        h_passes(2)
+        h_passes(3)
+        copy_h(1)
+        early_gathers(1)
+
+        late_a = [(4, 0), (5, 0), (6, 0), (7, 0)]
+        late_b = [(4, 1), (5, 1)]
+        late_c = [(6, 1), (7, 1)]
+        bf_a, bf_b, bf_c = weights_tile(late_a), weights_tile(late_b), weights_tile(late_c)
+        cast_dealing(bf_a[:], 0, 0, 4)
+        quantize_w1(late_a, bf_a)
+        copy_h(2)
+        early_gathers(2)
+        cast_dealing(bf_b[:], 1, 0, 2)
+        quantize_w1(late_b, bf_b)
+        h_passes(4)
+        h_passes(5)
+        copy_h(3)
+        near_whole(3)
+        cast_dealing(bf_c[:], 1, 2, 4)
+        quantize_w1(late_c, bf_c)
+        h_passes(6)
+        h_passes(7)
         far_whole(3)
         for t in range(PACK):
-            late_chunk(t)
-            gather_near_part(near3[t][:, 0 : 3 * P], t, 0, 3)
+            copy_h(4 + t)
+            blocks = BLOCKS if t < 2 else BLOCKS - 1
+            gather_near(near_late[t][:, 0 : P * blocks], 4 + t, 0, blocks)
 
-        first_place = late_raw[1][:, 0:2, :].rearrange("p j c -> p (j c)")[:, 2 * P : 6 * P].rearrange("p (t m) -> p t m", t=PACK)
-        second_place = dealt[:, :, 0:P]
-        block_sums = [first_place, second_place, first_place, first_place]
-        parts = [(0, 0, 4, 0), (1, 0, 2, 1), (1, 2, 4, 3), (2, 0, 4, 2), (3, 0, 2, 1), (3, 2, 4, 3)]
+        z0_bf = [
+            tile([P, 2 * P, PACK], BF16, "z0_bf")[:],
+            last_tile[:, 0:M].bitcast(BF16).rearrange("p (m i) -> p m i", i=PACK),
+        ]
+        z1_bf = [tile([P, P, PACK], BF16, "z1_bf%d" % u)[:] for u in range(BLOCKS)]
 
-        def far_block(u):
-            for t in range(PACK):
-                near = second_place[:, t, :] if u == 3 else near3[t][:, P * u : P * (u + 1)]
-                gather_far(block_sums[u][:, t, :], t, u, u + 1, near)
+        def far_block(u, chunks):
+            for t in chunks:
+                near = last_near[t] if u == 3 else near_late[t][:, P * u : P * (u + 1)]
+                gather_far(block_sums[u][:, t, :], 4 + t, u, u + 1, near)
 
         def early_half(half):
-            cols = slice(2 * P * half, 2 * P * (half + 1))
-            relu(z0_bf[:, cols, :], dealt[:, :, cols])
-            quantize_z(0, 2 * half, 2 * half + 2, z0_bf[:, cols, :])
-            for u, n0, n1, b in parts:
-                if u // 2 == half and u < 3:
-                    density(0, u, n0, n1, banks[b])
+            relu(z0_bf[half], dealt[half])
+            quantize_z(0, 2 * half, 2 * half + 2, z0_bf[half])
+            for u in range(2 * half, min(2 * half + 2, 3)):
+                density(0, u)
 
         def finish_block(u):
-            z_bf = tile([P, P, PACK], BF16, "z_bf1%d" % u)[:]
-            relu(z_bf, block_sums[u], on_vector=(u == 3))
-            quantize_z(1, u, u + 1, z_bf)
-            for v, n0, n1, b in parts:
-                if v == u:
-                    density(1, u, n0, n1, banks[b])
+            relu(z1_bf[u], block_sums[u], on_vector=(u == 3))
+            quantize_z(1, u, u + 1, z1_bf[u])
+            density(1, u)
 
-        far_block(0)
+        far_block(0, range(PACK))
         early_half(0)
-        far_block(1)
+        far_block(1, (0, 1, 2))
         finish_block(0)
+        far_block(1, (3,))
+        far_block(2, (1, 2, 3))
         early_half(1)
-        far_block(2)
         finish_block(1)
-        for t in range(PACK):
-            gather_near_part(second_place[:, t, :], t, 3, 4)
-        magnitude(0, 0, 4, banks[0])
+        far_block(2, (0,))
+        for t in (2, 3):
+            gather_near(last_near[t], 4 + t, 3, 4)
+        far_block(3, (0,))
+        magnitude(0)
         finish_block(2)
-        decay(0, 0, 4)
         for half in range(2):
-            magnitude(*parts[1 + half][0:3], banks[parts[1 + half][3]])
-            density(0, *parts[4 + half][0:3], banks[parts[4 + half][3]])
-        far_block(3)
+            magnitude(1, half)
+            density(0, 3, half)
+        decay(0, 0, 4)
+        far_block(3, (1, 2, 3))
         finish_block(3)
+        magnitude(2)
         decay(1, 0, 4)
-        magnitude(2, 0, 4, banks[2])
         decay(2, 0, 4)
         for u in range(3):
             store(u, 0, 4)
-        for u, n0, n1, b in parts[4:]:
-            magnitude(u, n0, n1, banks[b])
-        for u, n0, n1, b in parts[4:]:
-            decay(u, n0, n1)
-            store(u, n0, n1)
+        magnitude(3)
+        for n0, n1, b in parts[3]:
+            decay(3, n0, n1)
+            store(3, n0, n1)

@@ -40,13 +40,16 @@ def tile_list_voxel_edge_opacity_kernel(tc, tab_words, tab_scales, offs, pos1, p
         v_w = [tile([P, S], U32, "v_w%d" % a) for a in range(2)]
         v_rows = tile([P, S], U8, "v_rows")
         v_s = tile([P, 2, S // 4], I32, "v_s")
-        h = [tile([P, 2 * S if c == 2 else S], F32, "h%d" % c) for c in range(8)]
-        raw_first = [[tile([P, PACK * P], F32, "raw%d%d" % (c, a))[:] for a in range(2 - c)] for c in range(2)]
-        raw_first[1].append(h[0][:, 3 * P : 7 * P])
-        raw_second = [tile([P, S], F32, "raw_second0")[:], h[1][:]]
+        h = [tile([P, 2 * S], F32, "h%d" % c) for c in range(4)]
+        h = h + h[0:2] + [tile([P, S], F32, "h%d" % c) for c in range(6, 8)]
+        raw_first = [
+            [h[1][:, S : S + M], h[1][:, S + M : 2 * S]],
+            [tile([P, PACK * P], F32, "raw10")[:], h[0][:, 3 * P : 7 * P]],
+        ]
+        raw_second = [h[0][:, S : 2 * S], h[1][:, 0:S]]
         arena = tile([P, 3 * S], F32, "arena")
         raw_late = [h[2][:].rearrange("p (j c) -> p j c", j=PACK), arena[:, S : 3 * S].rearrange("p (j c) -> p j c", j=PACK)]
-        near_early = [tile([P, M], F32, "near%d" % c) for c in range(4)]
+        near_early = [h[3][:, S : S + M], h[3][:, S + M : 2 * S]] + [tile([P, M], F32, "near%d" % c)[:] for c in range(2, 4)]
         sums_early = [tile([P, M], F32, "sums%d" % c)[:] for c in range(3)] + [raw_late[1][:, 0, :]]
         near_tile = tile([P, P + 3 * M], F32, "near_tile")
         last_tile = tile([P, 6 * P], F32, "last_tile")
@@ -56,7 +59,7 @@ def tile_list_voxel_edge_opacity_kernel(tc, tab_words, tab_scales, offs, pos1, p
         last_near = [near_late[0][:, 3 * P : M], near_late[1][:, 3 * P : M], arena[:, 5 * P : 6 * P], arena[:, 6 * P : 7 * P]]
         one = tile([P, 1], F32, "one")
         zero = tile([P, 1], F32, "zero")
-        three = tile([P, M], F32, "three")
+        three = tile([P, 3 * P], F32, "three")
         w1_w = {}
         w1_s = {}
         z_w = {}
@@ -164,7 +167,10 @@ def tile_list_voxel_edge_opacity_kernel(tc, tab_words, tab_scales, offs, pos1, p
             return pos_sb[:, P // 16 * u0 : P // 16 * u1]
 
         def gather_near(dst, c, u0, u1):
-            nc.vector.tensor_tensor(dst, h[c][:].indirect(entries(pos2_sb, u0, u1)), three[:, 0 : P * (u1 - u0)], ALU.mult)
+            if u1 - u0 == BLOCKS:
+                nc.vector.tensor_scalar(dst, h[c][:].indirect(pos2_sb[:]), 3.0, 0.0, ALU.mult, ALU.add)
+            else:
+                nc.vector.tensor_tensor(dst, h[c][:].indirect(entries(pos2_sb, u0, u1)), three[:, 0 : P * (u1 - u0)], ALU.mult)
 
         def gather_far(dst, c, u0, u1, near):
             nc.vector.tensor_tensor(dst, h[c][:].indirect(entries(pos1_sb, u0, u1)), near, ALU.add)
@@ -182,10 +188,10 @@ def tile_list_voxel_edge_opacity_kernel(tc, tab_words, tab_scales, offs, pos1, p
                 deal(c, half)
 
         def near_whole(c):
-            gather_near(near_early[c][:], c, 0, BLOCKS)
+            gather_near(near_early[c], c, 0, BLOCKS)
 
         def far_whole(c):
-            gather_far(sums_early[c], c, 0, BLOCKS, near_early[c][:])
+            gather_far(sums_early[c], c, 0, BLOCKS, near_early[c])
             for half in range(2):
                 deal(c, half)
 

@@ -96,9 +96,9 @@ def tile_list_voxel_edge_opacity_kernel(tc, tab_words, tab_scales, offs, pos1, p
         for a in range(2):
             load_w1(a, 0, P, by_row(raw_first[0][a]))
         nc.vector.tensor_copy(out=v_rows[:], in_=tab_s[:].bitcast(U8).indirect(offs_sb[:]))
+        load_table_words(1)
         for q in range(4):
             nc.sync.dma_start(out=v_s[32 * q : 32 * q + 4], in_=v_rows[96 + 8 * q : 96 + 8 * q + 8, :].bitcast(I32))
-        load_table_words(1)
         for a in range(2):
             load_w1(a, P, 2 * P, by_row(raw_first[1][a]))
         for a in range(2):
@@ -239,7 +239,7 @@ def tile_list_voxel_edge_opacity_kernel(tc, tab_words, tab_scales, offs, pos1, p
         def store(u, n0, n1):
             part = slice(P * n0, P * n1)
             flat = res[u][:].rearrange("p n m -> p (n m)")
-            nc.vector.tensor_scalar(flat[:, part], expy[u][:, part], -1.0, one[:], ALU.mult, ALU.add)
+            nc.vector.tensor_scalar(flat[:, part], expy[u][:, part], -1.0, one[:] if u == 2 else 1.0, ALU.mult, ALU.add)
             rows = out[part, P * u : P * (u + 1)].rearrange("(n p) m -> p n m", p=P)
             nc.sync.dma_start(out=rows, in_=res[u][:, n0:n1, :])
 
@@ -348,6 +348,6 @@ def tile_list_voxel_edge_opacity_kernel(tc, tab_words, tab_scales, offs, pos1, p
         for u in range(3):
             store(u, 0, 4)
         magnitude(3)
-        for n0, n1, b in parts[3]:
+        for n0, n1 in ((0, 2), (2, 3), (3, 4)):
             decay(3, n0, n1)
             store(3, n0, n1)

@@ -19,7 +19,10 @@ ALU = mybir.AluOpType
 P = 128
 BANK = 512
 PACK = 4
-BLOCKS = M // P
+BATCHES = M // P
+SCALE_ROWS_FROM = 96
+WIDE = 2 * S
+FIRST_PART = 96
 
 
 def tile_list_voxel_edge_opacity_kernel(tc, tab_words, tab_scales, offs, pos1, pos2, w1, w2_words, w2_scales, out):
@@ -32,6 +35,9 @@ def tile_list_voxel_edge_opacity_kernel(tc, tab_words, tab_scales, offs, pos1, p
         def tile(shape, dtype, name):
             return keep.tile(shape, dtype, name=name, align_bytes=64)
 
+        def by_row(flat):
+            return flat.rearrange("p (j c) -> p j c", j=PACK)
+
         offs_sb = tile([P, S // 16], U16, "offs_sb")
         pos1_sb = tile([P, M // 16], U16, "pos1_sb")
         pos2_sb = tile([P, M // 16], U16, "pos2_sb")
@@ -40,23 +46,34 @@ def tile_list_voxel_edge_opacity_kernel(tc, tab_words, tab_scales, offs, pos1, p
         v_w = [tile([P, S], U32, "v_w%d" % a) for a in range(2)]
         v_rows = tile([P, S], U8, "v_rows")
         v_s = tile([P, 2, S // 4], I32, "v_s")
-        h = [tile([P, 2 * S], F32, "h%d" % c) for c in range(4)]
-        h = h + h[0:2] + [tile([P, S], F32, "h%d" % c) for c in range(6, 8)]
+
+        h = [tile([P, P + WIDE if c == 2 else WIDE], F32, "h%d" % c) for c in range(PACK)]
+        h = h + h[0:2] + [tile([P, S], F32, "h%d" % c) for c in (6, 7)]
+
         raw_first = [
-            [h[1][:, S : S + M], h[1][:, S + M : 2 * S]],
-            [tile([P, PACK * P], F32, "raw10")[:], h[0][:, 3 * P : 7 * P]],
+            [h[1][:, WIDE - BANK : WIDE], tile([P, BANK], F32, "raw01")[:]],
+            [tile([P, BANK], F32, "raw10")[:], h[0][:, 3 * P : 7 * P]],
         ]
-        raw_second = [h[0][:, S : 2 * S], h[1][:, 0:S]]
+        raw_second = [h[0][:, S:WIDE], h[1][:, 3 * P : 3 * P + S]]
+
         arena = tile([P, 3 * S], F32, "arena")
-        raw_late = [h[2][:].rearrange("p (j c) -> p j c", j=PACK), arena[:, S : 3 * S].rearrange("p (j c) -> p j c", j=PACK)]
-        near_early = [h[3][:, S : S + M], h[3][:, S + M : 2 * S]] + [tile([P, M], F32, "near%d" % c)[:] for c in range(2, 4)]
-        sums_early = [tile([P, M], F32, "sums%d" % c)[:] for c in range(3)] + [raw_late[1][:, 0, :]]
-        near_tile = tile([P, P + 3 * M], F32, "near_tile")
-        last_tile = tile([P, 6 * P], F32, "last_tile")
-        near_late = [near_tile[:, P + M * t : P + M * (t + 1)] for t in range(3)] + [last_tile[:, 3 * P : 6 * P]]
-        dealt = [arena[:, 0:S].rearrange("p (t m) -> p t m", t=PACK), tile([P, PACK, 2 * P], F32, "dealt1")[:]]
-        block_sums = [arena[:, P * s : P * (s + PACK)].rearrange("p (t m) -> p t m", t=PACK) for s in (8, 5, 8, 7)]
-        last_near = [near_late[0][:, 3 * P : M], near_late[1][:, 3 * P : M], arena[:, 5 * P : 6 * P], arena[:, 6 * P : 7 * P]]
+
+        def units(first, count):
+            return arena[:, P * first : P * (first + count)]
+
+        raw_late = [by_row(h[2][:, P:]), by_row(units(8, 16))]
+        near_early = [h[3][:, S : S + M], h[3][:, S + M : WIDE]] + [tile([P, M], F32, "near%d" % c)[:] for c in (2, 3)]
+        sums_early = [tile([P, M], F32, "sums%d" % c)[:] for c in range(3)] + [units(8, 4)]
+        dealt = [by_row(units(0, 8)), tile([P, PACK, 2 * P], F32, "dealt1")[:]]
+        shared = tile([P, 6 * P], F32, "shared")
+        near_late = [tile([P, M], F32, "near%d" % c)[:] for c in (4, 5, 6)] + [shared[:, 3 * P : 6 * P]]
+        near_last = [near_late[0][:, 3 * P : M], near_late[1][:, 3 * P : M], units(5, 1), units(6, 1)]
+        sums_late = [by_row(units(first, PACK)) for first in (8, 5, 8, 7)]
+        z0_bf = [
+            tile([P, 2 * P, PACK], BF16, "z0_bf")[:],
+            shared[:, 0:M].bitcast(BF16).rearrange("p (m i) -> p m i", i=PACK),
+        ]
+        z1_bf = [tile([P, P, PACK], BF16, "z1_bf%d" % u)[:] for u in range(BATCHES)]
         one = tile([P, 1], F32, "one")
         zero = tile([P, 1], F32, "zero")
         three = tile([P, 3 * P], F32, "three")
@@ -66,16 +83,17 @@ def tile_list_voxel_edge_opacity_kernel(tc, tab_words, tab_scales, offs, pos1, p
         z_s = tile([P, 2, M], U8, "z_s")
         w2_w = tile([P, 2, 2 * N // 4], I32, "w2_w")
         w2_s = tile([P, 2, N // 4], I32, "w2_s")
-        absy = [tile([P, BANK], F32, "absy%d" % u) for u in range(BLOCKS - 1)]
+        absy = [tile([P, N], F32, "absy%d" % u) for u in range(BATCHES - 1)]
         absy.append(absy[1])
-        expy = [near_tile[:, 0:BANK]] + [tile([P, BANK], F32, "expy%d" % u)[:] for u in range(1, BLOCKS)]
-        res = [tile([P, N // P, P], F32, "res%d" % u) for u in range(BLOCKS)]
+        expy = [tile([P, N], F32, "expy%d" % u) for u in range(BATCHES)]
+        res = [units(3, PACK), near_late[1]] + [tile([P, N], F32, "res%d" % u)[:] for u in (2, 3)]
 
         nc.vector.memset(zero[:], 0.0)
-        nc.vector.memset(tab_s[0:96, :], 0)
+        nc.vector.memset(tab_s[0:SCALE_ROWS_FROM, :], 0)
         nc.vector.memset(v_s[:], 0)
         nc.gpsimd.memset(w2_s[:], 0)
         nc.gpsimd.memset(three[:], 3.0)
+        nc.gpsimd.memset(h[1][:, 3 * P + S : WIDE - BANK], 0.0)
         nc.scalar.activation(one[:], zero[:], ACT.Exp, scale=-1.0)
 
         def load_table_words(a):
@@ -85,11 +103,8 @@ def tile_list_voxel_edge_opacity_kernel(tc, tab_words, tab_scales, offs, pos1, p
             rows = w1[BANK * a : BANK * (a + 1), c0:c1]
             nc.sync.dma_start(out=stage, in_=rows.rearrange("(p j) c -> p j c", j=PACK))
 
-        def by_row(stage):
-            return stage.rearrange("p (j c) -> p j c", j=PACK)
-
         nc.sync.dma_start(offs_sb[:], offs)
-        nc.sync.dma_start(out=tab_s[96:P, :], in_=tab_scales.rearrange("a s t -> s a t").bitcast(I32))
+        nc.sync.dma_start(out=tab_s[SCALE_ROWS_FROM:P, :], in_=tab_scales.rearrange("a s t -> s a t").bitcast(I32))
         nc.sync.dma_start(pos2_sb[:], pos2)
         nc.sync.dma_start(pos1_sb[:], pos1)
         load_table_words(0)
@@ -98,7 +113,8 @@ def tile_list_voxel_edge_opacity_kernel(tc, tab_words, tab_scales, offs, pos1, p
         nc.vector.tensor_copy(out=v_rows[:], in_=tab_s[:].bitcast(U8).indirect(offs_sb[:]))
         load_table_words(1)
         for q in range(4):
-            nc.sync.dma_start(out=v_s[32 * q : 32 * q + 4], in_=v_rows[96 + 8 * q : 96 + 8 * q + 8, :].bitcast(I32))
+            rows = v_rows[SCALE_ROWS_FROM + 8 * q : SCALE_ROWS_FROM + 8 * (q + 1), :]
+            nc.sync.dma_start(out=v_s[32 * q : 32 * q + 4], in_=rows.bitcast(I32))
         for a in range(2):
             load_w1(a, P, 2 * P, by_row(raw_first[1][a]))
         for a in range(2):
@@ -129,16 +145,16 @@ def tile_list_voxel_edge_opacity_kernel(tc, tab_words, tab_scales, offs, pos1, p
             raw = rows.rearrange("p j (c i) -> p c j i", i=PACK)
             copy(out=dst.rearrange("p t (c i) j -> p (t c) j i", i=PACK), in_=raw)
 
-        def cast_dealing(dst, a, t0, t1):
-            raw = raw_late[a].rearrange("p j (m t) -> p m j t", t=PACK)[:, :, :, t0:t1]
-            nc.scalar.copy(out=dst.rearrange("p t m j -> p m j t"), in_=raw)
+        def cast_dealing(dst, a, t0, t1, m0, m1):
+            raw = raw_late[a].rearrange("p j (m t) -> p m j t", t=PACK)[:, m0:m1, :, t0:t1]
+            nc.scalar.copy(out=dst.rearrange("p t m j -> p m j t")[:, m0:m1], in_=raw)
 
         def pieces(c):
             if c == 0:
-                return [(0, 0, 512), (1, 512, 768), (2, 768, 1024)]
+                return [(0, 0, S // 2), (1, S // 2, 3 * S // 4), (2, 3 * S // 4, S)]
             return [((2 * c + 1 + half) % 8, BANK * half, BANK * (half + 1)) for half in range(2)]
 
-        def h_pass(c, a, piece, first=0):
+        def h_pass(c, a, piece):
             b, j0, j1 = piece
             nc.tensor.matmul_mx(
                 out=banks[b][:, 0 : j1 - j0],
@@ -146,14 +162,14 @@ def tile_list_voxel_edge_opacity_kernel(tc, tab_words, tab_scales, offs, pos1, p
                 lhsT_scale=w1_s[(c, a)],
                 rhs=v_w[a][:, j0:j1].bitcast(FP8X4),
                 rhs_scale=v_s[:, a, :].bitcast(U8)[:, j0:j1],
-                start=(a == first),
-                stop=(a != first),
+                start=(a == 0),
+                stop=(a == 1),
             )
 
-        def h_passes(c, first=0):
+        def h_passes(c):
             for piece in pieces(c):
-                for a in (first, 1 - first):
-                    h_pass(c, a, piece, first)
+                for a in range(2):
+                    h_pass(c, a, piece)
 
         def copy_piece(copy, c, piece):
             b, j0, j1 = piece
@@ -167,12 +183,12 @@ def tile_list_voxel_edge_opacity_kernel(tc, tab_words, tab_scales, offs, pos1, p
             return pos_sb[:, P // 16 * u0 : P // 16 * u1]
 
         def gather_near(dst, c, u0, u1):
-            if u1 - u0 == BLOCKS:
+            if u1 - u0 == BATCHES:
                 nc.vector.tensor_scalar(dst, h[c][:].indirect(pos2_sb[:]), 3.0, 0.0, ALU.mult, ALU.add)
             else:
                 nc.vector.tensor_tensor(dst, h[c][:].indirect(entries(pos2_sb, u0, u1)), three[:, 0 : P * (u1 - u0)], ALU.mult)
 
-        def gather_far(dst, c, u0, u1, near):
+        def gather_sums(dst, c, u0, u1, near):
             nc.vector.tensor_tensor(dst, h[c][:].indirect(entries(pos1_sb, u0, u1)), near, ALU.add)
 
         halves = [slice(2 * P * half, 2 * P * (half + 1)) for half in range(2)]
@@ -180,28 +196,31 @@ def tile_list_voxel_edge_opacity_kernel(tc, tab_words, tab_scales, offs, pos1, p
         def deal(c, half):
             nc.sync.dma_start(out=dealt[half][32 * c : 32 * (c + 1)], in_=sums_early[c][:, halves[half]])
 
-        def early_gathers(c):
+        def gathers_in_halves(c):
             for half in range(2):
                 gather_near(near_early[c][:, halves[half]], c, 2 * half, 2 * half + 2)
             for half in range(2):
-                gather_far(sums_early[c][:, halves[half]], c, 2 * half, 2 * half + 2, near_early[c][:, halves[half]])
+                gather_sums(sums_early[c][:, halves[half]], c, 2 * half, 2 * half + 2, near_early[c][:, halves[half]])
                 deal(c, half)
 
         def near_whole(c):
-            gather_near(near_early[c], c, 0, BLOCKS)
+            gather_near(near_early[c], c, 0, BATCHES)
 
-        def far_whole(c):
-            gather_far(sums_early[c], c, 0, BLOCKS, near_early[c])
+        def sums_whole(c):
+            gather_sums(sums_early[c], c, 0, BATCHES, near_early[c])
             for half in range(2):
                 deal(c, half)
 
-        def relu(dst, src, on_vector=False):
-            src = src.rearrange("p t (c i) -> p c t i", i=PACK)
-            dst = dst.rearrange("p (c i) t -> p c t i", i=PACK)
-            if on_vector:
-                nc.vector.tensor_scalar(dst, src, 0.25, 0.0, ALU.mult, ALU.max)
-            else:
-                nc.scalar.activation(dst, src, ACT.Relu, scale=0.25)
+        def batch_sums(u, places):
+            for t in places:
+                near = near_last[t] if u == BATCHES - 1 else near_late[t][:, P * u : P * (u + 1)]
+                gather_sums(sums_late[u][:, t, :], PACK + t, u, u + 1, near)
+
+        def word_views(dst, src):
+            return dst.rearrange("p (c i) t -> p c t i", i=PACK), src.rearrange("p t (c i) -> p c t i", i=PACK)
+
+        def relu(dst, src):
+            nc.scalar.activation(*word_views(dst, src), ACT.Relu, scale=0.25)
 
         def quantize_z(g, u0, u1, src):
             cols = slice(P * u0, P * u1)
@@ -210,13 +229,13 @@ def tile_list_voxel_edge_opacity_kernel(tc, tab_words, tab_scales, offs, pos1, p
                 z_w[(g, u)] = codes[:, P * (u - u0) : P * (u - u0 + 1)]
             nc.vector.quantize_mx(out=codes[:].bitcast(FP8X4), scales=z_s[:, g, cols], in_=src.rearrange("p m i -> p (m i)"))
 
-        parts = {0: [(0, 4, 1)], 1: [(0, 2, 2), (2, 4, 3)], 2: [(0, 4, 4)], 3: [(0, 2, 2), (2, 4, 3)]}
+        parts = [[(0, 4, 1)], [(0, 2, 2), (2, 4, 3)], [(0, 4, 4)], [(0, 2, 2), (2, 4, 3)]]
 
-        def density(g, u, which=None):
+        def density(g, u, some):
             cols = slice(P * u, P * (u + 1))
             codes = w2_w[:].bitcast(U8)
             scales = w2_s[:].bitcast(U8)
-            for n0, n1, b in parts[u] if which is None else [parts[u][which]]:
+            for n0, n1, b in some:
                 for n in range(n0, n1):
                     nc.tensor.matmul_mx(
                         out=banks[b][:, P * (n - n0) : P * (n - n0 + 1)],
@@ -228,126 +247,118 @@ def tile_list_voxel_edge_opacity_kernel(tc, tab_words, tab_scales, offs, pos1, p
                         stop=(g == 1 and n == n1 - 1),
                     )
 
-        def magnitude(u, which=None):
-            for n0, n1, b in parts[u] if which is None else [parts[u][which]]:
-                nc.scalar.activation(absy[u][:, P * n0 : P * n1], banks[b][:, 0 : P * (n1 - n0)], ACT.Abs)
+        def magnitude(u, n0, n1):
+            first, b = [(m0, b) for m0, m1, b in parts[u] if m0 <= n0 < m1][0]
+            nc.scalar.activation(absy[u][:, P * n0 : P * n1], banks[b][:, P * (n0 - first) : P * (n1 - first)], ACT.Abs)
 
         def decay(u, n0, n1):
             part = slice(P * n0, P * n1)
             nc.scalar.activation(expy[u][:, part], absy[u][:, part], ACT.Exp, scale=-1.0)
 
-        def store(u, n0, n1):
+        def store(u, n0, n1, unit=1.0):
             part = slice(P * n0, P * n1)
-            flat = res[u][:].rearrange("p n m -> p (n m)")
-            nc.vector.tensor_scalar(flat[:, part], expy[u][:, part], -1.0, one[:] if u == 2 else 1.0, ALU.mult, ALU.add)
+            nc.vector.tensor_scalar(res[u][:, part], expy[u][:, part], -1.0, unit, ALU.mult, ALU.add)
             rows = out[part, P * u : P * (u + 1)].rearrange("(n p) m -> p n m", p=P)
-            nc.sync.dma_start(out=rows, in_=res[u][:, n0:n1, :])
+            nc.sync.dma_start(out=rows, in_=res[u][:, part].rearrange("p (n m) -> p n m", m=P))
 
         def first_weights(c):
             bf = weights_tile([(c, 0), (c, 1)])
             for a in range(2):
                 cast_neighbours(bf[:, a : a + 1], by_row(raw_first[c][a]))
-            return bf
+            quantize_w1([(c, 0), (c, 1)], bf)
+
+        def early_z(half):
+            relu(z0_bf[half], dealt[half])
+            quantize_z(0, 2 * half, 2 * half + 2, z0_bf[half])
+            for u in range(2 * half, min(2 * half + 2, BATCHES - 1)):
+                density(0, u, parts[u])
+
+        def late_z(u):
+            relu(z1_bf[u], sums_late[u])
+            quantize_z(1, u, u + 1, z1_bf[u])
+            density(1, u, parts[u])
 
         gather_table_words(0, 0, S)
-        quantize_w1([(0, 0), (0, 1)], first_weights(0))
+        first_weights(0)
         for piece in pieces(0):
             h_pass(0, 0, piece)
         for piece in pieces(0):
             gather_table_words(1, piece[1], piece[2])
             h_pass(0, 1, piece)
-        bf1 = first_weights(1)
-        quantize_w1([(1, 0), (1, 1)], bf1)
+        first_weights(1)
         h_passes(1)
         second = [[(2, a), (3, a)] for a in range(2)]
         bf_second = [weights_tile(second[a]) for a in range(2)]
-        copy_piece(nc.scalar.copy, 0, pieces(0)[0])
-        for i in range(2):
-            copy_piece(nc.vector.tensor_copy, 0, pieces(0)[1 + i])
-        for i, copy in enumerate((nc.scalar.copy, nc.vector.tensor_copy)):
-            cast_neighbours(bf_second[0][:, i : i + 1], by_row(raw_second[0])[:, :, P * i : P * (i + 1)], copy)
-        cast_neighbours(bf_second[1][:], by_row(raw_second[1]))
+        for copy, piece in zip((nc.scalar.copy, nc.vector.tensor_copy, nc.vector.tensor_copy), pieces(0)):
+            copy_piece(copy, 0, piece)
+        for a, copies in enumerate(((nc.scalar.copy, nc.vector.tensor_copy), (nc.scalar.copy, nc.scalar.copy))):
+            for i, copy in enumerate(copies):
+                cast_neighbours(bf_second[a][:, i : i + 1], by_row(raw_second[a])[:, :, P * i : P * (i + 1)], copy)
+
         near_whole(0)
         quantize_w1(second[0], bf_second[0])
-        far_whole(0)
+        sums_whole(0)
         quantize_w1(second[1], bf_second[1])
         h_passes(2)
         h_passes(3)
         copy_h(1)
-        early_gathers(1)
-
-        late_a = [(4, 0), (5, 0), (6, 0), (7, 0)]
-        late_b = [(4, 1), (5, 1)]
-        late_c = [(6, 1), (7, 1)]
-        bf_a, bf_b, bf_c = weights_tile(late_a), weights_tile(late_b), weights_tile(late_c)
-        cast_dealing(bf_a[:], 0, 0, 4)
-        quantize_w1(late_a, bf_a)
+        gathers_in_halves(1)
+        late = [[(4, 0), (5, 0), (6, 0), (7, 0)], [(4, 1), (5, 1)], [(6, 1), (7, 1)]]
+        bf_late = [weights_tile(members) for members in late]
+        cast_dealing(bf_late[0][:], 0, 0, PACK, 0, FIRST_PART)
+        cast_dealing(bf_late[0][:], 0, 0, PACK, FIRST_PART, P)
+        quantize_w1(late[0], bf_late[0])
         copy_h(2)
-        early_gathers(2)
-        cast_dealing(bf_b[:], 1, 0, 2)
-        quantize_w1(late_b, bf_b)
+        gathers_in_halves(2)
+        cast_dealing(bf_late[1][:], 1, 0, 2, 0, P)
+        quantize_w1(late[1], bf_late[1])
         h_passes(4)
         h_passes(5)
         copy_h(3)
         near_whole(3)
-        cast_dealing(bf_c[:], 1, 2, 4)
-        quantize_w1(late_c, bf_c)
+        cast_dealing(bf_late[2][:], 1, 2, PACK, 0, P)
+        quantize_w1(late[2], bf_late[2])
         h_passes(6)
         h_passes(7)
-        far_whole(3)
+        sums_whole(3)
+
         for t in range(PACK):
-            copy_h(4 + t)
-            blocks = BLOCKS if t < 2 else BLOCKS - 1
-            gather_near(near_late[t][:, 0 : P * blocks], 4 + t, 0, blocks)
-
-        z0_bf = [
-            tile([P, 2 * P, PACK], BF16, "z0_bf")[:],
-            last_tile[:, 0:M].bitcast(BF16).rearrange("p (m i) -> p m i", i=PACK),
-        ]
-        z1_bf = [tile([P, P, PACK], BF16, "z1_bf%d" % u)[:] for u in range(BLOCKS)]
-
-        def far_block(u, chunks):
-            for t in chunks:
-                near = last_near[t] if u == 3 else near_late[t][:, P * u : P * (u + 1)]
-                gather_far(block_sums[u][:, t, :], 4 + t, u, u + 1, near)
-
-        def early_half(half):
-            relu(z0_bf[half], dealt[half])
-            quantize_z(0, 2 * half, 2 * half + 2, z0_bf[half])
-            for u in range(2 * half, min(2 * half + 2, 3)):
-                density(0, u)
-
-        def finish_block(u):
-            relu(z1_bf[u], block_sums[u], on_vector=(u == 3))
-            quantize_z(1, u, u + 1, z1_bf[u])
-            density(1, u)
-
-        far_block(0, range(PACK))
-        early_half(0)
-        far_block(1, (0, 1, 2))
-        finish_block(0)
-        far_block(1, (3,))
-        far_block(2, (1, 2, 3))
-        early_half(1)
-        finish_block(1)
-        far_block(2, (0,))
+            copy_h(PACK + t)
+            batches = BATCHES if t < 2 else BATCHES - 1
+            gather_near(near_late[t][:, 0 : P * batches], PACK + t, 0, batches)
+        batch_sums(0, range(PACK))
+        early_z(0)
+        batch_sums(1, (0, 1, 2))
+        late_z(0)
+        batch_sums(1, (3,))
+        batch_sums(2, (1, 2, 3))
+        early_z(1)
+        late_z(1)
+        batch_sums(2, (0,))
         for t in (2, 3):
-            gather_near(last_near[t], 4 + t, 3, 4)
-        far_block(3, (0,))
-        magnitude(0)
-        finish_block(2)
+            gather_near(near_last[t], PACK + t, 3, 4)
+        batch_sums(3, (0,))
+        for step in (magnitude, decay):
+            for n0 in (0, 2):
+                step(0, n0, n0 + 2)
+        late_z(2)
         for half in range(2):
-            magnitude(1, half)
-            density(0, 3, half)
-        decay(0, 0, 4)
-        far_block(3, (1, 2, 3))
-        finish_block(3)
-        magnitude(2)
-        decay(1, 0, 4)
+            magnitude(1, 2 * half, 2 * half + 2)
+            density(0, 3, parts[3][half : half + 1])
+        for n0 in (0, 2):
+            decay(1, n0, n0 + 2)
+        batch_sums(3, (2, 3, 1))
+
+        store(0, 0, 4)
+        nc.vector.tensor_scalar(*word_views(z1_bf[3], sums_late[3]), 0.25, 0.0, ALU.mult, ALU.max)
+        store(1, 0, 4)
+        quantize_z(1, 3, 4, z1_bf[3])
+        density(1, 3, parts[3])
+        magnitude(2, 0, 4)
         decay(2, 0, 4)
-        for u in range(3):
-            store(u, 0, 4)
-        magnitude(3)
+        store(2, 0, 4, one[:])
+        for n0 in (0, 2):
+            magnitude(3, n0, n0 + 2)
         for n0, n1 in ((0, 2), (2, 3), (3, 4)):
             decay(3, n0, n1)
             store(3, n0, n1)

@@ -32,8 +32,8 @@ def tile_list_voxel_edge_opacity_kernel(tc, tab_words, tab_scales, offs, pos1, p
         psum = ctx.enter_context(tc.psum_pool(name="psum", bufs=1))
         banks = [psum.tile([P, BANK], F32, name="bank%d" % b) for b in range(8)]
 
-        def tile(shape, dtype, name):
-            return keep.tile(shape, dtype, name=name, align_bytes=64)
+        def tile(shape, dtype, name, tag=None):
+            return keep.tile(shape, dtype, name=name, tag=tag or name, align_bytes=64)
 
         def by_row(flat):
             return flat.rearrange("p (j c) -> p j c", j=PACK)
@@ -43,7 +43,15 @@ def tile_list_voxel_edge_opacity_kernel(tc, tab_words, tab_scales, offs, pos1, p
         pos2_sb = tile([P, M // 16], U16, "pos2_sb")
         tab_w = [tile([P, T], I32, "tab_w%d" % a) for a in range(2)]
         tab_s = tile([P, T // 4], I32, "tab_s")
-        v_w = [tile([P, S], U32, "v_w%d" % a) for a in range(2)]
+        first_words = tile([P, S], U32, "v_w0")
+        v_w = {(0, 0): first_words[:, 0:BANK], (0, 1): first_words[:, BANK:S], (1, 0): tile([P, BANK], U32, "v_w10")[:]}
+
+        def words(a, j0, j1):
+            if (a, j0, j1) == (0, 0, S):
+                return first_words[:]
+            half = j0 // BANK
+            return v_w[(a, half)][:, j0 - BANK * half : j1 - BANK * half]
+
         v_rows = tile([P, S], U8, "v_rows")
         v_s = tile([P, 2, S // 4], I32, "v_s")
 
@@ -52,7 +60,7 @@ def tile_list_voxel_edge_opacity_kernel(tc, tab_words, tab_scales, offs, pos1, p
 
         raw_first = [
             [h[1][:, WIDE - BANK : WIDE], tile([P, BANK], F32, "raw01")[:]],
-            [tile([P, BANK], F32, "raw10")[:], h[0][:, 3 * P : 7 * P]],
+            [tile([P, BANK], F32, "raw10")[:], h[0][:, BANK - 64 : S - 64]],
         ]
         raw_second = [h[0][:, S:WIDE], h[1][:, 3 * P : 3 * P + S]]
 
@@ -108,10 +116,10 @@ def tile_list_voxel_edge_opacity_kernel(tc, tab_words, tab_scales, offs, pos1, p
         nc.sync.dma_start(pos2_sb[:], pos2)
         nc.sync.dma_start(pos1_sb[:], pos1)
         load_table_words(0)
-        for a in range(2):
-            load_w1(a, 0, P, by_row(raw_first[0][a]))
+        load_w1(0, 0, P, by_row(raw_first[0][0]))
         nc.vector.tensor_copy(out=v_rows[:], in_=tab_s[:].bitcast(U8).indirect(offs_sb[:]))
         load_table_words(1)
+        load_w1(1, 0, P, by_row(raw_first[0][1]))
         for q in range(4):
             rows = v_rows[SCALE_ROWS_FROM + 8 * q : SCALE_ROWS_FROM + 8 * (q + 1), :]
             nc.sync.dma_start(out=v_s[32 * q : 32 * q + 4], in_=rows.bitcast(I32))
@@ -128,10 +136,11 @@ def tile_list_voxel_edge_opacity_kernel(tc, tab_words, tab_scales, offs, pos1, p
 
         def gather_table_words(a, j0, j1):
             window = tab_w[a][:].bitcast(U32).indirect(offs_sb[:, j0 // 16 : j1 // 16])
-            nc.vector.tensor_copy(out=v_w[a][:, j0:j1], in_=window)
+            nc.vector.tensor_copy(out=words(a, j0, j1), in_=window)
 
         def weights_tile(members):
-            return tile([P, len(members), P, PACK], BF16, "w1_bf%d%d" % members[0])
+            name = "w1_bf%d%d" % members[0]
+            return tile([P, len(members), P, PACK], BF16, name, "w1_w01" if members[0] == (2, 0) else name)
 
         def quantize_w1(members, src):
             codes = tile([P, P * len(members)], U32, "w1_w%d%d" % members[0])
@@ -151,7 +160,7 @@ def tile_list_voxel_edge_opacity_kernel(tc, tab_words, tab_scales, offs, pos1, p
 
         def pieces(c):
             if c == 0:
-                return [(0, 0, S // 2), (1, S // 2, 3 * S // 4), (2, 3 * S // 4, S)]
+                return [(0, 0, S // 2), (1, S // 2, 3 * S // 4), (2, 3 * S // 4, 7 * S // 8), (7, 7 * S // 8, S)]
             return [((2 * c + 1 + half) % 8, BANK * half, BANK * (half + 1)) for half in range(2)]
 
         def h_pass(c, a, piece):
@@ -160,7 +169,7 @@ def tile_list_voxel_edge_opacity_kernel(tc, tab_words, tab_scales, offs, pos1, p
                 out=banks[b][:, 0 : j1 - j0],
                 lhsT=w1_w[(c, a)].bitcast(FP8X4),
                 lhsT_scale=w1_s[(c, a)],
-                rhs=v_w[a][:, j0:j1].bitcast(FP8X4),
+                rhs=words(a, j0, j1).bitcast(FP8X4),
                 rhs_scale=v_s[:, a, :].bitcast(U8)[:, j0:j1],
                 start=(a == 0),
                 stop=(a == 1),
@@ -279,17 +288,26 @@ def tile_list_voxel_edge_opacity_kernel(tc, tab_words, tab_scales, offs, pos1, p
             density(1, u, parts[u])
 
         gather_table_words(0, 0, S)
-        first_weights(0)
+        def pass_weights(a):
+            bf = weights_tile([(0, a)])
+            cast_neighbours(bf[:], by_row(raw_first[0][a]))
+            quantize_w1([(0, a)], bf)
+
+        pass_weights(0)
         for piece in pieces(0):
             h_pass(0, 0, piece)
+        gather_table_words(1, 0, S // 2)
+        pass_weights(1)
+        v_w[(1, 1)] = tile([P, BANK], U32, "v_w11", "raw01")[:]
+        gather_table_words(1, S // 2, 3 * S // 4)
+        gather_table_words(1, 3 * S // 4, S)
         for piece in pieces(0):
-            gather_table_words(1, piece[1], piece[2])
             h_pass(0, 1, piece)
         first_weights(1)
         h_passes(1)
         second = [[(2, a), (3, a)] for a in range(2)]
         bf_second = [weights_tile(second[a]) for a in range(2)]
-        for copy, piece in zip((nc.scalar.copy, nc.vector.tensor_copy, nc.vector.tensor_copy), pieces(0)):
+        for copy, piece in zip((nc.scalar.copy, nc.vector.tensor_copy, nc.vector.tensor_copy, nc.scalar.copy), pieces(0)):
             copy_piece(copy, 0, piece)
         for a, copies in enumerate(((nc.scalar.copy, nc.vector.tensor_copy), (nc.scalar.copy, nc.scalar.copy))):
             for i, copy in enumerate(copies):
@@ -354,8 +372,9 @@ def tile_list_voxel_edge_opacity_kernel(tc, tab_words, tab_scales, offs, pos1, p
         store(1, 0, 4)
         quantize_z(1, 3, 4, z1_bf[3])
         density(1, 3, parts[3])
-        magnitude(2, 0, 4)
-        decay(2, 0, 4)
+        for step in (magnitude, decay):
+            for n0 in (0, 2):
+                step(2, n0, n0 + 2)
         store(2, 0, 4, one[:])
         for n0 in (0, 2):
             magnitude(3, n0, n0 + 2)

from contextlib import ExitStack

import concourse.mybir as mybir

K, T, S, M, H, N = 1024, 4096, 1024, 512, 1024, 512
FLOPS = 2 * K * H * S + 2 * H * N * M

F32 = mybir.dt.float32
BF16 = mybir.dt.bfloat16
I32 = mybir.dt.int32
U32 = mybir.dt.uint32
U16 = mybir.dt.uint16
U8 = mybir.dt.uint8
FP8X4 = mybir.dt.float8_e4m3fn_x4
FP4X4 = mybir.dt.float4_e2m1fn_x4
ACT = mybir.ActivationFunctionType
ALU = mybir.AluOpType

P = 128
BANK = 512
PACK = 4
BATCHES = M // P
SCALE_ROWS_FROM = 96
WIDE = 2 * S
FIRST_PART = 96


def tile_list_voxel_edge_opacity_kernel(tc, tab_words, tab_scales, offs, pos1, pos2, w1, w2_words, w2_scales, out):
    nc = tc.nc
    with ExitStack() as ctx:
        keep = ctx.enter_context(tc.tile_pool(name="keep", bufs=1))
        psum = ctx.enter_context(tc.psum_pool(name="psum", bufs=1))
        banks = [psum.tile([P, BANK], F32, name="bank%d" % b) for b in range(8)]

        def tile(shape, dtype, name, tag=None):
            return keep.tile(shape, dtype, name=name, tag=tag or name, align_bytes=64)

        def by_row(flat):
            return flat.rearrange("p (j c) -> p j c", j=PACK)

        offs_sb = tile([P, S // 16], U16, "offs_sb")
        pos1_sb = tile([P, M // 16], U16, "pos1_sb")
        pos2_sb = tile([P, M // 16], U16, "pos2_sb")
        tab_w = [tile([P, T], I32, "tab_w%d" % a) for a in range(2)]
        tab_s = tile([P, T // 4], I32, "tab_s")
        first_words = tile([P, S], U32, "v_w0")
        v_w = {(0, 0): first_words[:, 0:BANK], (0, 1): first_words[:, BANK:S], (1, 0): tile([P, BANK], U32, "v_w10")[:]}

        def words(a, j0, j1):
            if (a, j0, j1) == (0, 0, S):
                return first_words[:]
            half = j0 // BANK
            return v_w[(a, half)][:, j0 - BANK * half : j1 - BANK * half]

        v_rows = tile([P, S], U8, "v_rows")
        v_s = tile([P, 2, S // 4], I32, "v_s")

        h = [tile([P, P + WIDE if c == 2 else WIDE], F32, "h%d" % c) for c in range(PACK)]
        h = h + h[0:2] + [tile([P, S], F32, "h%d" % c) for c in (6, 7)]

        raw_first = [
            [h[1][:, WIDE - BANK : WIDE], tile([P, BANK], F32, "raw01")[:]],
            [tile([P, BANK], F32, "raw10")[:], h[0][:, BANK - 64 : S - 64]],
        ]
        raw_second = [h[0][:, S:WIDE], h[1][:, 3 * P : 3 * P + S]]

        arena = tile([P, 3 * S], F32, "arena")

        def units(first, count):
            return arena[:, P * first : P * (first + count)]

        raw_late = [by_row(h[2][:, P:]), by_row(units(8, 16))]
        near_early = [h[3][:, S : S + M], h[3][:, S + M : WIDE]] + [tile([P, M], F32, "near%d" % c)[:] for c in (2, 3)]
        sums_early = [tile([P, M], F32, "sums%d" % c)[:] for c in range(3)] + [units(8, 4)]
        dealt = [by_row(units(0, 8)), tile([P, PACK, 2 * P], F32, "dealt1")[:]]
        shared = tile([P, 6 * P], F32, "shared")
        near_late = [tile([P, M], F32, "near%d" % c)[:] for c in (4, 5, 6)] + [shared[:, 3 * P : 6 * P]]
        near_last = [near_late[0][:, 3 * P : M], near_late[1][:, 3 * P : M], units(5, 1), units(6, 1)]
        sums_late = [by_row(units(first, PACK)) for first in (8, 5, 8, 7)]
        z0_bf = [
            tile([P, 2 * P, PACK], BF16, "z0_bf")[:],
            shared[:, 0:M].bitcast(BF16).rearrange("p (m i) -> p m i", i=PACK),
        ]
        z1_bf = [tile([P, P, PACK], BF16, "z1_bf%d" % u)[:] for u in range(BATCHES)]
        one = tile([P, 1], F32, "one")
        zero = tile([P, 1], F32, "zero")
        three = tile([P, 3 * P], F32, "three")
        w1_w = {}
        w1_s = {}
        z_w = {}
        z_s = tile([P, 2, M], U8, "z_s")
        w2_w = tile([P, 2, 2 * N // 4], I32, "w2_w")
        w2_s = tile([P, 2, N // 4], I32, "w2_s")
        absy = [tile([P, N], F32, "absy%d" % u) for u in range(BATCHES - 1)]
        absy.append(absy[1])
        expy = [tile([P, N], F32, "expy%d" % u) for u in range(BATCHES)]
        res = [units(3, PACK), near_late[1]] + [tile([P, N], F32, "res%d" % u)[:] for u in (2, 3)]

        nc.vector.memset(zero[:], 0.0)
        nc.vector.memset(tab_s[0:SCALE_ROWS_FROM, :], 0)
        nc.vector.memset(v_s[:], 0)
        nc.gpsimd.memset(w2_s[:], 0)
        nc.gpsimd.memset(three[:], 3.0)
        nc.gpsimd.memset(h[1][:, 3 * P + S : WIDE - BANK], 0.0)
        nc.scalar.activation(one[:], zero[:], ACT.Exp, scale=-1.0)

        def load_table_words(a):
            nc.sync.dma_start(out=tab_w[a][:], in_=tab_words[a].rearrange("p t i -> p (t i)").bitcast(I32))

        def load_w1(a, c0, c1, stage):
            rows = w1[BANK * a : BANK * (a + 1), c0:c1]
            nc.sync.dma_start(out=stage, in_=rows.rearrange("(p j) c -> p j c", j=PACK))

        nc.sync.dma_start(offs_sb[:], offs)
        nc.sync.dma_start(out=tab_s[SCALE_ROWS_FROM:P, :], in_=tab_scales.rearrange("a s t -> s a t").bitcast(I32))
        nc.sync.dma_start(pos2_sb[:], pos2)
        nc.sync.dma_start(pos1_sb[:], pos1)
        load_table_words(0)
        load_w1(0, 0, P, by_row(raw_first[0][0]))
        nc.vector.tensor_copy(out=v_rows[:], in_=tab_s[:].bitcast(U8).indirect(offs_sb[:]))
        load_table_words(1)
        load_w1(1, 0, P, by_row(raw_first[0][1]))
        for q in range(4):
            rows = v_rows[SCALE_ROWS_FROM + 8 * q : SCALE_ROWS_FROM + 8 * (q + 1), :]
            nc.sync.dma_start(out=v_s[32 * q : 32 * q + 4], in_=rows.bitcast(I32))
        for a in range(2):
            load_w1(a, P, 2 * P, by_row(raw_first[1][a]))
        for a in range(2):
            load_w1(a, 2 * P, 4 * P, by_row(raw_second[a]))
        for a in range(2):
            load_w1(a, BANK, 2 * BANK, raw_late[a])
        nc.sync.dma_start(out=w2_w[:], in_=w2_words.rearrange("a p b -> p a b").bitcast(I32))
        for q in range(4):
            rows = w2_scales[:, 4 * q : 4 * q + 4, :].rearrange("a r n -> r a n")
            nc.sync.dma_start(out=w2_s[32 * q : 32 * q + 4, :, :], in_=rows.bitcast(I32))

        def gather_table_words(a, j0, j1):
            window = tab_w[a][:].bitcast(U32).indirect(offs_sb[:, j0 // 16 : j1 // 16])
            nc.vector.tensor_copy(out=words(a, j0, j1), in_=window)

        def weights_tile(members):
            name = "w1_bf%d%d" % members[0]
            return tile([P, len(members), P, PACK], BF16, name, "w1_w01" if members[0] == (2, 0) else name)

        def quantize_w1(members, src):
            codes = tile([P, P * len(members)], U32, "w1_w%d%d" % members[0])
            scales = tile([P, P * len(members)], U8, "w1_s%d%d" % members[0])
            for i, member in enumerate(members):
                w1_w[member] = codes[:, P * i : P * (i + 1)]
                w1_s[member] = scales[:, P * i : P * (i + 1)]
            nc.vector.quantize_mx(out=codes[:].bitcast(FP8X4), scales=scales[:], in_=src[:].rearrange("p t m j -> p (t m j)"))

        def cast_neighbours(dst, rows, copy=nc.scalar.copy):
            raw = rows.rearrange("p j (c i) -> p c j i", i=PACK)
            copy(out=dst.rearrange("p t (c i) j -> p (t c) j i", i=PACK), in_=raw)

        def cast_dealing(dst, a, t0, t1, m0, m1):
            raw = raw_late[a].rearrange("p j (m t) -> p m j t", t=PACK)[:, m0:m1, :, t0:t1]
            nc.scalar.copy(out=dst.rearrange("p t m j -> p m j t")[:, m0:m1], in_=raw)

        def pieces(c):
            if c == 0:
                return [(0, 0, S // 2), (1, S // 2, 3 * S // 4), (2, 3 * S // 4, 7 * S // 8), (7, 7 * S // 8, S)]
            return [((2 * c + 1 + half) % 8, BANK * half, BANK * (half + 1)) for half in range(2)]

        def h_pass(c, a, piece):
            b, j0, j1 = piece
            nc.tensor.matmul_mx(
                out=banks[b][:, 0 : j1 - j0],
                lhsT=w1_w[(c, a)].bitcast(FP8X4),
                lhsT_scale=w1_s[(c, a)],
                rhs=words(a, j0, j1).bitcast(FP8X4),
                rhs_scale=v_s[:, a, :].bitcast(U8)[:, j0:j1],
                start=(a == 0),
                stop=(a == 1),
            )

        def h_passes(c):
            for piece in pieces(c):
                for a in range(2):
                    h_pass(c, a, piece)

        def copy_piece(copy, c, piece):
            b, j0, j1 = piece
            copy(out=h[c][:, j0:j1], in_=banks[b][:, 0 : j1 - j0])

        def copy_h(c):
            for piece in pieces(c):
                copy_piece(nc.scalar.copy, c, piece)

        def entries(pos_sb, u0, u1):
            return pos_sb[:, P // 16 * u0 : P // 16 * u1]

        def gather_near(dst, c, u0, u1):
            if u1 - u0 == BATCHES:
                nc.vector.tensor_scalar(dst, h[c][:].indirect(pos2_sb[:]), 3.0, 0.0, ALU.mult, ALU.add)
            else:
                nc.vector.tensor_tensor(dst, h[c][:].indirect(entries(pos2_sb, u0, u1)), three[:, 0 : P * (u1 - u0)], ALU.mult)

        def gather_sums(dst, c, u0, u1, near):
            nc.vector.tensor_tensor(dst, h[c][:].indirect(entries(pos1_sb, u0, u1)), near, ALU.add)

        halves = [slice(2 * P * half, 2 * P * (half + 1)) for half in range(2)]

        def deal(c, half):
            nc.sync.dma_start(out=dealt[half][32 * c : 32 * (c + 1)], in_=sums_early[c][:, halves[half]])

        def gathers_in_halves(c):
            for half in range(2):
                gather_near(near_early[c][:, halves[half]], c, 2 * half, 2 * half + 2)
            for half in range(2):
                gather_sums(sums_early[c][:, halves[half]], c, 2 * half, 2 * half + 2, near_early[c][:, halves[half]])
                deal(c, half)

        def near_whole(c):
            gather_near(near_early[c], c, 0, BATCHES)

        def sums_whole(c):
            gather_sums(sums_early[c], c, 0, BATCHES, near_early[c])
            for half in range(2):
                deal(c, half)

        def batch_sums(u, places):
            for t in places:
                near = near_last[t] if u == BATCHES - 1 else near_late[t][:, P * u : P * (u + 1)]
                gather_sums(sums_late[u][:, t, :], PACK + t, u, u + 1, near)

        def word_views(dst, src):
            return dst.rearrange("p (c i) t -> p c t i", i=PACK), src.rearrange("p t (c i) -> p c t i", i=PACK)

        def relu(dst, src):
            nc.scalar.activation(*word_views(dst, src), ACT.Relu, scale=0.25)

        def quantize_z(g, u0, u1, src):
            cols = slice(P * u0, P * u1)
            codes = tile([P, P * (u1 - u0)], U32, "z_w%d%d" % (g, u0))
            for u in range(u0, u1):
                z_w[(g, u)] = codes[:, P * (u - u0) : P * (u - u0 + 1)]
            nc.vector.quantize_mx(out=codes[:].bitcast(FP8X4), scales=z_s[:, g, cols], in_=src.rearrange("p m i -> p (m i)"))

        parts = [[(0, 4, 1)], [(0, 2, 2), (2, 4, 3)], [(0, 4, 4)], [(0, 2, 2), (2, 4, 3)]]

        def density(g, u, some):
            cols = slice(P * u, P * (u + 1))
            codes = w2_w[:].bitcast(U8)
            scales = w2_s[:].bitcast(U8)
            for n0, n1, b in some:
                for n in range(n0, n1):
                    nc.tensor.matmul_mx(
                        out=banks[b][:, P * (n - n0) : P * (n - n0 + 1)],
                        lhsT=codes[:, g, 2 * P * n : 2 * P * (n + 1)].bitcast(FP4X4),
                        lhsT_scale=scales[:, g, P * n : P * (n + 1)],
                        rhs=z_w[(g, u)].bitcast(FP8X4),
                        rhs_scale=z_s[:, g, cols],
                        start=(g == 0 and n == n0),
                        stop=(g == 1 and n == n1 - 1),
                    )

        def magnitude(u, n0, n1):
            first, b = [(m0, b) for m0, m1, b in parts[u] if m0 <= n0 < m1][0]
            nc.scalar.activation(absy[u][:, P * n0 : P * n1], banks[b][:, P * (n0 - first) : P * (n1 - first)], ACT.Abs)

        def decay(u, n0, n1):
            part = slice(P * n0, P * n1)
            nc.scalar.activation(expy[u][:, part], absy[u][:, part], ACT.Exp, scale=-1.0)

        def store(u, n0, n1, unit=1.0):
            part = slice(P * n0, P * n1)
            nc.vector.tensor_scalar(res[u][:, part], expy[u][:, part], -1.0, unit, ALU.mult, ALU.add)
            rows = out[part, P * u : P * (u + 1)].rearrange("(n p) m -> p n m", p=P)
            nc.sync.dma_start(out=rows, in_=res[u][:, part].rearrange("p (n m) -> p n m", m=P))

        def first_weights(c):
            bf = weights_tile([(c, 0), (c, 1)])
            for a in range(2):
                cast_neighbours(bf[:, a : a + 1], by_row(raw_first[c][a]))
            quantize_w1([(c, 0), (c, 1)], bf)

        def early_z(half):
            relu(z0_bf[half], dealt[half])
            quantize_z(0, 2 * half, 2 * half + 2, z0_bf[half])
            for u in range(2 * half, min(2 * half + 2, BATCHES - 1)):
                density(0, u, parts[u])

        def late_z(u):
            relu(z1_bf[u], sums_late[u])
            quantize_z(1, u, u + 1, z1_bf[u])
            density(1, u, parts[u])

        gather_table_words(0, 0, S)
        def pass_weights(a):
            bf = weights_tile([(0, a)])
            cast_neighbours(bf[:], by_row(raw_first[0][a]))
            quantize_w1([(0, a)], bf)

        pass_weights(0)
        for piece in pieces(0):
            h_pass(0, 0, piece)
        gather_table_words(1, 0, S // 2)
        pass_weights(1)
        v_w[(1, 1)] = tile([P, BANK], U32, "v_w11", "raw01")[:]
        gather_table_words(1, S // 2, 3 * S // 4)
        gather_table_words(1, 3 * S // 4, S)
        for piece in pieces(0):
            h_pass(0, 1, piece)
        first_weights(1)
        h_passes(1)
        second = [[(2, a), (3, a)] for a in range(2)]
        bf_second = [weights_tile(second[a]) for a in range(2)]
        for copy, piece in zip((nc.scalar.copy, nc.vector.tensor_copy, nc.vector.tensor_copy, nc.scalar.copy), pieces(0)):
            copy_piece(copy, 0, piece)
        for a, copies in enumerate(((nc.scalar.copy, nc.vector.tensor_copy), (nc.scalar.copy, nc.scalar.copy))):
            for i, copy in enumerate(copies):
                cast_neighbours(bf_second[a][:, i : i + 1], by_row(raw_second[a])[:, :, P * i : P * (i + 1)], copy)

        near_whole(0)
        quantize_w1(second[0], bf_second[0])
        sums_whole(0)
        quantize_w1(second[1], bf_second[1])
        h_passes(2)
        h_passes(3)
        copy_h(1)
        gathers_in_halves(1)
        late = [[(4, 0), (5, 0), (6, 0), (7, 0)], [(4, 1), (5, 1)], [(6, 1), (7, 1)]]
        bf_late = [weights_tile(members) for members in late]
        cast_dealing(bf_late[0][:], 0, 0, PACK, 0, FIRST_PART)
        cast_dealing(bf_late[0][:], 0, 0, PACK, FIRST_PART, P)
        quantize_w1(late[0], bf_late[0])
        copy_h(2)
        gathers_in_halves(2)
        cast_dealing(bf_late[1][:], 1, 0, 2, 0, P)
        quantize_w1(late[1], bf_late[1])
        h_passes(4)
        h_passes(5)
        copy_h(3)
        near_whole(3)
        cast_dealing(bf_late[2][:], 1, 2, PACK, 0, P)
        quantize_w1(late[2], bf_late[2])
        h_passes(6)
        h_passes(7)
        sums_whole(3)

        for t in range(PACK):
            copy_h(PACK + t)
            batches = BATCHES if t < 2 else BATCHES - 1
            gather_near(near_late[t][:, 0 : P * batches], PACK + t, 0, batches)
        batch_sums(0, range(PACK))
        early_z(0)
        batch_sums(1, (0, 1, 2))
        late_z(0)
        batch_sums(1, (3,))
        batch_sums(2, (1, 2, 3))
        early_z(1)
        late_z(1)
        batch_sums(2, (0,))
        for t in (2, 3):
            gather_near(near_last[t], PACK + t, 3, 4)
        batch_sums(3, (0,))
        for step in (magnitude, decay):
            for n0 in (0, 2):
                step(0, n0, n0 + 2)
        late_z(2)
        for half in range(2):
            magnitude(1, 2 * half, 2 * half + 2)
            density(0, 3, parts[3][half : half + 1])
        for n0 in (0, 2):
            decay(1, n0, n0 + 2)
        batch_sums(3, (2, 3, 1))

        store(0, 0, 4)
        nc.vector.tensor_scalar(*word_views(z1_bf[3], sums_late[3]), 0.25, 0.0, ALU.mult, ALU.max)
        store(1, 0, 4)
        quantize_z(1, 3, 4, z1_bf[3])
        density(1, 3, parts[3])
        for step in (magnitude, decay):
            for n0 in (0, 2):
                step(2, n0, n0 + 2)
        store(2, 0, 4, one[:])
        for n0 in (0, 2):
            magnitude(3, n0, n0 + 2)
        for n0, n1 in ((0, 2), (2, 3), (3, 4)):
            decay(3, n0, n1)
            store(3, n0, n1)
